import numpy as np, ml_dtypes
CORES = [23,119,17,113]
N = 4
BF = ml_dtypes.bfloat16
W, I, B, S, RO, H = 4096, 128, 32, 6, 3, 9
def some(rng, k):
    o = np.argsort(rng.random(k.shape[:-1] + (16,) + k.shape[-1:]), axis=-2)
    return np.where(o < k[..., None, :], 0, 255)
def parts(rng):
    x = rng.integers(0, 256, (N, 8, 16, W)); w = rng.integers(0, 16, (N, 8, 16, 1)); c = rng.integers(0, 128, (N, 8, 16, I))
    l = rng.integers(1, 5, (N, 8, 16, I)); s = rng.integers(0, W, (N, 8, 16, I))
    v = rng.choice(np.array([96, 176, 208, 224, 236, 244, 252]), (N, 8, 1, I))
    return x, w, c, l, s, np.clip(v + rng.integers(-12, 13, (N, 8, 16, I)), 0, 255)
def small(a):
    return np.ascontiguousarray(a.reshape(N, 128, -1)).astype(np.float32).astype(BF)
def pack(x, w, c, l, s, fl):
    return {"x": small(x), "wt": small(w), "ch": small(c), "sp": small(l), "st": np.ascontiguousarray(s.reshape(N, 128, I)).astype(np.int32), "fl": small(fl)}
def setup_inputs(rng):
    return pack(*parts(rng))
def setup_inputs_spread(rng):
    x, w, c, l, s, fl = parts(rng)
    x = (np.exp2(8 * rng.random((N, 8, 1, W))) * rng.random(x.shape)).astype(np.int64)
    w = np.where(rng.random(w.shape) < 0.4, 0, w)
    c = np.where(rng.random((N, 8, 1, I)) < 0.5, c, np.exp2(7 * rng.random(c.shape)).astype(np.int64) - 1)
    l = rng.choice(np.array([1, 1, 1, 2, 3, 4]), l.shape)
    fl = (np.exp2(8 * rng.random((N, 8, 1, I))) * (0.5 + 0.5 * rng.random(fl.shape))).astype(np.int64)
    return pack(x, w, c, l, s, fl)
def setup_inputs_ends(rng):
    x, w, c, l, s, fl = parts(rng)
    d = rng.choice(np.array([0.04, 0.1, 0.3, 0.5]), (N, 8, 1, 1)); d[:, 7] = 0.5
    e = 255 * (rng.random(x.shape) < d); k = rng.random((N, 8, 1, W)); full = np.where(np.arange(8) == 7, 0.3, 0.03).reshape(1, 8, 1, 1)
    e = np.where(k < full, 255, np.where(k > 0.85, 0, e)); x = np.where((k > 0.5) & (k < 0.6), x, e)
    w = 15 * rng.integers(0, 2, w.shape); w[:, 7] = 15; w[:, 1] = 0; w[:, 0, 0] = 0; w[:, 0, 15] = 15
    b = rng.random((N, 8, 1, I)); c = np.where(b < 0.15, 127, np.where(b > 0.85, 0, 127 * rng.integers(0, 2, c.shape)))
    l = 1 + 3 * rng.integers(0, 2, l.shape); s = np.where(rng.random(s.shape) < 0.25, s, (W - 1) * rng.integers(0, 2, s.shape))
    fl = some(rng, rng.integers(0, 17, (N, 8, I))); fl[N - 2:] = some(rng, rng.integers(H, 17, (2, 8, I)))
    x[N - 2, 6, H - 1:] = 0; fl[N - 2, 6, :, I - 1] = np.where(np.arange(16) < H - 1, 0, 255)
    l[N - 1, 7, :, :2] = 4; s[N - 1, 7, :, :2] = W - 1
    l[N - 1, 7, 13:, I - 1] = np.array([1, 4, 4]); s[N - 1, 7, 13:, I - 1] = np.array([(0 - 613) & (W - 1), (W - 1 - 2452) & (W - 1), W - 1])
    c[N - 1, 7, 0, :2] = 127; c[N - 1, 7, 0, I - 1] = 127
    x[:, 7, :, (W - 1 + 2452) & (W - 1)] = 255; x[:, 7, :, W - 1] = 255; x[:, 7, 15] = 255
    return pack(x, w, c, l, s, fl)
def setup_inputs_corners(rng):
    x, w, c, l, s, fl = parts(rng); q = rng.permutation(N); ar = np.arange(16)[:, None]
    w[:, 0] = 0; b = rng.integers(0, 4, (N, 1, I)); c[:, 0] = np.where(b == 0, 3, np.where(b == 1, 0, np.where(b == 2, 127, c[:, 0])))
    x[:, 1] = np.minimum(x[:, 1], 254); fl[:, 1] = some(rng, rng.choice(np.array([0, H - 1, H, 16]), (N, I)))
    v = rng.integers(1, 255, (N, 16, 1)); x[:, 2] = v; fl[:, 2] = v + np.minimum(some(rng, rng.choice(np.array([H - 1, H, 16]), (N, I))), 1)
    w[:, 3] = 0; w[:, 3, 0] = 1; x[:, 3, 0, ::2] = 255; fl[:, 3] = fl[:, 3] // 2
    b = rng.integers(0, 4, (N, 1, I)); l[:, 4] = np.where(b == 0, 4, np.where(b == 1, 1, np.where(b == 2, 1 + 3 * (ar == 15), 1 + 3 * (ar & 1)))); fl[:, 4] = fl[:, 4] // 2
    e = (W - 1) * rng.integers(0, 2, (N, 16, I)); s[:, 5] = np.where(rng.random((N, 16, I)) < 0.5, e, (e - 613 * l[:, 5]) & (W - 1))
    w[:, 6] = 15; x[:, 6] = rng.integers(224, 256, (N, 16, W)); c[:, 6] = rng.choice(np.array([0, 126, 127]), (N, 16, I))
    x[q[0]] = np.minimum(x[q[0]], 254); fl[q[0]] = some(rng, np.full((8, I), H - 1))
    fl[q[1]] = some(rng, rng.integers(H, 17, (8, I))); fl[q[2]] = some(rng, rng.integers(H, 17, (8, I)))
    x[q[2], 7] = np.minimum(x[q[2], 7], 254); fl[q[2], 7, :, I - 1] = some(rng, np.full(1, H - 1))[:, 0]
    return pack(x, w, c, l, s, fl)
def setup_inputs_crowd(rng):
    x, w, c, l, s, fl = parts(rng); q = rng.permutation(N)
    s[:, :7] = rng.integers(0, W, (N, 7, 1, 1)); l[:, :7] = rng.integers(1, 5, (N, 7, 1, 1)); c[:, :7] = rng.integers(0, 128, (N, 7, 16, 1))
    s[:, 4:7, 15, I - 1] = rng.integers(0, W, (N, 3)); c[:, 4:7, :, I - 1] = rng.integers(0, 128, (N, 3, 16))
    fl = some(rng, rng.integers(H, 17, (N, 8, I)))
    for a in q[:N // 2]:
        x[a, 7] = np.minimum(x[a, 7], 254); fl[a, 7, :, I - 1] = some(rng, np.full(1, H - 1))[:, 0]
    return pack(x, w, c, l, s, fl)
def setup_inputs_late(rng):
    x, w, c, l, s, fl = parts(rng); q = rng.permutation(N); a, b = int(q[0]), int(q[1])
    x[a] = np.minimum(x[a], 254); fl[a] = some(rng, np.full((8, I), H - 1)); fl[b] = some(rng, rng.integers(H, 17, (8, I)))
    for r, g, low in ((a, 7, 8), (b, 0, 0)):
        hot = B * int(rng.integers(8, I)); w[r, g] = 0
        x[r, g] = rng.integers(0, 101, (16, W)); x[r, g, :, hot] = rng.integers(200, 255, 16)
        fl[r, g, :, low:] = rng.integers(110, 151, (16, I - low))
        l[r, g] = 1; s[r, g] = (hot - 613) & (W - 1)
        if g == 7: l[(a - 2) % N, 7] = 1; s[(a - 2) % N, 7] = (hot - 613) & (W - 1)
    s[(a - 1) % N, 7] = (16 * rng.integers(0, W // 16, (16, I)) - (I - 8)) & (W - 1)
    l[(b - 1) % N, 0] = 1; s[(b - 1) % N, 0] = W - 613 - 8 * I
    c[(b - 1) % N, 0] = 16 * rng.integers(0, 8, (16, I)) + 4 * rng.integers(1, 4, (16, I))
    return pack(x, w, c, l, s, fl)
def check_inputs(d):
    bad = []
    for k, lo, hi in (("x", 0, 255), ("wt", 0, 15), ("ch", 0, 127), ("sp", 1, 4), ("st", 0, W - 1), ("fl", 0, 255)):
        v = np.asarray(d[k]).astype(np.float64)
        if not (np.all(v >= lo) and np.all(v <= hi)): bad.append("range of " + k)
        if np.any(v != np.floor(v)): bad.append("whole numbers of " + k)
    return bad
def reference(x, wt, ch, sp, st, fl):
    X, Q, C, L, Z, F = [v.astype(np.float32).astype(np.int32).reshape(N, 8, 16, -1) for v in (x, wt, ch, sp, st, fl)]
    A = [0] * N; row = np.arange(16)[:, None]
    for t in range(RO):
        if t > 0: C, L, Z = np.roll(C, 1, axis=0), np.roll(L, 1, axis=0), np.roll(Z, 1, axis=0)
        for a in range(N):
            l = L[a]
            at = np.arange(16)[None, :, None, None]; at = at + np.where(at >= row[None, None], l[:, None], 0)
            e = np.take_along_axis(np.concatenate([C[a], np.zeros((8, 4, I), np.int32)], axis=1)[:, :, None, :], at, 1)
            e = np.concatenate([e, np.zeros((8, 1, 16, I), np.int32)], axis=1)
            s = (Z[a] + 613 * l + A[a]) & (W - 1); p = np.zeros((8, 16, I), np.int64); V = np.zeros((8, 16, 16, I), np.int32); log = []
            for k in range(S):
                z = np.take_along_axis(X[a], s.reshape(8, 1, 16 * I), 2).reshape(8, 16, 16, I)
                V = np.maximum(V, z); c = np.take_along_axis(e, np.minimum(p, 16)[:, None], 1)[:, 0].astype(np.int64)
                u = np.add.reduce(Q[a][..., None] * z, axis=1).astype(np.int64)
                n = 1 + (((u >> 3) + c) & 3); log.append((p, n))
                s = (((u * (2 * c + 1)) >> 3) + 37 * u + c) & (W - 1); p = p + n
            fails = np.add.reduce((V >= F[a][:, :, None, :]).astype(np.int32), axis=1) >= H
            best = np.argmax(np.where(fails, 16 * l + 15 - row[None], 0 - 1), axis=1)[:, None, :]; ok = np.any(fails, axis=1)[:, None, :]
            nl = np.ones((8, 16, I), np.int64)
            for p, n in log: nl = np.where(row[None] == np.take_along_axis(p, best, 1), np.take_along_axis(n, best, 1), nl)
            v = np.take_along_axis(V, best[:, None], 2)[:, :, 0]
            C[a] = np.where(ok, np.take_along_axis(e[:, :16], best[:, None], 2)[:, :, 0], C[a]); L[a] = np.where(ok, nl, l)
            to = B * np.arange(I)[None, None, :] + (np.add.reduce(Q[a] * v, axis=1)[:, None, :] & (B - 1))
            to = np.broadcast_to(to, (8, 16, I)); np.put_along_axis(X[a], to, np.where(ok, v, np.take_along_axis(X[a], to, 2)), 2)
            F[a] = np.where(ok, (F[a] + v) >> 1, F[a]); A[a] = int(np.sum(ok))
    sums = np.add.reduce(X.reshape(N, 128, I, B), axis=3)
    return {"yc": C.reshape(N, 128, I).astype(np.float32).astype(BF), "yl": L.reshape(N, 128, I).astype(np.float32).astype(BF),
            "yf": F.reshape(N, 128, I).astype(np.float32).astype(BF), "ys": sums.astype(np.float32)}

@@ -1,0 +1,536 @@
+import numpy as np
+from concourse.mybir import dt, AluOpType as O, AxisListType, ActivationFunctionType as AF
+
+H2 = 64
+NV = {"A": 4, "B": 8}
+EQS = {"A": 1, "B": 0}
+LV = {"A": (1, 2), "B": (1, 2)}
+TILE = (1, 1, 2, 3, 3, 3)
+WID = {1: 10, 2: 12, 3: 15}
+RR = {1: list(range(8, -1, -1)), 2: list(range(12, 2, -1)) + [17], 3: list(range(16, 3, -1)) + [18]}
+SCRATCH = {}
+SEMAPHORES = ["sv", "ss", "st_", "sg", "loc", "arst1", "arst2"] + ["arr%d%s%s" % (t, x, h) for t in (1, 2) for x in "LC" for h in "AB"]
+SEMAPHORES += ["d%d" % k for k in range(16)]
+_BF, _F32, _I32 = "bfloat16", "float32", "int32"
+for _n, _c, _d in (("X", 4096 + 128, _BF), ("chs", 128, _BF), ("sps", 128, _BF), ("fls", 128, _BF), ("wts", 1, _BF), ("stI", 128, _I32),
+                   ("st16", 128, "uint16"), ("stin1", 128, "uint16"), ("stin2", 128, "uint16"), ("pI", 1, _I32), ("aI", 1, _I32), ("jneg", 6, _F32),
+                   ("qc", 1, _F32), ("qk", 6, _F32), ("nq", 6, _F32), ("iz", 1, _F32), ("q6", 1, _F32), ("q16", 1, _F32),
+                   ("ones", 128, _BF), ("bm0", 128, _BF), ("bm", 128, _BF), ("nbm", 128, _BF), ("idn", 128, _BF), ("nid", 128, _BF),
+                   ("tri", 128, _BF), ("shm", 512, _BF), ("hsd", 512, _BF), ("hsh", 512, _BF), ("hid", 256, _BF), ("kc", 128, _BF),
+                   ("half", 5, _F32), ("onec", 1, _F32), ("g8", 8, _F32), ("g8w", 8, _F32), ("Wm", 2048, _BF), ("Em", 2048, _BF), ("Es", 2048, _BF),
+                   ("jrow", 18, _F32), ("cqx", 18, _F32), ("dif", 17, _F32), ("dif8", 19, _F32), ("Rm", 19 * 128, _BF), ("il0", 4, _F32),
+                   ("il", 4, _F32), ("m6", 1536, _BF), ("m16", 64, _BF)):
+    SCRATCH[_n] = ("sbuf", [128, _c], _d)
+_PACK = {}
+_SMALL = {_BF: (("w", 64), ("b", 64), ("key", 64), ("Kp", 64), ("okS", 64), ("aL", 64), ("aM", 64), ("acc", 64), ("nok", 64), ("nokL", 64),
+                ("Vsel", 64), ("xo", 64), ("yfs", 64), ("Fs", 64), ("kb", 64), ("kt", 64), ("aT", 64), ("kq", 128)),
+          _F32: (("stf", 64), ("sta", 64), ("tt", 4), ("fd", 64), ("asum", 1), ("K1", 4), ("K2", 4), ("Kv", 4), ("S0", 64), ("yss", 64),
+                 ("base", 64), ("xd", 64), ("xe", 64), ("t1", 64)),
+          _I32: (("n1", 64), ("k8", 64), ("h0", 4), ("h1", 4), ("h2", 4), ("h3", 4), ("fi", 64), ("s0", 64), ("s1", 64), ("t2", 64), ("t4", 64), ("t5", 64))}
+for _h in "AB":
+    for _d, _names in _SMALL.items():
+        _at = 0
+        for _n, _c in _names:
+            _PACK[_n + _h] = ("pk" + _d[0] + _h, _at, _c)
+            _at += -(-_c // 32) * 32
+        SCRATCH["pk" + _d[0] + _h] = ("sbuf", [128, _at], _d)
+    for _n, _c, _d in (("z", 6144, _BF), ("VS", 6144, _BF), ("ind", 1024, _BF), ("off", 64, "uint16"), ("mk", 960, _BF), ("co", 960, _BF),
+                       ("AP", 448, _BF), ("ES", 256, _BF), ("EC", 256, _BF), ("EQ", 384, _BF), ("EN", 384, _BF), ("SQ", 320, _BF),
+                       ("voff", 4, "uint16"), ("toff", 4, "uint16")):
+        SCRATCH[_n + _h] = ("sbuf", [128, _c], _d)
+    for _q in (1, 2, 3):
+        for _n in ("L", "da", "db"):
+            SCRATCH["%s%d%s" % (_n, _q, _h)] = ("sbuf", [128, 64 * WID[_q]], _BF)
+    for _x in "LC":
+        for _t in (0, 1, 2):
+            SCRATCH["s%d%s%s" % (_t, _x, _h)] = ("sbuf", [128, 64], _BF)
+        for _t in (1, 2):
+            SCRATCH["in%d%s%s" % (_t, _x, _h)] = ("sbuf", [128, 64], _BF)
+    for _n in ("pU", "p37", "pV", "pM"):
+        SCRATCH[_n + _h] = ("psum", [128, 512], _F32)
+
+
+def rank_program(g, core, T, topo):
+    rank = T.rank_of(core)
+    if rank is None:
+        return
+    N = len(T.cores)
+    eng = {"v": g.vector, "s": g.scalar, "t": g.tensor, "y": g.sync, "g": g}
+    qsem = {"v": "sv", "s": "ss", "t": "st_", "g": "sg"}
+    CV, CS, CT = 0.00083 * 1.2, 0.00083 * 1.2, 0.00083 * 0.85
+    GATH = 0.07 + 1024 * 1.56 * CS
+    ops = []
+    lastw, readers, bank = {}, {}, {}
+    ndma, loc = [0], [0]
+
+    def B(name, a=0, b=None, step=1):
+        big, at, c = _PACK[name] if name in _PACK else (name, 0, SCRATCH[name][1][1])
+        e = c if b is None else b
+        return T[big][:, at + a:at + e:step] if step != 1 else T[big][:, at + a:at + e]
+
+    def add(q, cost, fns, r=(), w=(), banks=(), sem=None, extra=(), after=()):
+        k = len(ops)
+        deps = set(extra)
+        for x in r:
+            if x in lastw:
+                deps.add(lastw[x])
+            readers.setdefault(x, []).append(k)
+        for x in w:
+            if x in lastw:
+                deps.add(lastw[x])
+            deps.update(readers.get(x, ()))
+            lastw[x] = k
+            readers[x] = []
+        for x in banks:
+            st = bank.setdefault(x, [None, [], []])
+            if st[0] != q:
+                st[0], st[1], st[2] = q, st[2], []
+            deps.update(st[1])
+            st[2].append(k)
+        deps.discard(k)
+        ops.append({"q": q, "cost": cost, "fns": fns, "deps": deps, "all": deps | set(after), "sem": sem})
+        return k
+
+    def V(n, fn, r, w, banks=(), **kw):
+        return add("v", max(64, n) * CV, [fn], r, w, banks, **kw)
+
+    def S(n, fn, r, w, banks=()):
+        return add("s", 0.03 + max(40, n) * CS, [fn], r, w, banks)
+
+    def P(cols, fns, r, w, banks=(), **kw):
+        return add("t", 0.02 + cols * CT, fns, r, w, banks, **kw)
+
+    def TS(out, in0, s1, s2, o0, o1=None):
+        if o1 is None:
+            return lambda: g.vector.tensor_scalar(out, in0, s1, None, o0)
+        return lambda: g.vector.tensor_scalar(out, in0, s1, s2, o0, o1)
+
+    def TT(out, a, b, op):
+        return lambda: g.vector.tensor_tensor(out, a, b, op)
+
+    def CP(out, a):
+        return lambda: g.vector.tensor_copy(out, a)
+
+    def MS(ap, c):
+        return lambda: g.vector.memset(ap, c)
+
+    def SCAN(out, d0, d1, o0, o1):
+        return lambda: g.vector.tensor_tensor_scan(out, d0, d1, 0.0, o0, o1)
+
+    def TURN(out, a):
+        return lambda: g.vector.transpose(out, a)
+
+    def ACT(out, in_, f, **kw):
+        return lambda: g.scalar.activation(out, in_, f, **kw)
+
+    def MM(out, l, r, a, z):
+        return lambda: g.tensor.matmul(out, l, r, a, z)
+
+    def dma(q, out, in_, r, w, cost=2.2):
+        s = "d%d" % ndma[0]
+        ndma[0] += 1
+        return add(q, cost, [lambda: eng[q].dma_start(out, in_)], r, w, sem=(s, 16))
+
+    def aff(out, in_, pat, cmp, base, cm, r, w):
+        return add("g", 0.4, [lambda: g.affine_select(out, in_, pat, cmp, 0.0, base, cm)], r, w)
+
+    def iota(out, pat, base, cost, w):
+        add("g", cost, [lambda: g.iota(out, pat, base, 0, allow_small_or_imprecise_dtypes=True)], (), w)
+
+    NE = min(len(topo.engines(core, c)) for c in T.cores if c != core)
+
+    def send(name_in, name_out, sem, hop, r):
+        dst = T.cores[(rank + hop) % N]
+        rid, pid = topo.addr(dst)[:2]
+        lanes = sum(1 << e for e in topo.engines(core, dst)[:NE])
+        loc[0] += NE
+        k = add("g", 0.3, [lambda: g.remote_dma(T[name_out][:], T[name_in][:], T.sem[sem], T.sem.loc, pid, rid, lanes)], r, (), sem=("loc", None))
+        return add("r", 3.5, [], (), (name_out,), sem=(sem, NE), extra=(k,))
+
+    dma("s", T.stI[:], T.st[:], (), ("stI",))
+    dma("y", T.sps[:], T.sp[:], (), ("sps",))
+    dma("y", T.X[:, 0:4096], T.x[:], (), ("X",), 6.0)
+    dma("s", T.wts[:], T.wt[:], (), ("wts",))
+    dma("s", T.chs[:], T.ch[:], (), ("chs",))
+    dma("s", T.fls[:], T.fl[:], (), ("fls",))
+    V(64, MS(T.X[:, 4096:4224], 0.0), (), ("Xd",))
+    V(128, CP(T.st16[:], T.stI[:]), ("stI",), ("st16",))
+    send("st16", "stin1", "arst1", 1, ("st16",))
+    send("st16", "stin2", "arst2", 2, ("st16",))
+    add("g", 0.2, [lambda: g.iota(T.pI[:], [[0, 1]], 0, 1)], (), ("pI",))
+    iota(T.jrow[:], [[1, 18]], -1, 0.2, ("jrow",))
+    iota(T.jneg[:], [[-1, 6]], 0, 0.2, ("jneg",))
+    iota(T.il0[:], [[16, 4]], 0, 0.2, ("il0",))
+    V(64, MS(T.ones[:], 1.0), (), ("ones",))
+    V(1, TS(T.aI[:], T.pI[:], 15, None, O.bitwise_and), ("pI",), ("aI",))
+    V(1, CP(T.qc[:], T.aI[:]), ("aI",), ("qc",))
+    V(6, TS(T.qk[:], T.jneg[:], T.qc[:], None, O.add), ("jneg", "qc"), tuple("qk%d" % k for k in range(6)))
+    V(5, TS(T.half[:], T.jneg[:, 0:5], 0.5, None, O.add), ("jneg",), tuple("half%d" % l for l in range(5)))
+    V(1, MS(T.onec[:], 1.0), (), ("onec",))
+    V(1, TS(T.iz[:], T.qc[:], 0.0, None, O.is_equal), ("qc",), ("iz",))
+    V(1, TS(T.q6[:], T.qc[:], 6.0, None, O.mult), ("qc",), ("q6",))
+    V(1, TS(T.q16[:], T.qc[:], -1.0, 16.0, O.mult, O.add), ("qc",), ("q16",))
+    V(6, TS(T.nq[:], T.qk[:], -1.0, None, O.mult), tuple("qk%d" % k for k in range(6)), ("nq",))
+    aff(T.bm0[:], T.ones[:], [[-16, 8], [0, 16]], O.is_ge, 0, 1, ("ones",), ("bm0",))
+    aff(T.bm[:], T.bm0[:], [[16, 8], [0, 16]], O.is_ge, 15, -1, ("bm0",), ("bm",))
+    aff(T.idn[:], T.ones[:], [[-1, 128]], O.is_equal, 0, 1, ("ones",), ("idn",))
+    V(4, TS(T.il[:], T.il0[:], T.qc[:], None, O.add), ("il0", "qc"), ("il",))
+    V(18, TS(T.cqx[:], T.jrow[:], T.qc[:], None, O.is_equal), ("jrow", "qc"), ("cqx",))
+    V(17, TT(T.dif[:], T.cqx[:, 1:18], T.cqx[:, 0:17], O.subtract), ("cqx",), ("dif",))
+    V(17, TS(T.dif8[:, 0:17], T.dif[:], 8.0, None, O.mult), ("dif",), ("dif8a",))
+    V(2, TS(T.dif8[:, 17:19], T.cqx[:, 3:5], 8.0, None, O.mult), ("cqx",), ("dif8b",))
+    for r in list(range(8, -1, -1)) + [17, 18] + list(range(16, 8, -1)):
+        tok = ("bm", "dif8b" if r > 16 else "dif8a")
+        if r < 9:
+            V(64, TS(T.Rm[:, r * 128:(r + 1) * 128], T.bm[:], T.dif8[:, r:r + 1], None, O.mult), tok, ("Rm%d" % r,))
+        else:
+            S(128, ACT(T.Rm[:, r * 128:(r + 1) * 128], T.bm[:], AF.Copy, scale=T.dif8[:, r:r + 1]), tok, ("Rm%d" % r,))
+    V(8, CP(T.g8[:], T.bm[:, 0::16]), ("bm",), ("g8",))
+    V(8, TS(T.g8w[:], T.g8[:], T.wts[:], None, O.mult), ("g8", "wts"), ("g8w",))
+    V(1024, MS(T.Wm[:], 0.0), (), ("Wz",))
+    V(1024, MS(T.Em[:], 0.0), (), ("Ez",))
+    for gg in range(8):
+        sl = slice(16 * gg, 16 * gg + 15 * 129 + 1, 129)
+        S(16, ACT(T.Wm[:, sl], T.ones[:, 0:16], AF.Copy, scale=T.g8w[:, gg:gg + 1]), ("g8w", "Wz", "ones"), ("Wm%d" % gg,))
+    for gg in range(8):
+        sl = slice(16 * gg, 16 * gg + 15 * 129 + 1, 129)
+        S(16, ACT(T.Em[:, sl], T.ones[:, 0:16], AF.Copy, scale=T.g8[:, gg:gg + 1]), ("g8", "Ez", "ones"), ("Em%d" % gg,))
+    EM = tuple("Em%d" % m for m in range(8))
+    WM = tuple("Wm%d" % m for m in range(8))
+    V(1024, TS(T.Es[:], T.Em[:], 160.0, None, O.mult), EM, ("Es",))
+    V(64, MS(T.kc[0:64, :], -512.0), (), ("kc0",))
+    V(64, MS(T.kc[64:128, :], 0.0625), (), ("kc1",))
+    V(64, TS(T.nid[:], T.idn[:], -1.0, None, O.mult), ("idn",), ("nid",))
+    V(64, TS(T.nbm[:], T.bm[:], -1.0, None, O.mult), ("bm",), ("nbm",))
+    aff(T.tri[:], T.bm[:], [[1, 128]], O.is_ge, 0, -1, ("bm",), ("tri",))
+    for l in range(1, 5):
+        aff(T.shm[:, (l - 1) * 128:l * 128], T.bm[:], [[-1, 128]], O.is_equal, -l, 1, ("bm",), ("shm%d" % l,))
+    for l in range(1, 5):
+        V(256, TT(T.hsd[:, (l - 1) * 128:l * 128], T.shm[:, (l - 1) * 128:l * 128],
+                  T.idn[:] if l == 1 else T.shm[:, (l - 2) * 128:(l - 1) * 128], O.subtract),
+          ("shm%d" % l, "idn" if l == 1 else "shm%d" % (l - 1)), ("hsd%d" % l,))
+    V(256, TS(T.hsh[:], T.hsd[:], 0.5, None, O.mult), ("hsd1", "hsd2", "hsd3", "hsd4"), ("hsh",))
+    V(64, TS(T.hid[:, 0:128], T.idn[:], 0.5, None, O.mult), ("idn",), ("hid0",))
+    V(64, TS(T.hid[:, 128:256], T.shm[:, 384:512], 0.5, None, O.mult), ("shm4",), ("hid1",))
+    V(768, MS(T.m6[:], 1.0), (), ("m6",))
+    V(256, MS(T.m6[:, 0::6], 0.0), (), ("m6",))
+    V(64, MS(T.m16[:], 1.0), (), ("m16",))
+    V(8, MS(T.m16[:, 0::16], 0.0), (), ("m16",))
+    for hi, h in enumerate("AB"):
+        for q in (1, 2, 3):
+            n = WID[q]
+            a, b, l = ("%s%d%s" % (x, q, h) for x in ("da", "db", "L"))
+            for x in (a, b):
+                if q == 1:
+                    V(n * 32, MS(T[x][:], 1.0), (), (x,))
+                else:
+                    iota(T[x][:], [[0, 64 * n]], 1, 0.13 + n * 128 * CS, (x,))
+            S(64, ACT(T[a][:, 0::n], T.ones[:, 0:64], AF.Copy, scale=64.0), ("ones",), (a,))
+            S(64, ACT(T[b][:, 1::n], T.ones[:, 0:64], AF.Copy, scale=0.0), ("ones",), (b,))
+            S(64, ACT(T[l][:, 0::n], T.ones[:, 0:64], AF.Copy, scale=0.0), ("ones",), (l + "z",))
+        V(4, TS(B("K1" + h), T.il[:], 31.0, float(31 * H2 * hi - 4096), O.mult, O.add), ("il",), ("K1" + h,))
+        V(4, TS(B("K2" + h), T.il[:], float(4096 + H2 * hi), None, O.add), ("il",), ("K2" + h,))
+        V(4, TS(B("Kv" + h), T.il[:], 96.0, 5.0, O.mult, O.add), ("il",), ("Kv" + h,))
+        V(64, MS(T["AP" + h][:, 0:64], 0.0), (), ("AP0" + h,))
+        V(64, TS(T["EQ" + h][:, 0:64], T.ones[:, 0:64], T.iz[:], None, O.mult), ("ones", "iz"), ("EQ0" + h,))
+        V(1, MS(B("asum" + h), 0.0), (), ("asum" + h,))
+        V(64, CP(T["pV" + h][:, 448:512], T.fls[:, H2 * hi:H2 * hi + H2]), ("fls",), ("F" + h,), ("pV" + h,))
+        V(64, CP(B("Fs" + h), T.fls[:, H2 * hi:H2 * hi + H2]), ("fls",), ("Fs" + h,))
+        V(64, MS(B("kq" + h), -1.25), (), ("kq" + h,))
+        for m in range(NV[h]):
+            V(64, MS(B("kq" + h, m, 128, 16), -10.625), (), ("kq" + h,))
+
+    def rec(t, h):
+        o = H2 * "AB".index(h)
+        if t == 0:
+            return T.chs[:, o:o + H2], T.sps[:, o:o + H2], "chs", "sps"
+        c, l = "in%dC%s" % (t, h), "in%dL%s" % (t, h)
+        return T[c][:], T[l][:], c, l
+
+    def vm(h, m):
+        return T["VS" + h][:, 6 * m + 5::96]
+
+    def entry(k, h):
+        q = TILE[k]
+        n = WID[q]
+        L = "L%d%s" % (q, h)
+        V(n * 32, SCAN(T["mk" + h][:, 0:64 * n], T["da%d%s" % (q, h)][:], T["db%d%s" % (q, h)][:], O.add, O.min),
+          ("da%d%s" % (q, h), "db%d%s" % (q, h)), ("mk" + h,))
+        V(n * 32, SCAN(T["co" + h][:, 0:64 * n], T["mk" + h][:, 0:64 * n], T[L][:], O.mult, O.add),
+          ("mk" + h, L + "z") + tuple("%s_%d" % (L, r) for r in RR[q]), ("co" + h,))
+        if k < 5:
+            V(64, TS(B("w" + h), T["co" + h][:, n - 1:64 * n:n], 0.25, 2.0, O.mult, O.add), ("co" + h,), ("w" + h,))
+
+    for t in range(3):
+        last = t == 2
+        for hi, h in enumerate("AB"):
+            C, L, ct, lt = rec(t, h)
+            pV, pM, pU, p37 = T["pV" + h], T["pM" + h], T["pU" + h], T["p37" + h]
+            o = H2 * hi
+            src, stt = ((T.stI, "stI"), (T.stin1, "stin1"), (T.stin2, "stin2"))[t]
+            V(64, CP(B("stf" + h), src[:, o:o + H2]), (stt,), ("stf" + h,))
+            V(64, TS(B("sta" + h), B("stf" + h), B("asumA"), B("asumB"), O.add, O.add), ("stf" + h, "asumA", "asumB"), ("sta" + h,))
+            V(64, TS(B("base" + h), L, 613.0, None, O.mult), (lt,), ("base" + h,))
+            V(128, TT(B("s0" + h), B("base" + h), B("sta" + h), O.add), ("base" + h, "sta" + h), ("s0" + h,))
+            V(64, TS(B("s1" + h), B("s0" + h), 4095, None, O.bitwise_and), ("s0" + h,), ("s1" + h,))
+            V(64, CP(T["off" + h][:], B("s1" + h)), ("s1" + h,), ("off" + h,))
+            V(64, CP(pV[:, 384:448], L), (lt,), ("L" + h,), ("pV" + h,))
+            S(64, ACT(B("Kp" + h), L, AF.Identity, scale=16.0, bias=T.q16[:]), (lt, "q16"), ("Kp" + h,))
+            S(64, ACT(T["da1" + h][:, 1::10], L, AF.Copy, scale=T.iz[:]), (lt, "iz"), ("da1" + h,))
+            S(64, ACT(T["db1" + h][:, 0::10], T.ones[:, 0:64], AF.Copy, scale=-8.0), ("ones",), ("db1" + h,))
+            P(512, [MM(pM[:, 64 * j:64 * j + 64], T.Rm[:, (8 - j) * 128:(9 - j) * 128], C, True, True) for j in range(8)],
+              (ct,) + tuple("Rm%d" % (8 - j) for j in range(8)), ("dM" + h,), ("pM" + h,))
+            P(192, [MM(pU[:, 64 * j:64 * j + 64], T.Rm[:, r * 128:(r + 1) * 128], C, True, True) for j, r in enumerate((0, 17, 18))],
+              (ct, "Rm0", "Rm17", "Rm18"), ("dU" + h,), ("pU" + h,))
+            P(512, [MM(p37[:, 64 * j:64 * j + 64], T.Rm[:, (16 - j) * 128:(17 - j) * 128], C, True, True) for j in range(8)],
+              (ct,) + tuple("Rm%d" % (16 - j) for j in range(8)), ("d37" + h,), ("p37" + h,))
+            at = {r: (pM, 8 - r, "dM" + h, "pM" + h) for r in range(1, 9)}
+            at.update({r: (p37, 16 - r, "d37" + h, "p37" + h) for r in range(9, 17)})
+            at.update({r: (pU, j, "dU" + h, "pU" + h) for j, r in enumerate((0, 17, 18))})
+            for q in (1, 2, 3):
+                n = WID[q]
+                todo = list(enumerate(RR[q]))
+                for j, r in (todo if q == 1 else todo[::-1]):
+                    ps, jj, tk, bk = at[r]
+                    out, in_ = T["L%d%s" % (q, h)][:, 1 + j::n], ps[:, 64 * jj:64 * jj + 64]
+                    low = r in (0, 17, 18)
+                    if q in LV[h]:
+                        V(64, TS(out, in_, -4.0, None, O.add) if low else CP(out, in_), (tk,), ("L%d%s_%d" % (q, h, r),), (bk,))
+                    else:
+                        S(64, ACT(out, in_, AF.Copy, bias=-4.0) if low else ACT(out, in_, AF.Copy), (tk,), ("L%d%s_%d" % (q, h, r),), (bk,))
+            entry(0, h)
+        for k in range(6):
+            for h in "AB":
+                pV, pU = T["pV" + h], T["pU" + h]
+                n = WID[TILE[k]]
+                c8 = T["co" + h][:, n - 1:64 * n:n]
+                zk, z = "z%d%s" % (k, h), T["z" + h]
+                add("s", GATH, [lambda o_=z[:, k::6], f_=T["off" + h]: g.scalar.activation(o_, T.X[:, 0:4096].indirect(f_[:, 0:64]), AF.Copy)],
+                    ("X", "off" + h), (zk,))
+                P(17 * 64, [MM(pU[:, 0:64], T.kc[:], T.ones[:, 0:64], True, False)]
+                  + [MM(pU[:, 0:64], T.Wm[:, 128 * m:128 * m + 128], z[:, 6 * m + k::96], False, m == 15) for m in range(16)],
+                  (zk, "kc0", "kc1", "ones") + WM, ("u" + h,), ("pU" + h,))
+                y4 = pU[:, 0:64]
+                if k < 5:
+                    V(64, TT(B("t1" + h), y4, B("w" + h), O.mult), ("u" + h, "w" + h), ("t1" + h,), ("pU" + h,))
+                    V(64, TS(pU[:, 64:128], y4, 37.0, -148.0, O.mult, O.add), ("u" + h,), ("t3" + h,), ("pU" + h,))
+                    V(64, TS(B("t2" + h), B("t1" + h), 0.125, -0.9375, O.mult, O.add), ("t1" + h,), ("t2" + h,))
+                    V(64, TT(B("t4" + h), B("t2" + h), pU[:, 64:128], O.add), ("t2" + h, "t3" + h), ("t4" + h,), ("pU" + h,))
+                    V(64, TS(B("t5" + h), B("t4" + h), 4095, None, O.bitwise_and), ("t4" + h,), ("t5" + h,))
+                    V(64, CP(T["off" + h][:], B("t5" + h)), ("t5" + h,), ("off" + h,))
+                V(64, TT(B("k8" + h), y4, c8, O.add), ("u" + h, "co" + h), ("k8" + h,), ("pU" + h,))
+                V(64, TS(B("n1" + h), B("k8" + h), 3, 3, O.arith_shift_right, O.bitwise_and), ("k8" + h,), ("n1" + h,))
+                Pk, pt = pV[:, 64 * k:64 * k + 64], "P%d%s" % (k + 1, h)
+                if k == 0:
+                    V(64, CP(Pk, B("n1" + h)), ("n1" + h,), (pt,), ("pV" + h,))
+                else:
+                    V(64, TT(Pk, B("n1" + h), pV[:, 64 * k - 64:64 * k], O.add), ("n1" + h, "P%d%s" % (k, h)), (pt,), ("pV" + h,))
+                if k < 5:
+                    q = TILE[k + 1]
+                    n2, da, db = WID[q], "da%d%s" % (q, h), "db%d%s" % (q, h)
+                    V(64, TS(T[db][:, 0::n2], Pk, float(k + 1 - RR[q][0]), None, O.add), (pt,), (db,), ("pV" + h,))
+                    V(64, TS(B("b" + h), Pk, T.qk[:, k + 1:k + 2], None, O.is_ge), (pt, "qk%d" % (k + 1)), ("b" + h,), ("pV" + h,))
+                    V(64, TT(T[da][:, 1::n2], B("b" + h), pV[:, 384:448], O.mult), ("b" + h, "L" + h), (da,), ("pV" + h,))
+                    entry(k + 1, h)
+        if last:
+            for hi, h in enumerate("AB"):
+                pM = T["pM" + h]
+                P(2048, [MM(pM[:, 0:64], T.idn[:], T.X[:, 2048 * hi + j:2048 * hi + 2048:32], j == 0, j == 31) for j in range(32)],
+                  ("X", "idn"), ("sums" + h,), ("pM" + h,))
+                V(64, CP(B("S0" + h), pM[:, 0:64]), ("sums" + h,), ("S0" + h,), ("pM" + h,))
+        for hi, h in enumerate("AB"):
+            C, L, ct, lt = rec(t, h)
+            pV, pM, pU, p37 = T["pV" + h], T["pM" + h], T["pU" + h], T["p37" + h]
+            tbn = "pUA" if h == "A" else "pMA"
+            tb = T[tbn]
+            o = H2 * hi
+            sL, sC = "s%dL%s" % (t, h), "s%dC%s" % (t, h)
+            for j in range(4):
+                sl = slice(1536 * j, 1536 * j + 1536)
+                V(768, SCAN(T["VS" + h][:, sl], T.m6[:], T["z" + h][:, sl], O.mult, O.max), tuple("z%d%s" % (k, h) for k in range(6)) + ("m6",), ("VS%d%s" % (j, h),))
+            vt = tuple("VS%d%s" % (j, h) for j in range(4))
+            for c, m0 in enumerate(range(NV[h], 16, 8)):
+                ms = range(m0, min(16, m0 + 8))
+                ps, bk = (p37, "p37" + h) if c == 0 else (pM, "pM" + h)
+                mm = []
+                for j, m in enumerate(ms):
+                    mm += [MM(ps[:, 64 * j:64 * j + 64], T.idn[:], vm(h, m), True, False), MM(ps[:, 64 * j:64 * j + 64], T.nid[:], B("Fs" + h), False, True)]
+                P(128 * len(ms), mm, vt + ("Fs" + h, "idn", "nid"), ("VF%d%s" % (c, h),), (bk,))
+                S(64 * len(ms), ACT(T["ind" + h][:, 64 * m0:64 * (m0 + len(ms))], ps[:, 0:64 * len(ms)], AF.Sign, bias=T.half[:, 0:1]),
+                  ("VF%d%s" % (c, h), "half0"), tuple("ind%d%s" % (m, h) for m in ms), (bk,))
+            for m in range(NV[h]):
+                V(64, TT(T["ind" + h][:, 64 * m:64 * m + 64], vm(h, m), pV[:, 448:512], O.is_ge), vt + ("F" + h,), ("ind%d%s" % (m, h),), ("pV" + h,))
+            prev = ()
+            for c in range(2):
+                prev = (P(512, ([MM(pU[:, 0:64], B("kq" + h), T.ones[:, 0:64], True, False)] if c == 0 else [])
+                          + [MM(pU[:, 0:64], T.Es[:, 128 * m:128 * m + 128], T["ind" + h][:, 64 * m:64 * m + 64], False, m == 15) for m in range(8 * c, 8 * c + 8)],
+                          tuple("ind%d%s" % (m, h) for m in range(8 * c, 8 * c + 8)) + ("Es", "kq" + h, "ones"), ("cnt%d%s" % (c, h),), ("pU" + h,), after=prev),)
+            V(64, TT(B("key" + h), pU[:, 0:64], B("Kp" + h), O.min), ("cnt0" + h, "cnt1" + h, "Kp" + h), ("key" + h,), ("pU" + h,))
+            kb, acc = B("kb" + h), B("acc" + h)
+            V(64, TURN(B("kt" + h), B("key" + h)), ("key" + h,), ("kt" + h,))
+            V(64, SCAN(kb, T.m16[:], B("kt" + h), O.mult, O.max), ("kt" + h, "m16"), ("kb" + h,))
+            for j in range(4):
+                V(64, TS(B("aT" + h, 16 * j, 16 * j + 16), B("kt" + h, 16 * j, 16 * j + 16), B("kb" + h, 16 * j + 15, 16 * j + 16), None, O.is_equal),
+                  ("kt" + h, "kb" + h), ("aT%d%s" % (j, h),))
+            V(64, TURN(acc, B("aT" + h)), tuple("aT%d%s" % (j, h) for j in range(4)), ("acc" + h,))
+            P(128, [MM(p37[:, 384:448], T.bm[:], acc, True, True), MM(p37[:, 448:512], T.ones[:], acc, True, True)],
+              ("acc" + h, "bm", "ones"), ("okB" + h,), ("p37" + h,))
+            AP = T["AP" + h]
+            for k in range(1, 7):
+                V(64, TT(AP[:, 64 * k:64 * k + 64], acc, pV[:, 64 * k - 64:64 * k], O.mult), ("acc" + h, "P%d%s" % (k, h)), ("AP%d%s" % (k, h),), ("pV" + h,))
+            S(64, ACT(B("okS" + h), p37[:, 384:448], AF.Copy), ("okB" + h,), ("okS" + h,), ("p37" + h,))
+            S(64, ACT(B("nok" + h), p37[:, 384:448], AF.Copy, scale=-1.0, bias=1.0), ("okB" + h,), ("nok" + h,), ("p37" + h,))
+            if not last:
+                V(64, lambda a_=B("asum" + h), b_=p37[:, 448:512]: g.vector.tensor_reduce(a_, b_, AxisListType.X, O.add), ("okB" + h,), ("asum" + h,), ("p37" + h,))
+            apt = tuple("AP%d%s" % (k, h) for k in range(7))
+            P(320, [MM(pU[:, 192:512], T.bm[:], AP[:, 64:384], True, True)], apt[1:6] + ("bm",), ("Pst" + h,), ("pU" + h,))
+            P(768, [MM(p37[:, 0:384], T.bm[:], AP[:, 64:448], True, False), MM(p37[:, 0:384], T.nbm[:], AP[:, 0:384], False, True)],
+              apt + ("bm", "nbm"), ("Nst" + h,), ("p37" + h,))
+            V(64, TT(B("aL" + h), acc, pV[:, 384:448], O.mult), ("acc" + h, "L" + h), ("aL" + h,), ("pV" + h,))
+            if EQS[h]:
+                for k in range(1, 6):
+                    S(64, ACT(T["SQ" + h][:, 64 * k - 64:64 * k], pU[:, 128 + 64 * k:192 + 64 * k], AF.Square, bias=T.nq[:, k:k + 1]),
+                      ("Pst" + h, "nq"), ("SQ%d%s" % (k, h),), ("pU" + h,))
+                S(320, ACT(T["EQ" + h][:, 64:384], T["SQ" + h][:], AF.Relu, scale=-1.0, bias=T.onec[:]), tuple("SQ%d%s" % (k, h) for k in range(1, 6)) + ("onec",),
+                  tuple("EQ%d%s" % (k, h) for k in range(1, 6)))
+            else:
+                for k in range(1, 6):
+                    V(64, TS(T["EQ" + h][:, 64 * k:64 * k + 64], pU[:, 128 + 64 * k:192 + 64 * k], T.qk[:, k:k + 1], None, O.is_equal),
+                      ("Pst" + h, "qk%d" % k), ("EQ%d%s" % (k, h),), ("pU" + h,))
+            V(384, TT(T["EN" + h][:], T["EQ" + h][:], p37[:, 0:384], O.mult), ("Nst" + h,) + tuple("EQ%d%s" % (k, h) for k in range(6)), ("EN" + h,), ("p37" + h,))
+            V(64, TT(B("nokL" + h), B("nok" + h), pV[:, 384:448], O.mult), ("nok" + h, "L" + h), ("nokL" + h,), ("pV" + h,))
+            P(512, [MM(p37[:, 384:448], T.idn[:], B("nokL" + h), True, False), MM(p37[:, 384:448], T.bm[:], acc, False, False)]
+              + [MM(p37[:, 384:448], T.idn[:], T["EN" + h][:, 64 * k:64 * k + 64], False, k == 5) for k in range(6)],
+              ("EN" + h, "nokL" + h, "acc" + h, "idn", "bm"), ("ls" + h,), ("p37" + h,))
+            S(64, ACT(T[sL][:], p37[:, 384:448], AF.Copy), ("ls" + h,), (sL,), ("p37" + h,))
+            if not last:
+                send(sL, "in%dL%s" % (t + 1, h), "arr%dL%s" % (t + 1, h), 1, (sL,))
+            else:
+                dma("y", T.yl[:, o:o + H2], T[sL][:], (sL,), ())
+            P(256, [MM(pM[:, 64 * l:64 * l + 64], T.hsh[:, 128 * l:128 * l + 128], C, True, True) for l in range(4)], (ct, "hsh"), ("SH" + h,), ("pM" + h,))
+            P(64, [MM(pM[:, 320:384], T.tri[:], B("aL" + h), True, True)], ("aL" + h, "tri"), ("sh" + h,), ("pM" + h,))
+            for l in range(1, 5):
+                S(64, ACT(T["ES" + h][:, 64 * l - 64:64 * l], pM[:, 320:384], AF.Sign, bias=T.half[:, l:l + 1]), ("sh" + h, "half%d" % l), ("ES%d%s" % (l, h),), ("pM" + h,))
+            V(256, TT(T["EC" + h][:], T["ES" + h][:], pM[:, 0:256], O.mult), ("SH" + h,) + tuple("ES%d%s" % (l, h) for l in range(1, 5)), ("EC" + h,), ("pM" + h,))
+            P(384, [MM(pM[:, 384:448], T.hid[:, 0:128], C, True, False), MM(pM[:, 384:448], T.hid[:, 128:256], C, False, False)]
+              + [MM(pM[:, 384:448], T.idn[:], T["EC" + h][:, 64 * l:64 * l + 64], False, l == 3) for l in range(4)],
+              ("EC" + h, "idn", "hid0", "hid1", ct), ("cs" + h,), ("pM" + h,))
+            S(64, ACT(T[sC][:], pM[:, 384:448], AF.Copy), ("cs" + h,), (sC,), ("pM" + h,))
+            if not last:
+                send(sC, "in%dC%s" % (t + 1, h), "arr%dC%s" % (t + 1, h), 1, (sC,))
+            else:
+                dma("y", T.yc[:, o:o + H2], T[sC][:], (sC,), ())
+            S(64, ACT(B("aM" + h), acc, AF.Copy, scale=T.q6[:]), ("acc" + h, "q6"), ("aM" + h,))
+            P(1024, [MM(tb[:, 0:8], T.Em[:, 128 * a:128 * a + 128], B("aM" + h, a, 128, 16), a == 0, a == 15) for a in range(16)],
+              ("aM" + h, "acc" + h) + EM, ("tb" + h,), (tbn,))
+            V(4, TT(T["voff" + h][:], tb[:, 0:4], B("Kv" + h), O.add), ("tb" + h, "Kv" + h), ("voff" + h,), (tbn,))
+            V(4, CP(B("tt" + h), tb[:, 4:8]), ("tb" + h,), ("okd" + h,), (tbn,))
+            add("s", 0.16, [lambda o_=B("Vsel" + h), v_=T["VS" + h], f_=T["voff" + h]: g.scalar.activation(o_, v_[:, 0:6144].indirect(f_[:, 0:4]), AF.Copy)],
+                vt + ("voff" + h,), ("Vsel" + h,))
+            P(1024, [MM(tb[:, 8:12], T.Wm[:, 128 * a:128 * a + 128], B("Vsel" + h, a, 64, 16), a == 0, a == 15) for a in range(16)],
+              ("Vsel" + h,) + WM, ("hd" + h,), (tbn,))
+            V(4, CP(B("h0" + h), tb[:, 8:12]), ("hd" + h,), ("h0" + h,), (tbn,))
+            V(4, TS(B("h1" + h), B("h0" + h), 31, None, O.bitwise_and), ("h0" + h,), ("h1" + h,))
+            V(4, TT(B("h2" + h), B("h1" + h), B("K1" + h), O.add), ("h1" + h, "K1" + h), ("h2" + h,))
+            V(4, TT(B("h3" + h), B("h2" + h), B("tt" + h), O.mult), ("h2" + h, "okd" + h), ("h3" + h,))
+            V(4, TT(T["toff" + h][:], B("h3" + h), B("K2" + h), O.add), ("h3" + h, "K2" + h), ("toff" + h,))
+            if not last:
+                add("v", 0.25, [lambda f_=T["toff" + h], i_=B("Vsel" + h): g.vector.tensor_copy(T.X[:, 0:4224].indirect(f_[:, 0:4]), i_)],
+                    ("toff" + h, "Vsel" + h, "Xd"), ("X",))
+            else:
+                add("s", 0.16, [lambda o_=B("xo" + h), f_=T["toff" + h]: g.scalar.activation(o_, T.X[:, 0:4224].indirect(f_[:, 0:4]), AF.Copy)],
+                    ("X", "Xd", "toff" + h), ("xo" + h,))
+                V(128, TT(B("xd" + h), B("Vsel" + h), B("xo" + h), O.subtract), ("Vsel" + h, "xo" + h), ("xd" + h,))
+                V(128, TT(B("xe" + h), B("xd" + h), B("okS" + h), O.mult), ("xd" + h, "okS" + h), ("xe" + h,))
+                V(128, TT(B("yss" + h), B("xe" + h), B("S0" + h), O.add), ("xe" + h, "S0" + h), ("yss" + h,))
+                dma("s", T.ys[:, o:o + H2], B("yss" + h), ("yss" + h,), ())
+            Fp = pV[:, 448:512]
+            V(64, TT(B("fd" + h), B("Vsel" + h), Fp, O.subtract), ("Vsel" + h, "F" + h), ("fd" + h,), ("pV" + h,))
+            V(128, TT(B("xd" + h), B("fd" + h), B("okS" + h), O.mult), ("fd" + h, "okS" + h), ("xd" + h,))
+            V(64, TS(B("fi" + h), B("xd" + h), 0.5, -0.25, O.mult, O.add), ("xd" + h,), ("fi" + h,))
+            if not last:
+                V(64, TT(B("Fs" + h), B("fi" + h), Fp, O.add), ("fi" + h, "F" + h), ("Fs" + h,), ("pV" + h,))
+                V(64, TT(Fp, B("fi" + h), Fp, O.add), ("fi" + h, "F" + h), ("F" + h,), ("pV" + h,))
+            else:
+                V(64, TT(B("yfs" + h), B("fi" + h), Fp, O.add), ("fi" + h, "F" + h), ("yfs" + h,), ("pV" + h,))
+                dma("s", T.yf[:, o:o + H2], B("yfs" + h), ("yfs" + h,), ())
+
+    n = len(ops)
+    succ = [[] for _ in range(n)]
+    for k, p in enumerate(ops):
+        for d in p["all"]:
+            succ[d].append(k)
+    prio = [0.0] * n
+    for k in range(n - 1, -1, -1):
+        prio[k] = ops[k]["cost"] + 0.1 + max([prio[s] for s in succ[k]], default=0.0)
+    left = [len(p["all"]) for p in ops]
+    ready = [0.0] * n
+    free, pool, order = {}, {}, []
+    for k in range(n):
+        if left[k] == 0:
+            pool.setdefault(ops[k]["q"], []).append(k)
+    while len(order) < n:
+        best = None
+        for q, lst in pool.items():
+            if lst:
+                s0 = max(free.get(q, 0.0) if q != "r" else 0.0, min(ready[k] for k in lst))
+                if best is None or s0 < best[0]:
+                    best = (s0, q)
+        s0, q = best
+        k = max((k for k in pool[q] if ready[k] <= s0 + 0.02), key=lambda k: prio[k])
+        s0 = max(s0, ready[k])
+        pool[q].remove(k)
+        order.append(k)
+        hold = 0.1 if (ops[k]["sem"] is not None and q != "r") else ops[k]["cost"]
+        free[q] = s0 + hold
+        end = s0 + ops[k]["cost"]
+        for s in succ[k]:
+            ready[s] = max(ready[s], end + (0.15 if ops[s]["q"] == q else 0.25))
+            left[s] -= 1
+            if left[s] == 0:
+                pool.setdefault(ops[s]["q"], []).append(s)
+    count = {q: 0 for q in qsem}
+    know = {q: {} for q in eng}
+    done, seen = {}, {}
+    for k in order:
+        p = ops[k]
+        q = p["q"]
+        if q == "r":
+            done[k], seen[k] = p["sem"], {}
+            continue
+        need, via = {}, {}
+        for d in p["deps"]:
+            if done[d] is None:
+                continue
+            s, v = done[d]
+            if know[q].get(s, 0) < v:
+                need[s] = max(need.get(s, 0), v)
+                for s2, v2 in seen[d].items():
+                    via[s2] = max(via.get(s2, 0), v2)
+        for s, v in need.items():
+            eng[q].wait_ge(T.sem[s], v)
+            know[q][s] = max(know[q].get(s, 0), v)
+        for s, v in via.items():
+            know[q][s] = max(know[q].get(s, 0), v)
+        seen[k] = dict(know[q])
+        if p["sem"] is not None:
+            s, v = p["sem"]
+            ins = p["fns"][0]()
+            if v is None:
+                done[k] = None
+            else:
+                ins.then_inc(T.sem[s], v)
+                done[k] = (s, v)
+        else:
+            for f in p["fns"]:
+                f().then_inc(T.sem[qsem[q]], 1)
+                count[q] += 1
+            done[k] = (qsem[q], count[q])
+    for q, s in qsem.items():
+        g.wait_ge(T.sem[s], count[q])
+    for j in range(ndma[0]):
+        g.wait_ge(T.sem["d%d" % j], 16)
+    for p in ops:
+        if p["q"] == "r":
+            g.wait_ge(T.sem[p["sem"][0]], p["sem"][1])
+    g.wait_ge(T.sem.loc, loc[0])

@@ -1,32 +1,33 @@
+import math
 import numpy as np
-from concourse.mybir import dt, AluOpType as O, AxisListType, ActivationFunctionType as AF
+from concourse.mybir import AluOpType as O, ActivationFunctionType as AF
 
 H2 = 64
-NV = {"A": 4, "B": 8}
-EQS = {"A": 1, "B": 0}
-LV = {"A": (1, 2), "B": (1, 2)}
-TILE = (1, 1, 2, 3, 3, 3)
-WID = {1: 10, 2: 12, 3: 15}
-RR = {1: list(range(8, -1, -1)), 2: list(range(12, 2, -1)) + [17], 3: list(range(16, 3, -1)) + [18]}
+OPT = {"tiles": 3, "te": {"A1": "s", "A2": "g", "A3": "g", "B1": "v", "B2": "g", "B3": "g"}, "na": {"A": 4, "B": 4}, "fast": "B", "gv": {}, "eqs": "", "w8": "v", "db": "v",
+       "ws": 0.2, "wx": 0.25, "f": 1.1, "tries": 1500, "seed": 0, "chunks": 16}
+PLAN = {}
+TILES = {3: ((0, 1, 2, 3, 3), {1: (8, 1), 2: (12, 2), 3: (16, 3)}),
+         2: ((0, 1, 1, 3, 3), {1: (12, 1), 3: (16, 3)})}
 SCRATCH = {}
 SEMAPHORES = ["sv", "ss", "st_", "sg", "loc", "arst1", "arst2"] + ["arr%d%s%s" % (t, x, h) for t in (1, 2) for x in "LC" for h in "AB"]
-SEMAPHORES += ["d%d" % k for k in range(16)]
-_BF, _F32, _I32 = "bfloat16", "float32", "int32"
-for _n, _c, _d in (("X", 4096 + 128, _BF), ("chs", 128, _BF), ("sps", 128, _BF), ("fls", 128, _BF), ("wts", 1, _BF), ("stI", 128, _I32),
-                   ("st16", 128, "uint16"), ("stin1", 128, "uint16"), ("stin2", 128, "uint16"), ("pI", 1, _I32), ("aI", 1, _I32), ("jneg", 6, _F32),
-                   ("qc", 1, _F32), ("qk", 6, _F32), ("nq", 6, _F32), ("iz", 1, _F32), ("q6", 1, _F32), ("q16", 1, _F32),
-                   ("ones", 128, _BF), ("bm0", 128, _BF), ("bm", 128, _BF), ("nbm", 128, _BF), ("idn", 128, _BF), ("nid", 128, _BF),
-                   ("tri", 128, _BF), ("shm", 512, _BF), ("hsd", 512, _BF), ("hsh", 512, _BF), ("hid", 256, _BF), ("kc", 128, _BF),
-                   ("half", 5, _F32), ("onec", 1, _F32), ("g8", 8, _F32), ("g8w", 8, _F32), ("Wm", 2048, _BF), ("Em", 2048, _BF), ("Es", 2048, _BF),
-                   ("jrow", 18, _F32), ("cqx", 18, _F32), ("dif", 17, _F32), ("dif8", 19, _F32), ("Rm", 19 * 128, _BF), ("il0", 4, _F32),
-                   ("il", 4, _F32), ("m6", 1536, _BF), ("m16", 64, _BF)):
+SEMAPHORES += ["d%d" % k for k in range(40)]
+_BF, _F32, _I32, _U16 = "bfloat16", "float32", "int32", "uint16"
+_COL = ("qc", "q8", "iz", "kb", "qA", "qB", "c0", "c1", "c2", "c3", "c4", "c5", "w", "one")
+_MAT = ("nid", "hid", "hs4", "kc", "ke", "kq", "bA", "bB", "bn", "b256", "n256", "hb", "Wb")
+for _n, _c, _d in (("X", 16384, _BF), ("C0", 128, _BF), ("C1", 128, _BF), ("C2", 128, _BF), ("L0", 128, _BF), ("L1", 128, _BF), ("L2", 128, _BF),
+                   ("wts", 1, _BF), ("st0", 128, _I32), ("st1", 128, _I32), ("st2", 128, _I32), ("pI", 1, _I32), ("aI", 1, _I32),
+                   ("col", 64, _F32), ("jrow", 18, _F32), ("cqx", 18, _F32), ("dif", 17, _F32), ("dif8", 21, _F32), ("il0", 4, _F32), ("il", 4, _F32),
+                   ("Kv", 8, _F32), ("Kt", 16, _F32), ("acnt", 1, _F32), ("junk", 64, _BF), ("b8", 128, _F32),
+                   ("ones", 960, _BF), ("bm0", 128, _BF), ("bm", 128, _BF), ("idn", 128, _BF), ("tri", 128, _BF), ("shm", 512, _BF),
+                   ("hsd", 512, _BF), ("hsh", 512, _BF), ("mat", len(_MAT) * 128, _BF), ("Wz", 144, _BF), ("Ez", 144, _BF), ("Rm", 21 * 128, _BF),
+                   ("mz2", 512, _BF), ("mz3", 768, _BF), ("mz4", 1024, _BF), ("mz5", 1280, _BF), ("mz6", 1536, _BF),
+                   ("m6", 384, _BF), ("k6", 384, _BF), ("Kq", 384, _BF), ("j16", 128, _BF), ("dg0", 128, _BF), ("dg", 128, _BF)):
     SCRATCH[_n] = ("sbuf", [128, _c], _d)
 _PACK = {}
-_SMALL = {_BF: (("w", 64), ("b", 64), ("key", 64), ("Kp", 64), ("okS", 64), ("aL", 64), ("aM", 64), ("acc", 64), ("nok", 64), ("nokL", 64),
-                ("Vsel", 64), ("xo", 64), ("yfs", 64), ("Fs", 64), ("kb", 64), ("kt", 64), ("aT", 64), ("kq", 128)),
-          _F32: (("stf", 64), ("sta", 64), ("tt", 4), ("fd", 64), ("asum", 1), ("K1", 4), ("K2", 4), ("Kv", 4), ("S0", 64), ("yss", 64),
-                 ("base", 64), ("xd", 64), ("xe", 64), ("t1", 64)),
-          _I32: (("n1", 64), ("k8", 64), ("h0", 4), ("h1", 4), ("h2", 4), ("h3", 4), ("fi", 64), ("s0", 64), ("s1", 64), ("t2", 64), ("t4", 64), ("t5", 64))}
+_SMALL = {_BF: (("b", 64), ("Kp", 64), ("f", 64), ("E", 64), ("acc", 64), ("aL", 64), ("e0", 64), ("t0", 64), ("Vsel", 64), ("xo", 64),
+                ("fr", 64), ("yfs", 64), ("w8", 64), ("c0", 64), ("e5", 64), ("keep", 64)),
+          _F32: (("base", 64), ("wr", 128), ("tb", 4), ("S0", 64), ("xd", 64), ("xe", 64), ("yss", 64), ("ay", 64)),
+          _I32: (("ab", 128), ("am", 128), ("k8", 64), ("Q", 64), ("s1", 64), ("n1", 64), ("hw", 64), ("h1", 4), ("k5", 64), ("n5", 64))}
 for _h in "AB":
     for _d, _names in _SMALL.items():
         _at = 0
@@ -34,19 +35,15 @@ for _h in "AB":
             _PACK[_n + _h] = ("pk" + _d[0] + _h, _at, _c)
             _at += -(-_c // 32) * 32
         SCRATCH["pk" + _d[0] + _h] = ("sbuf", [128, _at], _d)
-    for _n, _c, _d in (("z", 6144, _BF), ("VS", 6144, _BF), ("ind", 1024, _BF), ("off", 64, "uint16"), ("mk", 960, _BF), ("co", 960, _BF),
-                       ("AP", 448, _BF), ("ES", 256, _BF), ("EC", 256, _BF), ("EQ", 384, _BF), ("EN", 384, _BF), ("SQ", 320, _BF),
-                       ("voff", 4, "uint16"), ("toff", 4, "uint16")):
+    for _n, _c, _d in (("z", 6144, _BF), ("Y", 12288, _BF), ("VS", 6144, _BF), ("ind", 1024, _BF), ("off", 64, _U16), ("mk", 960, _BF), ("co", 960, _BF),
+                       ("AP", 384, _BF), ("SQ", 384, _BF), ("EQ", 384, _BF), ("EN", 384, _BF), ("LS", 384, _BF), ("ES", 256, _BF), ("EC", 256, _BF),
+                       ("F", 512, _BF), ("voff", 4, _U16), ("toff", 4, _U16), ("da1", 832, _BF), ("db1", 832, _BF), ("da2", 768, _BF),
+                       ("db2", 768, _BF), ("da3", 960, _BF), ("db3", 960, _BF), ("T1", 832, _BF), ("T2", 768, _BF), ("T3", 960, _BF)):
         SCRATCH[_n + _h] = ("sbuf", [128, _c], _d)
-    for _q in (1, 2, 3):
-        for _n in ("L", "da", "db"):
-            SCRATCH["%s%d%s" % (_n, _q, _h)] = ("sbuf", [128, 64 * WID[_q]], _BF)
     for _x in "LC":
         for _t in (0, 1, 2):
             SCRATCH["s%d%s%s" % (_t, _x, _h)] = ("sbuf", [128, 64], _BF)
-        for _t in (1, 2):
-            SCRATCH["in%d%s%s" % (_t, _x, _h)] = ("sbuf", [128, 64], _BF)
-    for _n in ("pU", "p37", "pV", "pM"):
+    for _n in ("pU", "pV", "pD", "pE"):
         SCRATCH[_n + _h] = ("psum", [128, 512], _F32)
 
 
@@ -55,10 +52,12 @@ def rank_program(g, core, T, topo):
     if rank is None:
         return
     N = len(T.cores)
+    TILE, ENDS = TILES[OPT["tiles"]]
+    WID = {q: a - b + 2 for q, (a, b) in ENDS.items()}
+    RR = {q: list(range(a, b, -1)) + [17 + b] for q, (a, b) in ENDS.items()}
     eng = {"v": g.vector, "s": g.scalar, "t": g.tensor, "y": g.sync, "g": g}
     qsem = {"v": "sv", "s": "ss", "t": "st_", "g": "sg"}
-    CV, CS, CT = 0.00083 * 1.2, 0.00083 * 1.2, 0.00083 * 0.85
-    GATH = 0.07 + 1024 * 1.56 * CS
+    CY = 0.00083 * OPT["f"]
     ops = []
     lastw, readers, bank = {}, {}, {}
     ndma, loc = [0], [0]
@@ -67,6 +66,35 @@ def rank_program(g, core, T, topo):
         big, at, c = _PACK[name] if name in _PACK else (name, 0, SCRATCH[name][1][1])
         e = c if b is None else b
         return T[big][:, at + a:at + e:step] if step != 1 else T[big][:, at + a:at + e]
+
+    def col(name):
+        j = _COL.index(name)
+        return T.col[:, j:j + 1]
+
+    def qk(k):
+        return T.col[:, 16 + k:17 + k]
+
+    def half(l):
+        return T.col[:, 24 + l:25 + l]
+
+    def mat(name):
+        j = _MAT.index(name)
+        return T.mat[:, 128 * j:128 * j + 128]
+
+    def rm(r):
+        return T.Rm[:, 128 * r:128 * r + 128]
+
+    def win(Z, m):
+        return Z[:, 15 - m:143 - m]
+
+    NB = {h: 6 if a == 6 else 7 - a for h, a in OPT["na"].items()}
+
+    def slot(h, k):
+        a, b = OPT["na"][h], NB[h]
+        if k < a:
+            return T["z" + h], a, k
+        v = (a - 1) * b
+        return T["Y" + h], a * b, [p for p in range(v % a, a * b, a) if p != v][k - a]
 
     def add(q, cost, fns, r=(), w=(), banks=(), sem=None, extra=(), after=()):
         k = len(ops)
@@ -88,17 +116,17 @@ def rank_program(g, core, T, topo):
             deps.update(st[1])
             st[2].append(k)
         deps.discard(k)
-        ops.append({"q": q, "cost": cost, "fns": fns, "deps": deps, "all": deps | set(after), "sem": sem})
+        ops.append({"q": q, "cost": cost, "fns": fns, "deps": deps, "all": deps | set(after), "sem": sem, "name": w[0] if w else "-"})
         return k
 
     def V(n, fn, r, w, banks=(), **kw):
-        return add("v", max(64, n) * CV, [fn], r, w, banks, **kw)
+        return add("v", 0.005 + max(64, n) * CY, [fn], r, w, banks, **kw)
 
     def S(n, fn, r, w, banks=()):
-        return add("s", 0.03 + max(40, n) * CS, [fn], r, w, banks)
+        return add("s", 0.035 + max(64, n) * CY, [fn], r, w, banks)
 
     def P(cols, fns, r, w, banks=(), **kw):
-        return add("t", 0.02 + cols * CT, fns, r, w, banks, **kw)
+        return add("t", 0.01 + cols * CY, fns, r, w, banks, **kw)
 
     def TS(out, in0, s1, s2, o0, o1=None):
         if o1 is None:
@@ -114,11 +142,8 @@ def rank_program(g, core, T, topo):
     def MS(ap, c):
         return lambda: g.vector.memset(ap, c)
 
-    def SCAN(out, d0, d1, o0, o1):
-        return lambda: g.vector.tensor_tensor_scan(out, d0, d1, 0.0, o0, o1)
-
-    def TURN(out, a):
-        return lambda: g.vector.transpose(out, a)
+    def SCAN(out, d0, d1, o0, o1, first=0.0):
+        return lambda: g.vector.tensor_tensor_scan(out, d0, d1, first, o0, o1)
 
     def ACT(out, in_, f, **kw):
         return lambda: g.scalar.activation(out, in_, f, **kw)
@@ -126,369 +151,402 @@ def rank_program(g, core, T, topo):
     def MM(out, l, r, a, z):
         return lambda: g.tensor.matmul(out, l, r, a, z)
 
-    def dma(q, out, in_, r, w, cost=2.2):
+    def SUM(out, pairs):
+        return [MM(out, l, r, j == 0, j == len(pairs) - 1) for j, (l, r) in enumerate(pairs)]
+
+    def LIN(q, out, in_, a, b, r, w, banks=()):
+        if q == "v":
+            return V(64, TS(out, in_, a, b, O.mult, O.add), r, w, banks)
+        return S(64, ACT(out, in_, AF.Copy, scale=a, bias=b), r, w, banks)
+
+    def gather(q, out, window, offs, n, r, w):
+        fn = (lambda: g.scalar.activation(out, window.indirect(offs), AF.Copy)) if q == "s" else (lambda: g.vector.tensor_copy(out, window.indirect(offs)))
+        return add(q, 0.065 + n * 1.56 * CY, [fn], r, w)
+
+    def dma(q, pairs, r, w, cost=2.2):
         s = "d%d" % ndma[0]
         ndma[0] += 1
-        return add(q, cost, [lambda: eng[q].dma_start(out, in_)], r, w, sem=(s, 16))
+        return add(q, cost, [lambda o_=o_, i_=i_: eng[q].dma_start(o_, i_) for o_, i_ in pairs], r, w, sem=(s, 16 * len(pairs)))
 
-    def aff(out, in_, pat, cmp, base, cm, r, w):
-        return add("g", 0.4, [lambda: g.affine_select(out, in_, pat, cmp, 0.0, base, cm)], r, w)
+    def aff(out, in_, pat, cmp, base, cm, r, w, n=128):
+        return add("g", 0.17 + 2 * n * CY, [lambda: g.affine_select(out, in_, pat, cmp, 0.0, base, cm)], r, w)
 
-    def iota(out, pat, base, cost, w):
-        add("g", cost, [lambda: g.iota(out, pat, base, 0, allow_small_or_imprecise_dtypes=True)], (), w)
+    def iota(out, pat, base, n, w):
+        add("g", 0.13 + 2 * n * CY, [lambda: g.iota(out, pat, base, 0, allow_small_or_imprecise_dtypes=True)], (), w)
 
     NE = min(len(topo.engines(core, c)) for c in T.cores if c != core)
 
-    def send(name_in, name_out, sem, hop, r):
+    def send(out, in_, sem, hop, r, w):
         dst = T.cores[(rank + hop) % N]
         rid, pid = topo.addr(dst)[:2]
         lanes = sum(1 << e for e in topo.engines(core, dst)[:NE])
         loc[0] += NE
-        k = add("g", 0.3, [lambda: g.remote_dma(T[name_out][:], T[name_in][:], T.sem[sem], T.sem.loc, pid, rid, lanes)], r, (), sem=("loc", None))
-        return add("r", 3.5, [], (), (name_out,), sem=(sem, NE), extra=(k,))
+        k = add("g", 0.8, [lambda: g.remote_dma(out, in_, T.sem[sem], T.sem.loc, pid, rid, lanes)], r, (), sem=("loc", None))
+        return add("r", 2.0, [], (), w, sem=(sem, NE), extra=(k,))
 
-    dma("s", T.stI[:], T.st[:], (), ("stI",))
-    dma("y", T.sps[:], T.sp[:], (), ("sps",))
-    dma("y", T.X[:, 0:4096], T.x[:], (), ("X",), 6.0)
-    dma("s", T.wts[:], T.wt[:], (), ("wts",))
-    dma("s", T.chs[:], T.ch[:], (), ("chs",))
-    dma("s", T.fls[:], T.fl[:], (), ("fls",))
-    V(64, MS(T.X[:, 4096:4224], 0.0), (), ("Xd",))
-    V(128, CP(T.st16[:], T.stI[:]), ("stI",), ("st16",))
-    send("st16", "stin1", "arst1", 1, ("st16",))
-    send("st16", "stin2", "arst2", 2, ("st16",))
-    add("g", 0.2, [lambda: g.iota(T.pI[:], [[0, 1]], 0, 1)], (), ("pI",))
-    iota(T.jrow[:], [[1, 18]], -1, 0.2, ("jrow",))
-    iota(T.jneg[:], [[-1, 6]], 0, 0.2, ("jneg",))
-    iota(T.il0[:], [[16, 4]], 0, 0.2, ("il0",))
-    V(64, MS(T.ones[:], 1.0), (), ("ones",))
+    def spread(h):
+        dma("y", [(T["F" + h][:, 64 * j:64 * j + 64], T["F" + h][:, 0:64]) for j in range(1, 8)], ("F" + h,), ("Fr" + h,), 2.6)
+
+    dma("y", [(T.X[:, 0:4096], T.x[:])], (), ("X",), 6.0)
+    dma("s", [(T.st0[:], T.st[:])], (), ("st0",))
+    dma("s", [(T.L0[:], T.sp[:])], (), ("L0A", "L0B"))
+    dma("s", [(T.wts[:], T.wt[:])], (), ("wts",))
+    dma("s", [(T.C0[:], T.ch[:])], (), ("C0A", "C0B"))
+    for hi, h in enumerate("AB"):
+        dma("y", [(T["F" + h][:, 0:64], T.fl[:, H2 * hi:H2 * hi + H2])], (), ("F" + h,))
+        spread(h)
+    send(T.st1[:], T.st0[:], "arst1", 1, ("st0",), ("st1",))
+    send(T.st2[:], T.st0[:], "arst2", 2, ("st0",), ("st2",))
+    V(2048, CP(T.X[:, 4096:8192], T.X[:, 0:4096]), ("X",), ("X2",))
+    ones = T.ones[:, 0:128]
+    LN3 = math.log(3.0)
+    add("g", 0.14, [lambda: g.iota(T.pI[:], [[0, 1]], 0, 1)], (), ("pI",))
+    iota(T.jrow[:], [[1, 18]], -1, 18, ("jrow",))
+    iota(T.il0[:], [[16, 4]], 0, 4, ("il0",))
+    V(64, MS(ones, 1.0), (), ("ones",))
+    V(416, MS(T.ones[:, 128:960], 1.0), (), ("onesw",))
     V(1, TS(T.aI[:], T.pI[:], 15, None, O.bitwise_and), ("pI",), ("aI",))
-    V(1, CP(T.qc[:], T.aI[:]), ("aI",), ("qc",))
-    V(6, TS(T.qk[:], T.jneg[:], T.qc[:], None, O.add), ("jneg", "qc"), tuple("qk%d" % k for k in range(6)))
-    V(5, TS(T.half[:], T.jneg[:, 0:5], 0.5, None, O.add), ("jneg",), tuple("half%d" % l for l in range(5)))
-    V(1, MS(T.onec[:], 1.0), (), ("onec",))
-    V(1, TS(T.iz[:], T.qc[:], 0.0, None, O.is_equal), ("qc",), ("iz",))
-    V(1, TS(T.q6[:], T.qc[:], 6.0, None, O.mult), ("qc",), ("q6",))
-    V(1, TS(T.q16[:], T.qc[:], -1.0, 16.0, O.mult, O.add), ("qc",), ("q16",))
-    V(6, TS(T.nq[:], T.qk[:], -1.0, None, O.mult), tuple("qk%d" % k for k in range(6)), ("nq",))
-    aff(T.bm0[:], T.ones[:], [[-16, 8], [0, 16]], O.is_ge, 0, 1, ("ones",), ("bm0",))
+    V(1, CP(col("qc"), T.aI[:]), ("aI",), ("qc",))
+    for name, a, b in (("q8", 8.0, 0.0), ("kb", -LN3, 2 * LN3), ("qA", float(NB["A"]), 0.0), ("qB", float(NB["B"]), 0.0),
+                       ("c0", -65536.0, 983039.0 + NB["A"]), ("c1", -65536.0, 983039.0 + NB["B"]), ("c2", -65536.0, 983040.0 + 8192),
+                       ("c3", -65536.0, 983040.0 + 10240), ("c4", 0.0, 0.0), ("c5", 0.0, 2048.0), ("one", 1.0, 64.0)):
+        V(1, TS(col(name), col("qc"), a, b, O.mult, O.add), ("qc",), (name,))
+    V(6, TS(T.col[:, 16:22], T.jrow[:, 1:7], -1.0, col("one"), O.mult, O.add), ("jrow", "one"), ("qk",))
+    V(5, TS(T.col[:, 24:29], T.jrow[:, 0:5], -1.0, -0.5, O.mult, O.add), ("jrow",), ("half",))
+    V(1, MS(T.col[:, 30:31], 1.0), (), ("onec",))
+    V(1, TS(col("iz"), col("qc"), 0.0, None, O.is_equal), ("qc",), ("iz",))
+    V(1, CP(col("w"), T.wts[:]), ("wts",), ("w",))
+    aff(T.bm0[:], ones, [[-16, 8], [0, 16]], O.is_ge, 0, 1, ("ones",), ("bm0",))
     aff(T.bm[:], T.bm0[:], [[16, 8], [0, 16]], O.is_ge, 15, -1, ("bm0",), ("bm",))
-    aff(T.idn[:], T.ones[:], [[-1, 128]], O.is_equal, 0, 1, ("ones",), ("idn",))
-    V(4, TS(T.il[:], T.il0[:], T.qc[:], None, O.add), ("il0", "qc"), ("il",))
-    V(18, TS(T.cqx[:], T.jrow[:], T.qc[:], None, O.is_equal), ("jrow", "qc"), ("cqx",))
+    aff(T.idn[:], ones, [[-1, 128]], O.is_equal, 0, 1, ("ones",), ("idn",))
+    V(4, TS(T.il[:], T.il0[:], col("qc"), None, O.add), ("il0", "qc"), ("il",))
+    for out, a, c, w in ((T.Kv[:, 0:4], 16.0 * NB["A"], "c0", "KvA"), (T.Kv[:, 4:8], 16.0 * NB["B"], "c1", "KvB"), (T.Kt[:, 0:4], 32.0, "c2", "KtA"), (T.Kt[:, 4:8], 32.0, "c3", "KtB"),
+                         (T.Kt[:, 8:12], 32.0, "c4", "KlA"), (T.Kt[:, 12:16], 32.0, "c5", "KlB")):
+        V(4, TS(out, T.il[:], a, col(c), O.mult, O.add), ("il", c), (w,))
+    V(18, TS(T.cqx[:], T.jrow[:], col("qc"), None, O.is_equal), ("jrow", "qc"), ("cqx",))
     V(17, TT(T.dif[:], T.cqx[:, 1:18], T.cqx[:, 0:17], O.subtract), ("cqx",), ("dif",))
     V(17, TS(T.dif8[:, 0:17], T.dif[:], 8.0, None, O.mult), ("dif",), ("dif8a",))
-    V(2, TS(T.dif8[:, 17:19], T.cqx[:, 3:5], 8.0, None, O.mult), ("cqx",), ("dif8b",))
-    for r in list(range(8, -1, -1)) + [17, 18] + list(range(16, 8, -1)):
+    V(4, TS(T.dif8[:, 17:21], T.cqx[:, 1:5], 8.0, None, O.mult), ("cqx",), ("dif8b",))
+    jobs = [r for q in sorted(RR) for r in RR[q]]
+    jobs = sorted(set(jobs), key=jobs.index)
+    for j, r in enumerate([17] + jobs):
         tok = ("bm", "dif8b" if r > 16 else "dif8a")
-        if r < 9:
-            V(64, TS(T.Rm[:, r * 128:(r + 1) * 128], T.bm[:], T.dif8[:, r:r + 1], None, O.mult), tok, ("Rm%d" % r,))
+        if j % 3:
+            V(64, TS(rm(r), T.bm[:], T.dif8[:, r:r + 1], None, O.mult), tok, ("Rm%d" % r,))
         else:
-            S(128, ACT(T.Rm[:, r * 128:(r + 1) * 128], T.bm[:], AF.Copy, scale=T.dif8[:, r:r + 1]), tok, ("Rm%d" % r,))
-    V(8, CP(T.g8[:], T.bm[:, 0::16]), ("bm",), ("g8",))
-    V(8, TS(T.g8w[:], T.g8[:], T.wts[:], None, O.mult), ("g8", "wts"), ("g8w",))
-    V(1024, MS(T.Wm[:], 0.0), (), ("Wz",))
-    V(1024, MS(T.Em[:], 0.0), (), ("Ez",))
-    for gg in range(8):
-        sl = slice(16 * gg, 16 * gg + 15 * 129 + 1, 129)
-        S(16, ACT(T.Wm[:, sl], T.ones[:, 0:16], AF.Copy, scale=T.g8w[:, gg:gg + 1]), ("g8w", "Wz", "ones"), ("Wm%d" % gg,))
-    for gg in range(8):
-        sl = slice(16 * gg, 16 * gg + 15 * 129 + 1, 129)
-        S(16, ACT(T.Em[:, sl], T.ones[:, 0:16], AF.Copy, scale=T.g8[:, gg:gg + 1]), ("g8", "Ez", "ones"), ("Em%d" % gg,))
-    EM = tuple("Em%d" % m for m in range(8))
-    WM = tuple("Wm%d" % m for m in range(8))
-    V(1024, TS(T.Es[:], T.Em[:], 160.0, None, O.mult), EM, ("Es",))
-    V(64, MS(T.kc[0:64, :], -512.0), (), ("kc0",))
-    V(64, MS(T.kc[64:128, :], 0.0625), (), ("kc1",))
-    V(64, TS(T.nid[:], T.idn[:], -1.0, None, O.mult), ("idn",), ("nid",))
-    V(64, TS(T.nbm[:], T.bm[:], -1.0, None, O.mult), ("bm",), ("nbm",))
+            S(128, ACT(rm(r), T.bm[:], AF.Copy, scale=T.dif8[:, r:r + 1]), tok, ("Rm%d" % r,))
+    V(72, MS(T.Wz[:], 0.0), (), ("Wz",))
+    V(8, TS(T.Wz[:, 15:143:16], T.bm[:, 0::16], col("w"), None, O.mult), ("bm", "w"), ("Wz",))
+    V(72, MS(T.Ez[:], 0.0), (), ("Ez",))
+    V(8, TS(T.Ez[:, 15:143:16], T.bm[:, 0::16], 8.0, None, O.mult), ("bm",), ("Ez",))
+    kc = _MAT.index("kc") * 128
+    V(64, MS(T.mat[0:64, kc:kc + 128], -512.0), (), ("kc0",))
+    V(64, MS(T.mat[64:128, kc:kc + 128], 0.0625), (), ("kc1",))
+    V(64, MS(mat("ke"), 1.0 / 65536), (), ("ke",))
+    V(64, MS(mat("kq"), -1.0 / 512), (), ("kq",))
     aff(T.tri[:], T.bm[:], [[1, 128]], O.is_ge, 0, -1, ("bm",), ("tri",))
     for l in range(1, 5):
         aff(T.shm[:, (l - 1) * 128:l * 128], T.bm[:], [[-1, 128]], O.is_equal, -l, 1, ("bm",), ("shm%d" % l,))
+    for name, src, tok, a in (("nid", T.idn[:], "idn", -1.0), ("hid", T.idn[:], "idn", 0.5), ("hs4", T.shm[:, 384:512], "shm4", 0.5),
+                              ("bA", T.bm[:], "bm", "qA"), ("bB", T.bm[:], "bm", "qB"), ("bn", T.bm[:], "bm", -8192.0), ("b256", T.bm[:], "bm", 256.0),
+                              ("n256", T.bm[:], "bm", -256.0), ("hb", T.bm[:], "bm", 0.5), ("Wb", T.bm[:], "bm", "w")):
+        V(64, TS(mat(name), src, col(a) if a in _COL else a, None, O.mult), (tok, a) if a in _COL else (tok,), (name + "m" if name in ("bA", "bB") else name,))
+    V(128, TS(T.b8[:], T.bm[:], 0.125, None, O.mult), ("bm",), ("b8",))
     for l in range(1, 5):
         V(256, TT(T.hsd[:, (l - 1) * 128:l * 128], T.shm[:, (l - 1) * 128:l * 128],
                   T.idn[:] if l == 1 else T.shm[:, (l - 2) * 128:(l - 1) * 128], O.subtract),
           ("shm%d" % l, "idn" if l == 1 else "shm%d" % (l - 1)), ("hsd%d" % l,))
     V(256, TS(T.hsh[:], T.hsd[:], 0.5, None, O.mult), ("hsd1", "hsd2", "hsd3", "hsd4"), ("hsh",))
-    V(64, TS(T.hid[:, 0:128], T.idn[:], 0.5, None, O.mult), ("idn",), ("hid0",))
-    V(64, TS(T.hid[:, 128:256], T.shm[:, 384:512], 0.5, None, O.mult), ("shm4",), ("hid1",))
-    V(768, MS(T.m6[:], 1.0), (), ("m6",))
-    V(256, MS(T.m6[:, 0::6], 0.0), (), ("m6",))
-    V(64, MS(T.m16[:], 1.0), (), ("m16",))
-    V(8, MS(T.m16[:, 0::16], 0.0), (), ("m16",))
+    for n in sorted(set(OPT["na"].values()) | set(NB.values())):
+        iota(T["mz%d" % n][:], [[0, 256], [256, n]], 0, 256 * n, ("mz%d" % n,))
+    iota(T.m6[:], [[0, 64], [4, 6]], 1, 384, ("m6",))
+    iota(T.k6[:], [[0, 64], [1, 6]], -64, 384, ("k6",))
+    iota(T.j16[:], [[0, 8], [1, 16]], 0, 128, ("j16",))
+    V(192, TS(T.Kq[:], T.k6[:], col("qc"), None, O.subtract), ("k6", "qc"), ("Kq",))
+    V(64, TS(T.Kq[:, 0::6], T.ones[:, 0:64], col("qc"), -1.0, O.mult, O.mult), ("ones", "qc"), ("Kq",))
+    V(64, TS(T.dg0[:], T.j16[:], col("qc"), 65.0 * 65536, O.is_equal, O.mult), ("j16", "qc"), ("dg0",))
+    V(64, TS(T.dg[:], T.dg0[:], -65536.0, None, O.add), ("dg0",), ("dg",))
     for hi, h in enumerate("AB"):
-        for q in (1, 2, 3):
+        for q in WID:
             n = WID[q]
-            a, b, l = ("%s%d%s" % (x, q, h) for x in ("da", "db", "L"))
-            for x in (a, b):
-                if q == 1:
-                    V(n * 32, MS(T[x][:], 1.0), (), (x,))
-                else:
-                    iota(T[x][:], [[0, 64 * n]], 1, 0.13 + n * 128 * CS, (x,))
-            S(64, ACT(T[a][:, 0::n], T.ones[:, 0:64], AF.Copy, scale=64.0), ("ones",), (a,))
-            S(64, ACT(T[b][:, 1::n], T.ones[:, 0:64], AF.Copy, scale=0.0), ("ones",), (b,))
-            S(64, ACT(T[l][:, 0::n], T.ones[:, 0:64], AF.Copy, scale=0.0), ("ones",), (l + "z",))
-        V(4, TS(B("K1" + h), T.il[:], 31.0, float(31 * H2 * hi - 4096), O.mult, O.add), ("il",), ("K1" + h,))
-        V(4, TS(B("K2" + h), T.il[:], float(4096 + H2 * hi), None, O.add), ("il",), ("K2" + h,))
-        V(4, TS(B("Kv" + h), T.il[:], 96.0, 5.0, O.mult, O.add), ("il",), ("Kv" + h,))
-        V(64, MS(T["AP" + h][:, 0:64], 0.0), (), ("AP0" + h,))
-        V(64, TS(T["EQ" + h][:, 0:64], T.ones[:, 0:64], T.iz[:], None, O.mult), ("ones", "iz"), ("EQ0" + h,))
-        V(1, MS(B("asum" + h), 0.0), (), ("asum" + h,))
-        V(64, CP(T["pV" + h][:, 448:512], T.fls[:, H2 * hi:H2 * hi + H2]), ("fls",), ("F" + h,), ("pV" + h,))
-        V(64, CP(B("Fs" + h), T.fls[:, H2 * hi:H2 * hi + H2]), ("fls",), ("Fs" + h,))
-        V(64, MS(B("kq" + h), -1.25), (), ("kq" + h,))
-        for m in range(NV[h]):
-            V(64, MS(B("kq" + h, m, 128, 16), -10.625), (), ("kq" + h,))
-
-    def rec(t, h):
-        o = H2 * "AB".index(h)
-        if t == 0:
-            return T.chs[:, o:o + H2], T.sps[:, o:o + H2], "chs", "sps"
-        c, l = "in%dC%s" % (t, h), "in%dL%s" % (t, h)
-        return T[c][:], T[l][:], c, l
-
-    def vm(h, m):
-        return T["VS" + h][:, 6 * m + 5::96]
+            a, b = "da%d%s" % (q, h), "db%d%s" % (q, h)
+            if q == 1:
+                for x in (a, b):
+                    V(n * 32, MS(T[x][:, 0:64 * n], 1.0), (), (x,))
+            else:
+                dma("y", [(T[x][:, 0:64 * n], T.ones[:, 0:64 * n]) for x in (a, b)], ("ones", "onesw", "X"), (a, b), 3.0)
+            V(64, MS(T[b][:, 1:64 * n:n], 0.0), (), (b,))
+            V(64, MS(T["T%d%s" % (q, h)][:, 0:64 * n:n], 0.0), (), ("T%dz%s" % (q, h),))
+        V(64, MS(T["AP" + h][:, 0::6], 0.0), (), ("AP0" + h,))
 
     def entry(k, h):
         q = TILE[k]
         n = WID[q]
-        L = "L%d%s" % (q, h)
-        V(n * 32, SCAN(T["mk" + h][:, 0:64 * n], T["da%d%s" % (q, h)][:], T["db%d%s" % (q, h)][:], O.add, O.min),
+        V(n * 32, SCAN(T["mk" + h][:, 0:64 * n], T["da%d%s" % (q, h)][:, 0:64 * n], T["db%d%s" % (q, h)][:, 0:64 * n], O.add, O.min, 1.0),
           ("da%d%s" % (q, h), "db%d%s" % (q, h)), ("mk" + h,))
-        V(n * 32, SCAN(T["co" + h][:, 0:64 * n], T["mk" + h][:, 0:64 * n], T[L][:], O.mult, O.add),
-          ("mk" + h, L + "z") + tuple("%s_%d" % (L, r) for r in RR[q]), ("co" + h,))
-        if k < 5:
-            V(64, TS(B("w" + h), T["co" + h][:, n - 1:64 * n:n], 0.25, 2.0, O.mult, O.add), ("co" + h,), ("w" + h,))
+        V(n * 32, SCAN(T["co" + h][:, 0:64 * n], T["mk" + h][:, 0:64 * n], T["T%d%s" % (q, h)][:, 0:64 * n], O.mult, O.add),
+          ("mk" + h, "T%dz%s" % (q, h)) + tuple("T%d_%d%s" % (q, r, h) for r in RR[q]), ("co" + h,))
+        LIN(OPT["w8"], B("w8" + h), T["co" + h][:, n - 1:64 * n:n], 1.0 / 32, 0.25, ("co" + h,), ("w8" + h,))
 
     for t in range(3):
         last = t == 2
+        Cw, Lw, St = T["C%d" % t], T["L%d" % t], T["st%d" % t]
         for hi, h in enumerate("AB"):
-            C, L, ct, lt = rec(t, h)
-            pV, pM, pU, p37 = T["pV" + h], T["pM" + h], T["pU" + h], T["p37" + h]
             o = H2 * hi
-            src, stt = ((T.stI, "stI"), (T.stin1, "stin1"), (T.stin2, "stin2"))[t]
-            V(64, CP(B("stf" + h), src[:, o:o + H2]), (stt,), ("stf" + h,))
-            V(64, TS(B("sta" + h), B("stf" + h), B("asumA"), B("asumB"), O.add, O.add), ("stf" + h, "asumA", "asumB"), ("sta" + h,))
-            V(64, TS(B("base" + h), L, 613.0, None, O.mult), (lt,), ("base" + h,))
-            V(128, TT(B("s0" + h), B("base" + h), B("sta" + h), O.add), ("base" + h, "sta" + h), ("s0" + h,))
-            V(64, TS(B("s1" + h), B("s0" + h), 4095, None, O.bitwise_and), ("s0" + h,), ("s1" + h,))
-            V(64, CP(T["off" + h][:], B("s1" + h)), ("s1" + h,), ("off" + h,))
-            V(64, CP(pV[:, 384:448], L), (lt,), ("L" + h,), ("pV" + h,))
-            S(64, ACT(B("Kp" + h), L, AF.Identity, scale=16.0, bias=T.q16[:]), (lt, "q16"), ("Kp" + h,))
-            S(64, ACT(T["da1" + h][:, 1::10], L, AF.Copy, scale=T.iz[:]), (lt, "iz"), ("da1" + h,))
-            S(64, ACT(T["db1" + h][:, 0::10], T.ones[:, 0:64], AF.Copy, scale=-8.0), ("ones",), ("db1" + h,))
-            P(512, [MM(pM[:, 64 * j:64 * j + 64], T.Rm[:, (8 - j) * 128:(9 - j) * 128], C, True, True) for j in range(8)],
-              (ct,) + tuple("Rm%d" % (8 - j) for j in range(8)), ("dM" + h,), ("pM" + h,))
-            P(192, [MM(pU[:, 64 * j:64 * j + 64], T.Rm[:, r * 128:(r + 1) * 128], C, True, True) for j, r in enumerate((0, 17, 18))],
-              (ct, "Rm0", "Rm17", "Rm18"), ("dU" + h,), ("pU" + h,))
-            P(512, [MM(p37[:, 64 * j:64 * j + 64], T.Rm[:, (16 - j) * 128:(17 - j) * 128], C, True, True) for j in range(8)],
-              (ct,) + tuple("Rm%d" % (16 - j) for j in range(8)), ("d37" + h,), ("p37" + h,))
-            at = {r: (pM, 8 - r, "dM" + h, "pM" + h) for r in range(1, 9)}
-            at.update({r: (p37, 16 - r, "d37" + h, "p37" + h) for r in range(9, 17)})
-            at.update({r: (pU, j, "dU" + h, "pU" + h) for j, r in enumerate((0, 17, 18))})
-            for q in (1, 2, 3):
-                n = WID[q]
-                todo = list(enumerate(RR[q]))
-                for j, r in (todo if q == 1 else todo[::-1]):
-                    ps, jj, tk, bk = at[r]
-                    out, in_ = T["L%d%s" % (q, h)][:, 1 + j::n], ps[:, 64 * jj:64 * jj + 64]
-                    low = r in (0, 17, 18)
-                    if q in LV[h]:
-                        V(64, TS(out, in_, -4.0, None, O.add) if low else CP(out, in_), (tk,), ("L%d%s_%d" % (q, h, r),), (bk,))
-                    else:
-                        S(64, ACT(out, in_, AF.Copy, bias=-4.0) if low else ACT(out, in_, AF.Copy), (tk,), ("L%d%s_%d" % (q, h, r),), (bk,))
-            entry(0, h)
+            C, L, ct, lt = Cw[:, o:o + H2], Lw[:, o:o + H2], "C%d%s" % (t, h), "L%d%s" % (t, h)
+            bV = "pV" + h
+            pV = T[bV]
+            if t and h in OPT["fast"]:
+                V(64, TS(B("Q" + h), St[:, o:o + H2], T.acnt[:], None, O.add), ("st%d" % t, "acnt"), ("Q" + h,))
+                V(64, TS(B("s1" + h), B("Q" + h), 4095, None, O.bitwise_and), ("Q" + h,), ("s1" + h,))
+                V(64, TS(B("base" + h), L, 613.0, None, O.mult), (lt,), ("base" + h,))
+                V(128, TT(T["off" + h][:], B("base" + h), B("s1" + h), O.add), ("base" + h, "s1" + h), ("off" + h,))
+            else:
+                V(64, TS(B("base" + h), L, 613.0, None, O.mult), (lt,), ("base" + h,))
+                V(128, TT(pV[:, 384:448], B("base" + h), St[:, o:o + H2], O.add), ("base" + h, "st%d" % t), ("bs" + h,), (bV,))
+                V(64, TS(B("Q" + h), pV[:, 384:448], T.acnt[:] if t else 0.0, None, O.add), ("bs" + h, "acnt"), ("Q" + h,), (bV,))
+                V(64, TS(B("s1" + h), B("Q" + h), 4095, None, O.bitwise_and), ("Q" + h,), ("s1" + h,))
+                V(64, CP(T["off" + h][:], B("s1" + h)), ("s1" + h,), ("off" + h,))
+            P(64, SUM(pV[:, 0:64], [(rm(17), L)]), (lt, "Rm17"), ("Lb" + h,), (bV,))
+            V(64, TS(B("e0" + h), pV[:, 0:64], col("q8"), col("iz"), O.is_equal, O.subtract), ("Lb" + h, "q8", "iz"), ("e0" + h,), (bV,))
+            V(64, CP(pV[:, 448:512], L), (lt,), ("L" + h,), (bV,))
+            V(128, TT(B("t0" + h), B("e0" + h), C, O.mult), ("e0" + h, ct), ("t0" + h,))
+            P(128, SUM(pV[:, 64:128], [(rm(17), C), (win(T.Ez, 0), B("t0" + h))]), (ct, "t0" + h, "Rm17", "Ez"), ("c80" + h,), (bV,))
+            LIN("v", B("w8" + h), pV[:, 64:128], 1.0 / 32, 0.125, ("c80" + h,), ("w8" + h,), (bV,))
+            LIN("v", B("c0" + h), pV[:, 64:128], 1.0, -4.0, ("c80" + h,), ("c0" + h,), (bV,))
+            S(64, ACT(B("Kp" + h), L, AF.Exp, scale=16 * LN3, bias=col("kb")), (lt, "kb"), ("Kp" + h,))
+            for j0 in range(0, len(jobs), 8):
+                bk = ("pD" + h, "pE" + h)[j0 // 8 % 2]
+                rs = jobs[j0:j0 + 8]
+                P(64 * len(rs), [MM(T[bk][:, 64 * j:64 * j + 64], rm(r), C, True, True) for j, r in enumerate(rs)],
+                  (ct,) + tuple("Rm%d" % r for r in rs), ("dM" + bk,), (bk,))
+                for q in sorted(RR):
+                    for j, r in enumerate(rs):
+                        if r in RR[q]:
+                            n = WID[q]
+                            out, e = T["T%d%s" % (q, h)][:, 1 + RR[q].index(r):64 * n:n], OPT["te"][h + str(q)]
+                            src = [p_ for p_ in sorted(RR) if p_ < q and r in RR[p_]]
+                            if e == "g" and src:
+                                aff(out, T["T%d%s" % (src[0], h)][:, 1 + RR[src[0]].index(r):64 * WID[src[0]]:WID[src[0]]], [[0, 64]], O.is_equal, 0, 0,
+                                    ("T%d_%d%s" % (src[0], r, h),), ("T%d_%d%s" % (q, r, h),), 64)
+                            else:
+                                LIN("v" if e == "v" else "s", out, T[bk][:, 64 * j:64 * j + 64], 1.0, -4.0 if r > 16 else 0.0, ("dM" + bk,),
+                                    ("T%d_%d%s" % (q, r, h),), (bk,))
+        if last:
+            for hi, h in enumerate("AB"):
+                pE, prev = T["pE" + h], ()
+                for c in range(4):
+                    prev = (P(512, [MM(pE[:, 0:64], T.idn[:], T.X[:, 2048 * hi + j:2048 * hi + 2048:32], j == 0, j == 31) for j in range(8 * c, 8 * c + 8)],
+                              ("X", "idn"), ("sums%d%s" % (c, h),), ("pE" + h,), after=prev),)
+                S(64, ACT(B("S0" + h), pE[:, 0:64], AF.Copy), tuple("sums%d%s" % (c, h) for c in range(4)), ("S0" + h,), ("pE" + h,))
         for k in range(6):
-            for h in "AB":
-                pV, pU = T["pV" + h], T["pU" + h]
-                n = WID[TILE[k]]
-                c8 = T["co" + h][:, n - 1:64 * n:n]
-                zk, z = "z%d%s" % (k, h), T["z" + h]
-                add("s", GATH, [lambda o_=z[:, k::6], f_=T["off" + h]: g.scalar.activation(o_, T.X[:, 0:4096].indirect(f_[:, 0:64]), AF.Copy)],
-                    ("X", "off" + h), (zk,))
-                P(17 * 64, [MM(pU[:, 0:64], T.kc[:], T.ones[:, 0:64], True, False)]
-                  + [MM(pU[:, 0:64], T.Wm[:, 128 * m:128 * m + 128], z[:, 6 * m + k::96], False, m == 15) for m in range(16)],
-                  (zk, "kc0", "kc1", "ones") + WM, ("u" + h,), ("pU" + h,))
-                y4 = pU[:, 0:64]
-                if k < 5:
-                    V(64, TT(B("t1" + h), y4, B("w" + h), O.mult), ("u" + h, "w" + h), ("t1" + h,), ("pU" + h,))
-                    V(64, TS(pU[:, 64:128], y4, 37.0, -148.0, O.mult, O.add), ("u" + h,), ("t3" + h,), ("pU" + h,))
-                    V(64, TS(B("t2" + h), B("t1" + h), 0.125, -0.9375, O.mult, O.add), ("t1" + h,), ("t2" + h,))
-                    V(64, TT(B("t4" + h), B("t2" + h), pU[:, 64:128], O.add), ("t2" + h, "t3" + h), ("t4" + h,), ("pU" + h,))
-                    V(64, TS(B("t5" + h), B("t4" + h), 4095, None, O.bitwise_and), ("t4" + h,), ("t5" + h,))
-                    V(64, CP(T["off" + h][:], B("t5" + h)), ("t5" + h,), ("off" + h,))
-                V(64, TT(B("k8" + h), y4, c8, O.add), ("u" + h, "co" + h), ("k8" + h,), ("pU" + h,))
+            for hi, h in enumerate("AB"):
+                bU, bV = "pU" + h, "pV" + h
+                pV = T[bV]
+                z, zr, zs = slot(h, k)
+                wide = k > 0 or (t and h in OPT["fast"])
+                nv = OPT["gv"].get((k, h), 0)
+                zk = ()
+                for q, a, b in (("s", 0, 64 - nv), ("v", 64 - nv, 64)):
+                    if a < b:
+                        zk += ("z%d%s%s" % (k, q, h),)
+                        gather(q, z[:, 16 * zr * a + zs:16 * zr * b:zr], T.X[:, 0:8192 if wide else 4096], T["off" + h][:, a:b], 16 * (b - a),
+                               ("X", "off" + h) + (("X2",) if wide else ()), zk[-1:])
+                y, by = (T[bU][:, 0:64], bU) if k < 5 else (pV[:, 320:384], bV)
+                k0 = P(128, [MM(y, mat("kc"), T.ones[:, 0:64], True, False), MM(y, mat("ke"), T.ones[:, 0:64], False, False)],
+                       ("kc0", "kc1", "ke", "ones"), ("u0" + h,), (by,))
+                P(1024, [MM(y, win(T.Wz, m), z[:, zr * m + zs:1024 * zr:16 * zr], False, m == 15) for m in range(16)], zk + ("Wz",), ("u" + h,), (by,), after=(k0,))
+                ut = ("u0" + h, "u" + h)
+                na, nb = OPT["na"][h], NB[h]
+                if k == na - 1 and k < 5:
+                    zt = tuple(x for x in lastw if x[0] == "z" and x[-1] == h and int(x[1]) < na)
+                    c = 1024 // OPT["chunks"] * na
+                    for j in range(OPT["chunks"]):
+                        V(c // 2, SCAN(T["Y" + h][:, c * nb * j:c * nb * (j + 1):nb], T["mz%d" % na][:, 0:c], T["z" + h][:, c * j:c * (j + 1)],
+                                       O.min, O.max), zt + ("mz%d" % na,), ("Y%d%s" % (j, h),))
+                if k == 5:
+                    continue
+                V(64, TT(B("ab" + h, 0, 64), y, B("w8" + h), O.mult), ut + ("w8" + h,), ("a0" + h,), (bU,))
+                V(64, TS(B("ab" + h, 64, 128), y, 37.0, -149.0 - 37.0 / 512, O.mult, O.add), ut, ("b0" + h,), (bU,))
+                V(128, TS(B("am" + h), B("ab" + h), 4095, None, O.bitwise_and), ("a0" + h, "b0" + h), ("am" + h,))
+                V(128, TT(T["off" + h][:], B("am" + h, 0, 64), B("am" + h, 64, 128), O.add), ("am" + h,), ("off" + h,))
+                n = WID.get(TILE[k], 1)
+                V(64, TT(B("k8" + h), y, T["co" + h][:, n - 1:64 * n:n] if k else B("c0" + h), O.add), ut + ("co" + h if k else "c0" + h,), ("k8" + h,), (bU,))
                 V(64, TS(B("n1" + h), B("k8" + h), 3, 3, O.arith_shift_right, O.bitwise_and), ("k8" + h,), ("n1" + h,))
                 Pk, pt = pV[:, 64 * k:64 * k + 64], "P%d%s" % (k + 1, h)
                 if k == 0:
-                    V(64, CP(Pk, B("n1" + h)), ("n1" + h,), (pt,), ("pV" + h,))
+                    V(64, TS(Pk, B("n1" + h), 64.0, None, O.add), ("n1" + h,), (pt,), (bV,))
                 else:
-                    V(64, TT(Pk, B("n1" + h), pV[:, 64 * k - 64:64 * k], O.add), ("n1" + h, "P%d%s" % (k, h)), (pt,), ("pV" + h,))
-                if k < 5:
+                    V(64, TT(Pk, B("n1" + h), pV[:, 64 * k - 64:64 * k], O.add), ("n1" + h, "P%d%s" % (k, h)), (pt,), (bV,))
+                if k < 4:
                     q = TILE[k + 1]
                     n2, da, db = WID[q], "da%d%s" % (q, h), "db%d%s" % (q, h)
-                    V(64, TS(T[db][:, 0::n2], Pk, float(k + 1 - RR[q][0]), None, O.add), (pt,), (db,), ("pV" + h,))
-                    V(64, TS(B("b" + h), Pk, T.qk[:, k + 1:k + 2], None, O.is_ge), (pt, "qk%d" % (k + 1)), ("b" + h,), ("pV" + h,))
-                    V(64, TT(T[da][:, 1::n2], B("b" + h), pV[:, 384:448], O.mult), ("b" + h, "L" + h), (da,), ("pV" + h,))
+                    V(64, TS(B("b" + h), Pk, qk(k + 1), None, O.is_ge), (pt, "qk"), ("b" + h,), (bV,))
+                    V(64, TT(T[da][:, 1:64 * n2:n2], B("b" + h), pV[:, 448:512], O.mult), ("b" + h, "L" + h), (da,), (bV,))
+                    LIN(OPT["db"], T[db][:, 0:64 * n2:n2], Pk, 1.0, float(k + 1 - 64 - RR[q][0]), (pt,), (db,), (bV,))
                     entry(k + 1, h)
-        if last:
-            for hi, h in enumerate("AB"):
-                pM = T["pM" + h]
-                P(2048, [MM(pM[:, 0:64], T.idn[:], T.X[:, 2048 * hi + j:2048 * hi + 2048:32], j == 0, j == 31) for j in range(32)],
-                  ("X", "idn"), ("sums" + h,), ("pM" + h,))
-                V(64, CP(B("S0" + h), pM[:, 0:64]), ("sums" + h,), ("S0" + h,), ("pM" + h,))
         for hi, h in enumerate("AB"):
-            C, L, ct, lt = rec(t, h)
-            pV, pM, pU, p37 = T["pV" + h], T["pM" + h], T["pU" + h], T["p37" + h]
-            tbn = "pUA" if h == "A" else "pMA"
-            tb = T[tbn]
             o = H2 * hi
+            C, L, ct, lt = Cw[:, o:o + H2], Lw[:, o:o + H2], "C%d%s" % (t, h), "L%d%s" % (t, h)
+            bU, bV, bD, bE = ("p" + x + h for x in "UVDE")
+            pU, pV, pD, pE = T[bU], T[bV], T[bD], T[bE]
             sL, sC = "s%dL%s" % (t, h), "s%dC%s" % (t, h)
+            acc, F, VS = B("acc" + h), T["F" + h][:, 0:64], T["VS" + h]
+            na, nb = OPT["na"][h], NB[h]
+            zt = tuple(x for x in lastw if x[0] == "z" and x[-1] == h and (na == 6 or int(x[1]) >= na))
             for j in range(4):
-                sl = slice(1536 * j, 1536 * j + 1536)
-                V(768, SCAN(T["VS" + h][:, sl], T.m6[:], T["z" + h][:, sl], O.mult, O.max), tuple("z%d%s" % (k, h) for k in range(6)) + ("m6",), ("VS%d%s" % (j, h),))
+                src = T["z" + h][:, 1536 * j:1536 * (j + 1)] if na == 6 else T["Y" + h][:, 256 * na * nb * j + (na - 1) * nb % na:256 * na * nb * (j + 1):na]
+                V(128 * nb, SCAN(VS[:, 256 * nb * j:256 * nb * (j + 1)], T["mz%d" % nb][:], src, O.min, O.max),
+                  zt + ("mz%d" % nb,) + (() if na == 6 else tuple("Y%d%s" % (i, h) for i in range(OPT["chunks"] // 4 * j, OPT["chunks"] // 4 * (j + 1)))), ("VS%d%s" % (j, h),))
             vt = tuple("VS%d%s" % (j, h) for j in range(4))
-            for c, m0 in enumerate(range(NV[h], 16, 8)):
-                ms = range(m0, min(16, m0 + 8))
-                ps, bk = (p37, "p37" + h) if c == 0 else (pM, "pM" + h)
-                mm = []
-                for j, m in enumerate(ms):
-                    mm += [MM(ps[:, 64 * j:64 * j + 64], T.idn[:], vm(h, m), True, False), MM(ps[:, 64 * j:64 * j + 64], T.nid[:], B("Fs" + h), False, True)]
-                P(128 * len(ms), mm, vt + ("Fs" + h, "idn", "nid"), ("VF%d%s" % (c, h),), (bk,))
-                S(64 * len(ms), ACT(T["ind" + h][:, 64 * m0:64 * (m0 + len(ms))], ps[:, 0:64 * len(ms)], AF.Sign, bias=T.half[:, 0:1]),
-                  ("VF%d%s" % (c, h), "half0"), tuple("ind%d%s" % (m, h) for m in ms), (bk,))
-            for m in range(NV[h]):
-                V(64, TT(T["ind" + h][:, 64 * m:64 * m + 64], vm(h, m), pV[:, 448:512], O.is_ge), vt + ("F" + h,), ("ind%d%s" % (m, h),), ("pV" + h,))
+            for c, bk in enumerate((bD, bE)):
+                ps = T[bk]
+                k0 = P(512, [MM(ps[:], mat("nid"), T["F" + h][:], True, False)], ("F" + h, "Fr" + h, "nid"), ("VF" + bk,), (bk,))
+                P(512, [MM(ps[:, 64 * j:64 * j + 64], T.idn[:], VS[:, nb * (8 * c + j) + nb - 1:1024 * nb:16 * nb], False, j == 7) for j in range(8)], vt + ("idn",),
+                  ("VG" + bk,), (bk,), after=(k0,))
+                S(512, ACT(T["ind" + h][:, 512 * c:512 * c + 512], ps[:], AF.Sign, bias=half(0)), ("VF" + bk, "VG" + bk, "half"), ("ind%d%s" % (c, h),), (bk,))
             prev = ()
             for c in range(2):
-                prev = (P(512, ([MM(pU[:, 0:64], B("kq" + h), T.ones[:, 0:64], True, False)] if c == 0 else [])
-                          + [MM(pU[:, 0:64], T.Es[:, 128 * m:128 * m + 128], T["ind" + h][:, 64 * m:64 * m + 64], False, m == 15) for m in range(8 * c, 8 * c + 8)],
-                          tuple("ind%d%s" % (m, h) for m in range(8 * c, 8 * c + 8)) + ("Es", "kq" + h, "ones"), ("cnt%d%s" % (c, h),), ("pU" + h,), after=prev),)
-            V(64, TT(B("key" + h), pU[:, 0:64], B("Kp" + h), O.min), ("cnt0" + h, "cnt1" + h, "Kp" + h), ("key" + h,), ("pU" + h,))
-            kb, acc = B("kb" + h), B("acc" + h)
-            V(64, TURN(B("kt" + h), B("key" + h)), ("key" + h,), ("kt" + h,))
-            V(64, SCAN(kb, T.m16[:], B("kt" + h), O.mult, O.max), ("kt" + h, "m16"), ("kb" + h,))
-            for j in range(4):
-                V(64, TS(B("aT" + h, 16 * j, 16 * j + 16), B("kt" + h, 16 * j, 16 * j + 16), B("kb" + h, 16 * j + 15, 16 * j + 16), None, O.is_equal),
-                  ("kt" + h, "kb" + h), ("aT%d%s" % (j, h),))
-            V(64, TURN(acc, B("aT" + h)), tuple("aT%d%s" % (j, h) for j in range(4)), ("acc" + h,))
-            P(128, [MM(p37[:, 384:448], T.bm[:], acc, True, True), MM(p37[:, 448:512], T.ones[:], acc, True, True)],
-              ("acc" + h, "bm", "ones"), ("okB" + h,), ("p37" + h,))
-            AP = T["AP" + h]
-            for k in range(1, 7):
-                V(64, TT(AP[:, 64 * k:64 * k + 64], acc, pV[:, 64 * k - 64:64 * k], O.mult), ("acc" + h, "P%d%s" % (k, h)), ("AP%d%s" % (k, h),), ("pV" + h,))
-            S(64, ACT(B("okS" + h), p37[:, 384:448], AF.Copy), ("okB" + h,), ("okS" + h,), ("p37" + h,))
-            S(64, ACT(B("nok" + h), p37[:, 384:448], AF.Copy, scale=-1.0, bias=1.0), ("okB" + h,), ("nok" + h,), ("p37" + h,))
+                prev = (P(512, [MM(pD[:, 0:64], win(T.Ez, m), T["ind" + h][:, 64 * m:64 * m + 64], m == 0, m == 15) for m in range(8 * c, 8 * c + 8)],
+                          ("ind%d%s" % (c, h), "Ez"), ("cnt%d%s" % (c, h),), (bD,), after=prev),)
+            V(64, TS(B("f" + h), pD[:, 0:64], 8.0, None, O.is_ge), ("cnt0" + h, "cnt1" + h), ("f" + h,), (bD,))
+            V(128, TT(B("E" + h), B("f" + h), B("Kp" + h), O.mult), ("f" + h, "Kp" + h), ("E" + h,))
+            P(64, SUM(pD[:, 64:128], [(mat("hb"), B("E" + h))]), ("E" + h, "hb"), ("Es" + h,), (bD,))
+            V(64, TT(acc, B("E" + h), pD[:, 64:128], O.is_gt), ("E" + h, "Es" + h), ("acc" + h,), (bD,))
+            V(64, TT(B("keep" + h), L, pD[:, 64:128], O.subtract), (lt, "Es" + h), ("keep" + h,), (bD,))
+            segs = [mat("b" + h)] + ([] if last else [mat("bn")])
+            ns = 64 * len(segs)
+            P(ns, [MM(pD[:, 128 + 64 * j:192 + 64 * j], m_, acc, True, True) for j, m_ in enumerate(segs)], ("acc" + h, "b" + h + "m", "bn"), ("sg" + h,), (bD,))
+            V(ns, SCAN(B("wr" + h, 0, ns), T.dg[:, 0:ns], pD[:, 128:128 + ns], O.add, O.min), ("sg" + h, "dg"), ("wr" + h,), (bD,))
+            V(4, TT(T["voff" + h][:], B("wr" + h, 15, 64, 16), T.Kv[:, 4 * hi:4 * hi + 4], O.add), ("wr" + h, "Kv" + h), ("voff" + h,))
+            gather("v", B("Vsel" + h), VS[:, 0:1024 * nb], T["voff" + h][:], 64, vt + ("voff" + h,), ("Vsel" + h,))
             if not last:
-                V(64, lambda a_=B("asum" + h), b_=p37[:, 448:512]: g.vector.tensor_reduce(a_, b_, AxisListType.X, O.add), ("okB" + h,), ("asum" + h,), ("p37" + h,))
-            apt = tuple("AP%d%s" % (k, h) for k in range(7))
-            P(320, [MM(pU[:, 192:512], T.bm[:], AP[:, 64:384], True, True)], apt[1:6] + ("bm",), ("Pst" + h,), ("pU" + h,))
-            P(768, [MM(p37[:, 0:384], T.bm[:], AP[:, 64:448], True, False), MM(p37[:, 0:384], T.nbm[:], AP[:, 0:384], False, True)],
-              apt + ("bm", "nbm"), ("Nst" + h,), ("p37" + h,))
-            V(64, TT(B("aL" + h), acc, pV[:, 384:448], O.mult), ("acc" + h, "L" + h), ("aL" + h,), ("pV" + h,))
-            if EQS[h]:
-                for k in range(1, 6):
-                    S(64, ACT(T["SQ" + h][:, 64 * k - 64:64 * k], pU[:, 128 + 64 * k:192 + 64 * k], AF.Square, bias=T.nq[:, k:k + 1]),
-                      ("Pst" + h, "nq"), ("SQ%d%s" % (k, h),), ("pU" + h,))
-                S(320, ACT(T["EQ" + h][:, 64:384], T["SQ" + h][:], AF.Relu, scale=-1.0, bias=T.onec[:]), tuple("SQ%d%s" % (k, h) for k in range(1, 6)) + ("onec",),
-                  tuple("EQ%d%s" % (k, h) for k in range(1, 6)))
-            else:
-                for k in range(1, 6):
-                    V(64, TS(T["EQ" + h][:, 64 * k:64 * k + 64], pU[:, 128 + 64 * k:192 + 64 * k], T.qk[:, k:k + 1], None, O.is_equal),
-                      ("Pst" + h, "qk%d" % k), ("EQ%d%s" % (k, h),), ("pU" + h,))
-            V(384, TT(T["EN" + h][:], T["EQ" + h][:], p37[:, 0:384], O.mult), ("Nst" + h,) + tuple("EQ%d%s" % (k, h) for k in range(6)), ("EN" + h,), ("p37" + h,))
-            V(64, TT(B("nokL" + h), B("nok" + h), pV[:, 384:448], O.mult), ("nok" + h, "L" + h), ("nokL" + h,), ("pV" + h,))
-            P(512, [MM(p37[:, 384:448], T.idn[:], B("nokL" + h), True, False), MM(p37[:, 384:448], T.bm[:], acc, False, False)]
-              + [MM(p37[:, 384:448], T.idn[:], T["EN" + h][:, 64 * k:64 * k + 64], False, k == 5) for k in range(6)],
-              ("EN" + h, "nokL" + h, "acc" + h, "idn", "bm"), ("ls" + h,), ("p37" + h,))
-            S(64, ACT(T[sL][:], p37[:, 384:448], AF.Copy), ("ls" + h,), (sL,), ("p37" + h,))
+                V(4, TT(B("tb" + h), B("wr" + h, 79, 128, 16), T.Kt[:, 4 * hi:4 * hi + 4], O.add), ("wr" + h, "Kt" + h), ("tb" + h,))
+            P(128 if last else 64, SUM(pD[:, 320:384], [(mat("Wb"), B("Vsel" + h))]) + (SUM(pD[:, 384:448], [(T.bm[:], acc)]) if last else []),
+              ("Vsel" + h, "Wb", "acc" + h, "bm"), ("hb" + h,), (bD,))
+            V(64, SCAN(B("hw" + h), T.dg[:, 0:64], pD[:, 320:384], O.add, O.min), ("hb" + h, "dg"), ("hw" + h,), (bD,))
+            V(4, TS(B("h1" + h), B("hw" + h, 15, 64, 16), 31, None, O.bitwise_and), ("hw" + h,), ("h1" + h,))
+            V(4, TT(T["toff" + h][:], B("h1" + h), T.Kt[:, 8 + 4 * hi:12 + 4 * hi] if last else B("tb" + h), O.add), ("h1" + h, "tb" + h, "Kl" + h), ("toff" + h,))
             if not last:
-                send(sL, "in%dL%s" % (t + 1, h), "arr%dL%s" % (t + 1, h), 1, (sL,))
+                for a, x in ((0, "X"), (4096, "X2")):
+                    add("v", 0.25, [lambda f_=T["toff" + h], i_=B("Vsel" + h), a_=a: g.vector.tensor_copy(T.X[:, a_:a_ + 12288].indirect(f_[:, 0:4]), i_)],
+                        ("toff" + h, "Vsel" + h), (x, "Xw"))
             else:
-                dma("y", T.yl[:, o:o + H2], T[sL][:], (sL,), ())
-            P(256, [MM(pM[:, 64 * l:64 * l + 64], T.hsh[:, 128 * l:128 * l + 128], C, True, True) for l in range(4)], (ct, "hsh"), ("SH" + h,), ("pM" + h,))
-            P(64, [MM(pM[:, 320:384], T.tri[:], B("aL" + h), True, True)], ("aL" + h, "tri"), ("sh" + h,), ("pM" + h,))
-            for l in range(1, 5):
-                S(64, ACT(T["ES" + h][:, 64 * l - 64:64 * l], pM[:, 320:384], AF.Sign, bias=T.half[:, l:l + 1]), ("sh" + h, "half%d" % l), ("ES%d%s" % (l, h),), ("pM" + h,))
-            V(256, TT(T["EC" + h][:], T["ES" + h][:], pM[:, 0:256], O.mult), ("SH" + h,) + tuple("ES%d%s" % (l, h) for l in range(1, 5)), ("EC" + h,), ("pM" + h,))
-            P(384, [MM(pM[:, 384:448], T.hid[:, 0:128], C, True, False), MM(pM[:, 384:448], T.hid[:, 128:256], C, False, False)]
-              + [MM(pM[:, 384:448], T.idn[:], T["EC" + h][:, 64 * l:64 * l + 64], False, l == 3) for l in range(4)],
-              ("EC" + h, "idn", "hid0", "hid1", ct), ("cs" + h,), ("pM" + h,))
-            S(64, ACT(T[sC][:], pM[:, 384:448], AF.Copy), ("cs" + h,), (sC,), ("pM" + h,))
-            if not last:
-                send(sC, "in%dC%s" % (t + 1, h), "arr%dC%s" % (t + 1, h), 1, (sC,))
-            else:
-                dma("y", T.yc[:, o:o + H2], T[sC][:], (sC,), ())
-            S(64, ACT(B("aM" + h), acc, AF.Copy, scale=T.q6[:]), ("acc" + h, "q6"), ("aM" + h,))
-            P(1024, [MM(tb[:, 0:8], T.Em[:, 128 * a:128 * a + 128], B("aM" + h, a, 128, 16), a == 0, a == 15) for a in range(16)],
-              ("aM" + h, "acc" + h) + EM, ("tb" + h,), (tbn,))
-            V(4, TT(T["voff" + h][:], tb[:, 0:4], B("Kv" + h), O.add), ("tb" + h, "Kv" + h), ("voff" + h,), (tbn,))
-            V(4, CP(B("tt" + h), tb[:, 4:8]), ("tb" + h,), ("okd" + h,), (tbn,))
-            add("s", 0.16, [lambda o_=B("Vsel" + h), v_=T["VS" + h], f_=T["voff" + h]: g.scalar.activation(o_, v_[:, 0:6144].indirect(f_[:, 0:4]), AF.Copy)],
-                vt + ("voff" + h,), ("Vsel" + h,))
-            P(1024, [MM(tb[:, 8:12], T.Wm[:, 128 * a:128 * a + 128], B("Vsel" + h, a, 64, 16), a == 0, a == 15) for a in range(16)],
-              ("Vsel" + h,) + WM, ("hd" + h,), (tbn,))
-            V(4, CP(B("h0" + h), tb[:, 8:12]), ("hd" + h,), ("h0" + h,), (tbn,))
-            V(4, TS(B("h1" + h), B("h0" + h), 31, None, O.bitwise_and), ("h0" + h,), ("h1" + h,))
-            V(4, TT(B("h2" + h), B("h1" + h), B("K1" + h), O.add), ("h1" + h, "K1" + h), ("h2" + h,))
-            V(4, TT(B("h3" + h), B("h2" + h), B("tt" + h), O.mult), ("h2" + h, "okd" + h), ("h3" + h,))
-            V(4, TT(T["toff" + h][:], B("h3" + h), B("K2" + h), O.add), ("h3" + h, "K2" + h), ("toff" + h,))
-            if not last:
-                add("v", 0.25, [lambda f_=T["toff" + h], i_=B("Vsel" + h): g.vector.tensor_copy(T.X[:, 0:4224].indirect(f_[:, 0:4]), i_)],
-                    ("toff" + h, "Vsel" + h, "Xd"), ("X",))
-            else:
-                add("s", 0.16, [lambda o_=B("xo" + h), f_=T["toff" + h]: g.scalar.activation(o_, T.X[:, 0:4224].indirect(f_[:, 0:4]), AF.Copy)],
-                    ("X", "Xd", "toff" + h), ("xo" + h,))
+                gather("v", B("xo" + h), T.X[:, 0:4096], T["toff" + h][:, 0:4], 64, ("X", "toff" + h), ("xo" + h,))
                 V(128, TT(B("xd" + h), B("Vsel" + h), B("xo" + h), O.subtract), ("Vsel" + h, "xo" + h), ("xd" + h,))
-                V(128, TT(B("xe" + h), B("xd" + h), B("okS" + h), O.mult), ("xd" + h, "okS" + h), ("xe" + h,))
+                V(64, TT(B("xe" + h), B("xd" + h), pD[:, 384:448], O.mult), ("xd" + h, "hb" + h), ("xe" + h,), (bD,))
                 V(128, TT(B("yss" + h), B("xe" + h), B("S0" + h), O.add), ("xe" + h, "S0" + h), ("yss" + h,))
-                dma("s", T.ys[:, o:o + H2], B("yss" + h), ("yss" + h,), ())
-            Fp = pV[:, 448:512]
-            V(64, TT(B("fd" + h), B("Vsel" + h), Fp, O.subtract), ("Vsel" + h, "F" + h), ("fd" + h,), ("pV" + h,))
-            V(128, TT(B("xd" + h), B("fd" + h), B("okS" + h), O.mult), ("fd" + h, "okS" + h), ("xd" + h,))
-            V(64, TS(B("fi" + h), B("xd" + h), 0.5, -0.25, O.mult, O.add), ("xd" + h,), ("fi" + h,))
+                dma("s", [(T.ys[:, o:o + H2], B("yss" + h))], ("yss" + h,), ())
+            P(256, [MM(pE[:, 64 * l:64 * l + 64], T.hsh[:, 128 * l:128 * l + 128], C, True, True) for l in range(4)], (ct, "hsh"), ("SH" + h,), (bE,))
+            V(64, TT(B("aL" + h), acc, pV[:, 448:512], O.mult), ("acc" + h, "L" + h), ("aL" + h,), (bV,))
+            V(64, TT(B("ay" + h), acc, pV[:, 320:384], O.mult), ("acc" + h, "u0" + h, "u" + h), ("ay" + h,), (bV,))
+            P(64, SUM(pE[:, 256:320], [(T.tri[:], B("aL" + h))]), ("aL" + h, "tri"), ("sh" + h,), (bE,))
+            for l in range(1, 5):
+                S(64, ACT(T["ES" + h][:, 64 * l - 64:64 * l], pE[:, 256:320], AF.Sign, bias=half(l)), ("sh" + h, "half"), ("ES%d%s" % (l, h),), (bE,))
+            V(256, TT(T["EC" + h][:], T["ES" + h][:], pE[:, 0:256], O.mult), ("SH" + h,) + tuple("ES%d%s" % (l, h) for l in range(1, 5)), ("EC" + h,), (bE,))
+            new = [(mat("hid"), C), (mat("hs4"), C)] + [(T.idn[:], T["EC" + h][:, 64 * l:64 * l + 64]) for l in range(4)]
+            P(384, SUM(pE[:, 320:384], new), ("EC" + h, "idn", "hid", "hs4", ct), ("cs" + h,), (bE,))
+            S(64, ACT(T[sC][:], pE[:, 320:384], AF.Copy), ("cs" + h,), (sC,), (bE,))
             if not last:
-                V(64, TT(B("Fs" + h), B("fi" + h), Fp, O.add), ("fi" + h, "F" + h), ("Fs" + h,), ("pV" + h,))
-                V(64, TT(Fp, B("fi" + h), Fp, O.add), ("fi" + h, "F" + h), ("F" + h,), ("pV" + h,))
+                send(T["C%d" % (t + 1)][:, o:o + H2], T[sC][:], "arr%dC%s" % (t + 1, h), 1, (sC,), ("C%d%s" % (t + 1, h),))
             else:
-                V(64, TT(B("yfs" + h), B("fi" + h), Fp, O.add), ("fi" + h, "F" + h), ("yfs" + h,), ("pV" + h,))
-                dma("s", T.yf[:, o:o + H2], B("yfs" + h), ("yfs" + h,), ())
+                dma("y", [(T.yc[:, o:o + H2], T[sC][:])], (sC,), ())
+            AP = T["AP" + h]
+            k0 = P(384, [MM(pU[:, 64:448], T.idn[:], T.Kq[:], True, False)], ("idn", "Kq"), ("Pd0" + h,), (bU,))
+            for k in range(1, 6):
+                V(64, TT(AP[:, k::6], acc, pV[:, 64 * k - 64:64 * k], O.mult), ("acc" + h, "P%d%s" % (k, h)), ("AP%d%s" % (k, h),), (bV,))
+            P(384, [MM(pU[:, 64:448], T.bm[:], AP[:], False, True)], tuple("AP%d%s" % (k, h) for k in range(6)) + ("bm",), ("Pd" + h,), (bU,), after=(k0,))
+            k1 = P(384, [MM(pV[:, 384:448], l_, r_, j == 0, False) for j, (l_, r_) in enumerate([(T.b8[:], B("ay" + h))] + new[:2])],
+                   ("ay" + h, "b8", "hid", "hs4", ct), ("k5a" + h,), (bV,))
+            P(256, [MM(pV[:, 384:448], l_, r_, False, j == 3) for j, (l_, r_) in enumerate(new[2:])], ("EC" + h, "idn"), ("k5b" + h,), (bV,), after=(k1,))
+            if h in OPT["eqs"]:
+                S(384, ACT(T["SQ" + h][:], pU[:, 64:448], AF.Square), ("Pd0" + h, "Pd" + h), ("SQ" + h,), (bU,))
+                S(384, ACT(T["EQ" + h][:], T["SQ" + h][:], AF.Relu, scale=-1.0, bias=T.col[:, 30:31]), ("SQ" + h, "onec"), ("EQ" + h,))
+            else:
+                V(384, TS(T["EQ" + h][:], pU[:, 64:448], 0.0, None, O.is_equal), ("Pd0" + h, "Pd" + h), ("EQ" + h,), (bU,))
+            V(384, TT(T["EN" + h][:, 0:383], T["EQ" + h][:, 0:383], pU[:, 65:448], O.mult), ("EQ" + h, "Pd0" + h, "Pd" + h), ("EN" + h,), (bU,))
+            V(192, SCAN(T["LS" + h][:, 0:383], T.m6[:, 0:383], T["EN" + h][:, 0:383], O.min, O.max, 1.0), ("EN" + h, "m6"), ("LS" + h,))
+            V(128, TT(pU[:, 0:64], T["LS" + h][:, 4::6], B("keep" + h), O.max), ("LS" + h, "keep" + h), ("Lm" + h,), (bU,))
+            V(64, TS(B("k5" + h), pV[:, 384:448], -0.9375, None, O.add), ("k5a" + h, "k5b" + h), ("k5" + h,), (bV,))
+            V(64, TS(B("n5" + h), B("k5" + h), 3, None, O.bitwise_and), ("k5" + h,), ("n5" + h,))
+            V(128, TT(B("e5" + h), B("n5" + h), T["EQ" + h][:, 5::6], O.mult), ("n5" + h, "EQ" + h), ("e5" + h,))
+            V(64, TT(T[sL][:], B("e5" + h), pU[:, 0:64], O.add), ("e5" + h, "Lm" + h), (sL,), (bU,))
+            if not last:
+                send(T["L%d" % (t + 1)][:, o:o + H2], T[sL][:], "arr%dL%s" % (t + 1, h), 1, (sL,), ("L%d%s" % (t + 1, h),))
+            else:
+                dma("y", [(T.yl[:, o:o + H2], T[sL][:])], (sL,), ())
+            P(384, SUM(pE[:, 384:448], [(mat("hid"), F), (mat("b256"), acc), (mat("kq"), T.ones[:, 0:64]), (mat("hid"), B("Vsel" + h))])
+              + SUM(pE[:, 448:512], [(T.idn[:], F), (mat("n256"), acc)]),
+              ("F" + h, "acc" + h, "Vsel" + h, "hid", "idn", "b256", "n256", "kq", "ones"), ("fa" + h,), (bE,))
+            V(64, TS(B("fr" + h), pE[:, 384:448], 12582912.0 - 256, -12582912.0, O.add, O.add), ("fa" + h,), ("fr" + h,), (bE,))
+            if not last:
+                V(64, TT(F, B("fr" + h), pE[:, 448:512], O.max), ("fr" + h, "fa" + h), ("F" + h,), (bE,))
+                spread(h)
+            else:
+                V(64, TT(B("yfs" + h), B("fr" + h), pE[:, 448:512], O.max), ("fr" + h, "fa" + h), ("yfs" + h,), (bE,))
+                dma("s", [(T.yf[:, o:o + H2], B("yfs" + h))], ("yfs" + h,), ())
+            if hi and not last:
+                P(128, SUM(T.pUA[:, 0:64], [(ones, B("accA")), (ones, acc)]), ("accA", "accB", "ones"), ("As",), ("pUA",))
+                S(64, ACT(T.junk[:], T.pUA[:, 0:64], AF.Copy, accum_out=T.acnt[:]), ("As",), ("acnt", "junk"), ("pUA",))
 
     n = len(ops)
     succ = [[] for _ in range(n)]
     for k, p in enumerate(ops):
         for d in p["all"]:
             succ[d].append(k)
+
+    def gap(a, b):
+        a, b = min(a, b), max(a, b)
+        return 0.0 if a not in ops[b]["deps"] else OPT["ws"] if ops[a]["q"] == ops[b]["q"] else OPT["wx"]
+    cost = [p["cost"] for p in ops]
+    hold = [0.0 if p["q"] == "r" else 0.06 * len(p["fns"]) if p["sem"] is not None and p["q"] in "sy" else p["cost"] for p in ops]
+    pred = [[(d, gap(d, k)) for d in sorted(p["all"])] for k, p in enumerate(ops)]
+    next_ = [[(d, gap(d, k)) for d in succ[k]] for k in range(n)]
+
+    def place(seq, before, back):
+        at, taken = [0.0] * n, {}
+        for k in seq:
+            lead = cost[k] - hold[k] if back else 0.0
+            s0 = max([at[d] + (hold[d] if back else cost[d]) + w for d, w in before[k]], default=0.0) + lead
+            line = taken.setdefault(ops[k]["q"], [])
+            lo, hi_ = 0, len(line)
+            while lo < hi_:
+                mid = (lo + hi_) // 2
+                lo, hi_ = (mid + 1, hi_) if line[mid][1] <= s0 else (lo, mid)
+            while lo < len(line) and line[lo][0] < s0 + hold[k] - 1e-9:
+                s0 = max(s0, line[lo][1])
+                lo += 1
+            if hold[k]:
+                line.insert(lo, (s0, s0 + hold[k]))
+            at[k] = s0
+        return at
+
     prio = [0.0] * n
     for k in range(n - 1, -1, -1):
-        prio[k] = ops[k]["cost"] + 0.1 + max([prio[s] for s in succ[k]], default=0.0)
-    left = [len(p["all"]) for p in ops]
-    ready = [0.0] * n
-    free, pool, order = {}, {}, []
-    for k in range(n):
-        if left[k] == 0:
-            pool.setdefault(ops[k]["q"], []).append(k)
-    while len(order) < n:
-        best = None
-        for q, lst in pool.items():
-            if lst:
-                s0 = max(free.get(q, 0.0) if q != "r" else 0.0, min(ready[k] for k in lst))
-                if best is None or s0 < best[0]:
-                    best = (s0, q)
-        s0, q = best
-        k = max((k for k in pool[q] if ready[k] <= s0 + 0.02), key=lambda k: prio[k])
-        s0 = max(s0, ready[k])
-        pool[q].remove(k)
-        order.append(k)
-        hold = 0.1 if (ops[k]["sem"] is not None and q != "r") else ops[k]["cost"]
-        free[q] = s0 + hold
-        end = s0 + ops[k]["cost"]
-        for s in succ[k]:
-            ready[s] = max(ready[s], end + (0.15 if ops[s]["q"] == q else 0.25))
-            left[s] -= 1
-            if left[s] == 0:
-                pool.setdefault(ops[s]["q"], []).append(s)
+        prio[k] = cost[k] + max([prio[s] + w for s, w in next_[k]], default=0.0)
+
+    def tighten(seq):
+        at = place(seq, pred, False)
+        back = place(sorted(range(n), key=lambda k: (-(at[k] + cost[k]), -k)), next_, True)
+        at = place(sorted(range(n), key=lambda k: (-(back[k] + hold[k]), k)), pred, False)
+        return max(at[k] + cost[k] for k in range(n)), at
+
+    if n not in PLAN:
+        best = tighten(sorted(range(n), key=lambda k: -prio[k]))
+        rng = np.random.RandomState(OPT["seed"])
+        for _ in range(OPT["tries"]):
+            mid, wide, key = rng.uniform(0, best[0]), rng.uniform(2, 12), rng.normal(0, 0.6, n).tolist()
+            for k in range(n):
+                key[k] = max([best[1][k] + (key[k] if abs(best[1][k] - mid) < wide else 0.0)] + [key[d] + 1e-6 for d, _w in pred[k]])
+            other = tighten(sorted(range(n), key=lambda k: key[k]))
+            if other[0] <= best[0]:
+                best = other
+        if "hook" in OPT:
+            best = OPT["hook"](ops, place, pred, next_, cost, hold, best)
+        PLAN[n] = best
+    best = PLAN[n]
+    order = sorted(range(n), key=lambda k: (best[1][k], k))
+    OPT["span"] = best[0]
     count = {q: 0 for q in qsem}
     know = {q: {} for q in eng}
     done, seen = {}, {}
@@ -515,12 +573,11 @@ def rank_program(g, core, T, topo):
         seen[k] = dict(know[q])
         if p["sem"] is not None:
             s, v = p["sem"]
-            ins = p["fns"][0]()
-            if v is None:
-                done[k] = None
-            else:
-                ins.then_inc(T.sem[s], v)
-                done[k] = (s, v)
+            for f in p["fns"]:
+                ins = f()
+                if v is not None:
+                    ins.then_inc(T.sem[s], 16)
+            done[k] = None if v is None else (s, v)
         else:
             for f in p["fns"]:
                 f().then_inc(T.sem[qsem[q]], 1)
@@ -528,9 +585,7 @@ def rank_program(g, core, T, topo):
             done[k] = (qsem[q], count[q])
     for q, s in qsem.items():
         g.wait_ge(T.sem[s], count[q])
-    for j in range(ndma[0]):
-        g.wait_ge(T.sem["d%d" % j], 16)
     for p in ops:
-        if p["q"] == "r":
+        if p["sem"] is not None and p["sem"][1] is not None:
             g.wait_ge(T.sem[p["sem"][0]], p["sem"][1])
     g.wait_ge(T.sem.loc, loc[0])

@@ -1,32 +1,32 @@
 import math
 import numpy as np
+from concourse.bass import DstId, RemoteDMATransfer
 from concourse.mybir import AluOpType as O, ActivationFunctionType as AF
 
 H2 = 64
-OPT = {"tiles": 3, "te": {"A1": "s", "A2": "g", "A3": "g", "B1": "v", "B2": "g", "B3": "g"}, "na": {"A": 4, "B": 4}, "fast": "B", "gv": {}, "eqs": "", "w8": "v", "db": "v",
-       "ws": 0.2, "wx": 0.25, "f": 1.1, "tries": 1500, "seed": 0, "chunks": 16}
+OPT = {"tiles": 3, "te": {"A1": "s", "A2": "g", "A3": "g", "B1": "v", "B2": "g", "B3": "g"}, "na": {"A": 3, "B": 4}, "fast": "B", "gv": {}, "eqs": "", "w8": "v", "db": "v",
+       "nf": {"A": 0, "B": 0}, "fold": 6.0, "lg": "s", "b": "v", "gs": 0, "x2": "v", "c0": "v", "c5": "AB", "cmpv": "B", "ws": 0.22, "wx": 0.22, "f": 1.15, "gr": 1.7, "paces": ((1.0, 1.56), (1.35, 2.08), (1.4, 1.25)), "tries": 5000, "shake": 0.6, "seed": 0, "chunks": 16}
 PLAN = {}
-TILES = {3: ((0, 1, 2, 3, 3), {1: (8, 1), 2: (12, 2), 3: (16, 3)}),
-         2: ((0, 1, 1, 3, 3), {1: (12, 1), 3: (16, 3)})}
+TILES = {3: ((0, 1, 2, 3, 3, 3), {1: (8, 1), 2: (12, 2), 3: (16, 3)})}
 SCRATCH = {}
 SEMAPHORES = ["sv", "ss", "st_", "sg", "loc", "arst1", "arst2"] + ["arr%d%s%s" % (t, x, h) for t in (1, 2) for x in "LC" for h in "AB"]
-SEMAPHORES += ["d%d" % k for k in range(40)]
+SEMAPHORES += ["d%d" % k for k in range(40)] + ["f%s%d%s" % (x, t, h) for x in "abl" for t in range(3) for h in "AB"]
 _BF, _F32, _I32, _U16 = "bfloat16", "float32", "int32", "uint16"
-_COL = ("qc", "q8", "iz", "kb", "qA", "qB", "c0", "c1", "c2", "c3", "c4", "c5", "w", "one")
-_MAT = ("nid", "hid", "hs4", "kc", "ke", "kq", "bA", "bB", "bn", "b256", "n256", "hb", "Wb")
+_COL = ("qc", "q8", "iz", "kb", "qA", "qB", "c0", "c1", "c2", "c3", "c4", "c5", "w", "one", "c6", "c7")
+_MAT = ("nid", "hid", "hs4", "kc", "ke", "kq", "bA", "bB", "bn", "b256", "n256", "hb", "Wb", "kd", "a1", "a2", "a3", "a4", "a5")
 for _n, _c, _d in (("X", 16384, _BF), ("C0", 128, _BF), ("C1", 128, _BF), ("C2", 128, _BF), ("L0", 128, _BF), ("L1", 128, _BF), ("L2", 128, _BF),
                    ("wts", 1, _BF), ("st0", 128, _I32), ("st1", 128, _I32), ("st2", 128, _I32), ("pI", 1, _I32), ("aI", 1, _I32),
                    ("col", 64, _F32), ("jrow", 18, _F32), ("cqx", 18, _F32), ("dif", 17, _F32), ("dif8", 21, _F32), ("il0", 4, _F32), ("il", 4, _F32),
-                   ("Kv", 8, _F32), ("Kt", 16, _F32), ("acnt", 1, _F32), ("junk", 64, _BF), ("b8", 128, _F32),
+                   ("Kv", 16, _F32), ("Kt", 16, _F32), ("acnt", 1, _F32), ("junk", 64, _BF), ("b8", 128, _F32),
                    ("ones", 960, _BF), ("bm0", 128, _BF), ("bm", 128, _BF), ("idn", 128, _BF), ("tri", 128, _BF), ("shm", 512, _BF),
                    ("hsd", 512, _BF), ("hsh", 512, _BF), ("mat", len(_MAT) * 128, _BF), ("Wz", 144, _BF), ("Ez", 144, _BF), ("Rm", 21 * 128, _BF),
                    ("mz2", 512, _BF), ("mz3", 768, _BF), ("mz4", 1024, _BF), ("mz5", 1280, _BF), ("mz6", 1536, _BF),
-                   ("m6", 384, _BF), ("k6", 384, _BF), ("Kq", 384, _BF), ("j16", 128, _BF), ("dg0", 128, _BF), ("dg", 128, _BF)):
+                   ("SP", 4276, _BF), ("TB", 1368, _BF), ("shd", 512, _BF), ("jj", 128, _BF), ("j16", 128, _BF), ("dg0", 128, _BF), ("dg", 128, _BF)):
     SCRATCH[_n] = ("sbuf", [128, _c], _d)
 _PACK = {}
 _SMALL = {_BF: (("b", 64), ("Kp", 64), ("f", 64), ("E", 64), ("acc", 64), ("aL", 64), ("e0", 64), ("t0", 64), ("Vsel", 64), ("xo", 64),
                 ("fr", 64), ("yfs", 64), ("w8", 64), ("c0", 64), ("e5", 64), ("keep", 64)),
-          _F32: (("base", 64), ("wr", 128), ("tb", 4), ("S0", 64), ("xd", 64), ("xe", 64), ("yss", 64), ("ay", 64)),
+          _F32: (("base", 64), ("wr", 128), ("tb", 4), ("S0", 64), ("xd", 64), ("xe", 64), ("yss", 64), ("ay", 64), ("wc", 64)),
           _I32: (("ab", 128), ("am", 128), ("k8", 64), ("Q", 64), ("s1", 64), ("n1", 64), ("hw", 64), ("h1", 4), ("k5", 64), ("n5", 64))}
 for _h in "AB":
     for _d, _names in _SMALL.items():
@@ -35,8 +35,8 @@ for _h in "AB":
             _PACK[_n + _h] = ("pk" + _d[0] + _h, _at, _c)
             _at += -(-_c // 32) * 32
         SCRATCH["pk" + _d[0] + _h] = ("sbuf", [128, _at], _d)
-    for _n, _c, _d in (("z", 6144, _BF), ("Y", 12288, _BF), ("VS", 6144, _BF), ("ind", 1024, _BF), ("off", 64, _U16), ("mk", 960, _BF), ("co", 960, _BF),
-                       ("AP", 384, _BF), ("SQ", 384, _BF), ("EQ", 384, _BF), ("EN", 384, _BF), ("LS", 384, _BF), ("ES", 256, _BF), ("EC", 256, _BF),
+    for _n, _c, _d in (("z", 5120, _BF), ("Y", 12288, _BF), ("VS", 4096, _BF), ("ind", 1024, _BF), ("off", 64, _U16), ("mk", 960, _BF), ("co", 960, _BF),
+                       ("ES", 256, _BF), ("EC", 256, _BF), ("db4", 960, _BF), ("db5", 960, _BF), ("loff", 4, _U16),
                        ("F", 512, _BF), ("voff", 4, _U16), ("toff", 4, _U16), ("da1", 832, _BF), ("db1", 832, _BF), ("da2", 768, _BF),
                        ("db2", 768, _BF), ("da3", 960, _BF), ("db3", 960, _BF), ("T1", 832, _BF), ("T2", 768, _BF), ("T3", 960, _BF)):
         SCRATCH[_n + _h] = ("sbuf", [128, _c], _d)
@@ -49,15 +49,30 @@ for _h in "AB":
 
 def rank_program(g, core, T, topo):
     rank = T.rank_of(core)
+    helper = {}
+    for c in T.cores:
+        helper[c] = [x for x in topo.cores_of(c) if topo.die(x) == topo.die(c) and x not in T.cores and x not in helper.values()][0]
     if rank is None:
+        for c in [c for c in T.cores if helper[c] == core]:
+            rid, pid = topo.addr(c)[:2]
+            n, sent = len(topo.engines(core, c)), 0
+            for t in range(3):
+                for h in "AB":
+                    if OPT["nf"][h]:
+                        g.wait_ge(T.sem["fa%d%s" % (t, h)], n)
+                        g.remote_dma(T["Y" + h][:, 4096 + 1024 * t:5120 + 1024 * t], T["Y" + h][:, 1024 * t:1024 * t + 1024], T.sem["fb%d%s" % (t, h)],
+                                     T.sem.loc, pid, rid, topo.mask(core, c))
+                        sent += n
+            if sent:
+                g.wait_ge(T.sem.loc, sent)
         return
+    NH = len(topo.engines(core, helper[core]))
     N = len(T.cores)
     TILE, ENDS = TILES[OPT["tiles"]]
     WID = {q: a - b + 2 for q, (a, b) in ENDS.items()}
     RR = {q: list(range(a, b, -1)) + [17 + b] for q, (a, b) in ENDS.items()}
     eng = {"v": g.vector, "s": g.scalar, "t": g.tensor, "y": g.sync, "g": g}
     qsem = {"v": "sv", "s": "ss", "t": "st_", "g": "sg"}
-    CY = 0.00083 * OPT["f"]
     ops = []
     lastw, readers, bank = {}, {}, {}
     ndma, loc = [0], [0]
@@ -87,10 +102,12 @@ def rank_program(g, core, T, topo):
     def win(Z, m):
         return Z[:, 15 - m:143 - m]
 
-    NB = {h: 6 if a == 6 else 7 - a for h, a in OPT["na"].items()}
+    NB = {h: 1 if OPT["nf"][h] else 7 - a for h, a in OPT["na"].items()}
 
     def slot(h, k):
         a, b = OPT["na"][h], NB[h]
+        if OPT["nf"][h]:
+            return (T["z" + h], 1, 1024 * k) if k < OPT["nf"][h] else (T["Y" + h], 1, 1024 * (k - OPT["nf"][h]))
         if k < a:
             return T["z" + h], a, k
         v = (a - 1) * b
@@ -120,13 +137,13 @@ def rank_program(g, core, T, topo):
         return k
 
     def V(n, fn, r, w, banks=(), **kw):
-        return add("v", 0.005 + max(64, n) * CY, [fn], r, w, banks, **kw)
+        return add("v", (0.002, max(64, n), 0), [fn], r, w, banks, **kw)
 
     def S(n, fn, r, w, banks=()):
-        return add("s", 0.035 + max(64, n) * CY, [fn], r, w, banks)
+        return add("s", (0.03, max(64, n), 0), [fn], r, w, banks)
 
     def P(cols, fns, r, w, banks=(), **kw):
-        return add("t", 0.01 + cols * CY, fns, r, w, banks, **kw)
+        return add("t", (0.002, cols, 0), fns, r, w, banks, **kw)
 
     def TS(out, in0, s1, s2, o0, o1=None):
         if o1 is None:
@@ -161,7 +178,7 @@ def rank_program(g, core, T, topo):
 
     def gather(q, out, window, offs, n, r, w):
         fn = (lambda: g.scalar.activation(out, window.indirect(offs), AF.Copy)) if q == "s" else (lambda: g.vector.tensor_copy(out, window.indirect(offs)))
-        return add(q, 0.065 + n * 1.56 * CY, [fn], r, w)
+        return add(q, (0.065, 0, n), [fn], r, w)
 
     def dma(q, pairs, r, w, cost=2.2):
         s = "d%d" % ndma[0]
@@ -169,10 +186,10 @@ def rank_program(g, core, T, topo):
         return add(q, cost, [lambda o_=o_, i_=i_: eng[q].dma_start(o_, i_) for o_, i_ in pairs], r, w, sem=(s, 16 * len(pairs)))
 
     def aff(out, in_, pat, cmp, base, cm, r, w, n=128):
-        return add("g", 0.17 + 2 * n * CY, [lambda: g.affine_select(out, in_, pat, cmp, 0.0, base, cm)], r, w)
+        return add("g", (0.17, 2 * n, 0), [lambda: g.affine_select(out, in_, pat, cmp, 0.0, base, cm)], r, w)
 
     def iota(out, pat, base, n, w):
-        add("g", 0.13 + 2 * n * CY, [lambda: g.iota(out, pat, base, 0, allow_small_or_imprecise_dtypes=True)], (), w)
+        add("g", (0.13, 2 * n, 0), [lambda: g.iota(out, pat, base, 0, allow_small_or_imprecise_dtypes=True)], (), w)
 
     NE = min(len(topo.engines(core, c)) for c in T.cores if c != core)
 
@@ -185,7 +202,8 @@ def rank_program(g, core, T, topo):
         return add("r", 2.0, [], (), w, sem=(sem, NE), extra=(k,))
 
     def spread(h):
-        dma("y", [(T["F" + h][:, 64 * j:64 * j + 64], T["F" + h][:, 0:64]) for j in range(1, 8)], ("F" + h,), ("Fr" + h,), 2.6)
+        if h not in OPT["cmpv"]:
+            dma("y", [(T["F" + h][:, 64 * j:64 * j + 64], T["F" + h][:, 0:64]) for j in range(1, 8)], ("F" + h,), ("Fr" + h,), 2.6)
 
     dma("y", [(T.X[:, 0:4096], T.x[:])], (), ("X",), 6.0)
     dma("s", [(T.st0[:], T.st[:])], (), ("st0",))
@@ -197,7 +215,10 @@ def rank_program(g, core, T, topo):
         spread(h)
     send(T.st1[:], T.st0[:], "arst1", 1, ("st0",), ("st1",))
     send(T.st2[:], T.st0[:], "arst2", 2, ("st0",), ("st2",))
-    V(2048, CP(T.X[:, 4096:8192], T.X[:, 0:4096]), ("X",), ("X2",))
+    if OPT["x2"] == "v":
+        V(2048, CP(T.X[:, 4096:8192], T.X[:, 0:4096]), ("X",), ("X2",))
+    else:
+        dma("y", [(T.X[:, 4096:8192], T.x[:])], ("X",), ("X2",), 4.0)
     ones = T.ones[:, 0:128]
     LN3 = math.log(3.0)
     add("g", 0.14, [lambda: g.iota(T.pI[:], [[0, 1]], 0, 1)], (), ("pI",))
@@ -209,9 +230,11 @@ def rank_program(g, core, T, topo):
     V(1, CP(col("qc"), T.aI[:]), ("aI",), ("qc",))
     for name, a, b in (("q8", 8.0, 0.0), ("kb", -LN3, 2 * LN3), ("qA", float(NB["A"]), 0.0), ("qB", float(NB["B"]), 0.0),
                        ("c0", -65536.0, 983039.0 + NB["A"]), ("c1", -65536.0, 983039.0 + NB["B"]), ("c2", -65536.0, 983040.0 + 8192),
-                       ("c3", -65536.0, 983040.0 + 10240), ("c4", 0.0, 0.0), ("c5", 0.0, 2048.0), ("one", 1.0, 64.0)):
+                       ("c3", -65536.0, 983040.0 + 10240), ("c4", 0.0, 0.0), ("c5", 0.0, 2048.0), ("one", 1.0, 64.0),
+                       ("c6", -65536.0, 983040.0 + 4148), ("c7", -65536.0, 983040.0 + 4212)):
         V(1, TS(col(name), col("qc"), a, b, O.mult, O.add), ("qc",), (name,))
     V(6, TS(T.col[:, 16:22], T.jrow[:, 1:7], -1.0, col("one"), O.mult, O.add), ("jrow", "one"), ("qk",))
+    V(6, TS(T.col[:, 32:38], T.col[:, 16:22], -4.0, 4.0, O.mult, O.add), ("qk",), ("qk4",))
     V(5, TS(T.col[:, 24:29], T.jrow[:, 0:5], -1.0, -0.5, O.mult, O.add), ("jrow",), ("half",))
     V(1, MS(T.col[:, 30:31], 1.0), (), ("onec",))
     V(1, TS(col("iz"), col("qc"), 0.0, None, O.is_equal), ("qc",), ("iz",))
@@ -221,7 +244,8 @@ def rank_program(g, core, T, topo):
     aff(T.idn[:], ones, [[-1, 128]], O.is_equal, 0, 1, ("ones",), ("idn",))
     V(4, TS(T.il[:], T.il0[:], col("qc"), None, O.add), ("il0", "qc"), ("il",))
     for out, a, c, w in ((T.Kv[:, 0:4], 16.0 * NB["A"], "c0", "KvA"), (T.Kv[:, 4:8], 16.0 * NB["B"], "c1", "KvB"), (T.Kt[:, 0:4], 32.0, "c2", "KtA"), (T.Kt[:, 4:8], 32.0, "c3", "KtB"),
-                         (T.Kt[:, 8:12], 32.0, "c4", "KlA"), (T.Kt[:, 12:16], 32.0, "c5", "KlB")):
+                         (T.Kt[:, 8:12], 32.0, "c4", "KlA"), (T.Kt[:, 12:16], 32.0, "c5", "KlB"), (T.Kv[:, 8:12], 1.0, "c6", "KsA"),
+                         (T.Kv[:, 12:16], 1.0, "c7", "KsB")):
         V(4, TS(out, T.il[:], a, col(c), O.mult, O.add), ("il", c), (w,))
     V(18, TS(T.cqx[:], T.jrow[:], col("qc"), None, O.is_equal), ("jrow", "qc"), ("cqx",))
     V(17, TT(T.dif[:], T.cqx[:, 1:18], T.cqx[:, 0:17], O.subtract), ("cqx",), ("dif",))
@@ -251,42 +275,72 @@ def rank_program(g, core, T, topo):
                               ("bA", T.bm[:], "bm", "qA"), ("bB", T.bm[:], "bm", "qB"), ("bn", T.bm[:], "bm", -8192.0), ("b256", T.bm[:], "bm", 256.0),
                               ("n256", T.bm[:], "bm", -256.0), ("hb", T.bm[:], "bm", 0.5), ("Wb", T.bm[:], "bm", "w")):
         V(64, TS(mat(name), src, col(a) if a in _COL else a, None, O.mult), (tok, a) if a in _COL else (tok,), (name + "m" if name in ("bA", "bB") else name,))
-    V(128, TS(T.b8[:], T.bm[:], 0.125, None, O.mult), ("bm",), ("b8",))
+    V(128, CP(T.b8[:], T.bm[:]), ("bm",), ("b8",))
     for l in range(1, 5):
         V(256, TT(T.hsd[:, (l - 1) * 128:l * 128], T.shm[:, (l - 1) * 128:l * 128],
                   T.idn[:] if l == 1 else T.shm[:, (l - 2) * 128:(l - 1) * 128], O.subtract),
           ("shm%d" % l, "idn" if l == 1 else "shm%d" % (l - 1)), ("hsd%d" % l,))
     V(256, TS(T.hsh[:], T.hsd[:], 0.5, None, O.mult), ("hsd1", "hsd2", "hsd3", "hsd4"), ("hsh",))
-    for n in sorted(set(OPT["na"].values()) | set(NB.values())):
+    for n in sorted({x for h in "AB" if not OPT["nf"][h] for x in (OPT["na"][h], NB[h])}):
         iota(T["mz%d" % n][:], [[0, 256], [256, n]], 0, 256 * n, ("mz%d" % n,))
-    iota(T.m6[:], [[0, 64], [4, 6]], 1, 384, ("m6",))
-    iota(T.k6[:], [[0, 64], [1, 6]], -64, 384, ("k6",))
+    iota(T.jj[:], [[1, 128]], 0, 128, ("jj",))
     iota(T.j16[:], [[0, 8], [1, 16]], 0, 128, ("j16",))
-    V(192, TS(T.Kq[:], T.k6[:], col("qc"), None, O.subtract), ("k6", "qc"), ("Kq",))
-    V(64, TS(T.Kq[:, 0::6], T.ones[:, 0:64], col("qc"), -1.0, O.mult, O.mult), ("ones", "qc"), ("Kq",))
+    digit = {k: 3.0 * 4 ** (5 - k) if k < 5 else 4.0 for k in range(1, 6)}
+    for k in digit:
+        S(128, ACT(mat("a%d" % k), T.idn[:], AF.Copy, scale=digit[k]), ("idn",), ("a%d" % k,))
+    V(64, MS(mat("kd"), (8 - 4148 - sum(digit[k] * (k - RR[TILE[k]][0]) for k in digit)) / 128), (), ("kd",))
+    for d in range(4):
+        aff(T.shd[:, 128 * d:128 * d + 128], T.bm[:], [[-1, 128]], O.is_equal, d + 1, 1, ("bm",), ("shd%d" % d,))
     V(64, TS(T.dg0[:], T.j16[:], col("qc"), 65.0 * 65536, O.is_equal, O.mult), ("j16", "qc"), ("dg0",))
     V(64, TS(T.dg[:], T.dg0[:], -65536.0, None, O.add), ("dg0",), ("dg",))
     for hi, h in enumerate("AB"):
         for q in WID:
             n = WID[q]
-            a, b = "da%d%s" % (q, h), "db%d%s" % (q, h)
+            a, bs = "da%d%s" % (q, h), tuple("db%d%s" % (k, h) for k in range(1, 6) if TILE[k] == q)
             if q == 1:
-                for x in (a, b):
+                for x in (a,) + bs:
                     V(n * 32, MS(T[x][:, 0:64 * n], 1.0), (), (x,))
             else:
-                dma("y", [(T[x][:, 0:64 * n], T.ones[:, 0:64 * n]) for x in (a, b)], ("ones", "onesw", "X"), (a, b), 3.0)
-            V(64, MS(T[b][:, 1:64 * n:n], 0.0), (), (b,))
+                dma("y", [(T[x][:, 0:64 * n], T.ones[:, 0:64 * n]) for x in (a,) + bs], ("ones", "onesw", "X"), (a,) + bs, 3.0)
+            for b in bs:
+                V(64, MS(T[b][:, 1:64 * n:n], 0.0), (), (b,))
             V(64, MS(T["T%d%s" % (q, h)][:, 0:64 * n:n], 0.0), (), ("T%dz%s" % (q, h),))
-        V(64, MS(T["AP" + h][:, 0::6], 0.0), (), ("AP0" + h,))
 
     def entry(k, h):
         q = TILE[k]
         n = WID[q]
-        V(n * 32, SCAN(T["mk" + h][:, 0:64 * n], T["da%d%s" % (q, h)][:, 0:64 * n], T["db%d%s" % (q, h)][:, 0:64 * n], O.add, O.min, 1.0),
-          ("da%d%s" % (q, h), "db%d%s" % (q, h)), ("mk" + h,))
+        V(n * 32, SCAN(T["mk" + h][:, 0:64 * n], T["da%d%s" % (q, h)][:, 0:64 * n], T["db%d%s" % (k, h)][:, 0:64 * n], O.add, O.min, 1.0),
+          ("da%d%s" % (q, h), "db%d%s" % (k, h)), ("mk" + h,))
         V(n * 32, SCAN(T["co" + h][:, 0:64 * n], T["mk" + h][:, 0:64 * n], T["T%d%s" % (q, h)][:, 0:64 * n], O.mult, O.add),
           ("mk" + h, "T%dz%s" % (q, h)) + tuple("T%d_%d%s" % (q, r, h) for r in RR[q]), ("co" + h,))
-        LIN(OPT["w8"], B("w8" + h), T["co" + h][:, n - 1:64 * n:n], 1.0 / 32, 0.25, ("co" + h,), ("w8" + h,))
+        if k < 5:
+            LIN(OPT["w8"], B("w8" + h), T["co" + h][:, n - 1:64 * n:n], 1.0 / 32, 0.25, ("co" + h,), ("w8" + h,))
+
+    def spans(n, a, b):
+        for d in range(4):
+            bk = "pEB" if n < 256 else ("pDB", "pEB")[d % 2]
+            ps = T[bk][:, 64 * d:64 * d + n] if n < 256 else T[bk][:, 0:n]
+            P(max(64, n), SUM(ps, [(T.shd[:, 128 * d:128 * d + 128], T.TB[:, a:a + n])]),
+              ("shd%d" % d,) + tuple("TB%d_%d" % (n, e) for e in range(4)), ("tp%d_%d" % (n, d),), (bk,))
+            if n == 256:
+                S(n, ACT(T.TB[:, b + n * d:b + n * d + n], ps, AF.Identity, bias=T.col[:, 44 + d:45 + d]), ("tp%d_%d" % (n, d), "diz"), ("TB%d_%d" % (4 * n, d),), (bk,))
+        for d in range(4 if n < 256 else 0):
+            V(64, TS(T.TB[:, b + n * d:b + n * d + n], T.pEB[:, 64 * d:64 * d + n], T.col[:, 40 + d:41 + d], None, O.add), ("tp%d_%d" % (n, d), "diz"),
+              ("TB%d_%d" % (4 * n, d),), ("pEB",))
+
+    V(4, TS(T.col[:, 40:44], T.jrow[:, 1:5], col("iz"), None, O.mult), ("jrow", "iz"), ("diz",))
+    V(4, TS(T.col[:, 44:48], T.col[:, 40:44], 1.0, None, O.add), ("diz",), ("diz",))
+    V(4, CP(T.TB[:, 0:4], T.col[:, 40:44]), ("diz",), tuple("TB4_%d" % e for e in range(4)))
+    V(4, MS(T.SP[:, 0:8], 0.0), (), ("SPz",))
+    V(44, MS(T.SP[:, 4104:4148], 0.0), (), ("SPz",))
+    for d in range(4):
+        V(64, TS(T.SP[:, 8 + 1024 * d:136 + 1024 * d], ones, T.col[:, 44 + d:45 + d], None, O.mult), ("ones", "diz"), ("SP",))
+    for c in (128, 512):
+        dma("y", [(T.SP[:, 8 + 1024 * d + c * j:8 + 1024 * d + c * j + c], T.SP[:, 8 + 1024 * d:8 + 1024 * d + c]) for d in range(4) for j in range(1, 512 // c + (c > 128))],
+            ("X",), ("SP",), 2.6)
+    spans(4, 0, 4)
+    spans(16, 4, 20)
+    spans(64, 20, 84)
 
     for t in range(3):
         last = t == 2
@@ -297,10 +351,9 @@ def rank_program(g, core, T, topo):
             bV = "pV" + h
             pV = T[bV]
             if t and h in OPT["fast"]:
-                V(64, TS(B("Q" + h), St[:, o:o + H2], T.acnt[:], None, O.add), ("st%d" % t, "acnt"), ("Q" + h,))
-                V(64, TS(B("s1" + h), B("Q" + h), 4095, None, O.bitwise_and), ("Q" + h,), ("s1" + h,))
+                V(64, TS(pV[:, 384:448], St[:, o:o + H2], T.acnt[:], None, O.add), ("st%d" % t, "acnt"), ("bs" + h,), (bV,))
                 V(64, TS(B("base" + h), L, 613.0, None, O.mult), (lt,), ("base" + h,))
-                V(128, TT(T["off" + h][:], B("base" + h), B("s1" + h), O.add), ("base" + h, "s1" + h), ("off" + h,))
+                V(64, TT(T["off" + h][:], B("base" + h), pV[:, 384:448], O.add), ("base" + h, "bs" + h), ("off" + h,), (bV,))
             else:
                 V(64, TS(B("base" + h), L, 613.0, None, O.mult), (lt,), ("base" + h,))
                 V(128, TT(pV[:, 384:448], B("base" + h), St[:, o:o + H2], O.add), ("base" + h, "st%d" % t), ("bs" + h,), (bV,))
@@ -309,12 +362,13 @@ def rank_program(g, core, T, topo):
                 V(64, CP(T["off" + h][:], B("s1" + h)), ("s1" + h,), ("off" + h,))
             P(64, SUM(pV[:, 0:64], [(rm(17), L)]), (lt, "Rm17"), ("Lb" + h,), (bV,))
             V(64, TS(B("e0" + h), pV[:, 0:64], col("q8"), col("iz"), O.is_equal, O.subtract), ("Lb" + h, "q8", "iz"), ("e0" + h,), (bV,))
-            V(64, CP(pV[:, 448:512], L), (lt,), ("L" + h,), (bV,))
             V(128, TT(B("t0" + h), B("e0" + h), C, O.mult), ("e0" + h, ct), ("t0" + h,))
             P(128, SUM(pV[:, 64:128], [(rm(17), C), (win(T.Ez, 0), B("t0" + h))]), (ct, "t0" + h, "Rm17", "Ez"), ("c80" + h,), (bV,))
-            LIN("v", B("w8" + h), pV[:, 64:128], 1.0 / 32, 0.125, ("c80" + h,), ("w8" + h,), (bV,))
-            LIN("v", B("c0" + h), pV[:, 64:128], 1.0, -4.0, ("c80" + h,), ("c0" + h,), (bV,))
+            LIN(OPT["c0"], B("w8" + h), pV[:, 64:128], 1.0 / 32, 0.125, ("c80" + h,), ("w8" + h,), (bV,))
+            LIN(OPT["c0"], B("c0" + h), pV[:, 64:128], 1.0, -4.0, ("c80" + h,), ("c0" + h,), (bV,))
             S(64, ACT(B("Kp" + h), L, AF.Exp, scale=16 * LN3, bias=col("kb")), (lt, "kb"), ("Kp" + h,))
+            S(64, ACT(pV[:, 448:512], L, AF.Copy), (lt,), ("L" + h,), (bV,))
+            S(64, ACT(T.SP[:, 4148 + o:4148 + o + H2], L, AF.Copy), (lt,), ("SP" + h,))
             for j0 in range(0, len(jobs), 8):
                 bk = ("pD" + h, "pE" + h)[j0 // 8 % 2]
                 rs = jobs[j0:j0 + 8]
@@ -326,12 +380,16 @@ def rank_program(g, core, T, topo):
                             n = WID[q]
                             out, e = T["T%d%s" % (q, h)][:, 1 + RR[q].index(r):64 * n:n], OPT["te"][h + str(q)]
                             src = [p_ for p_ in sorted(RR) if p_ < q and r in RR[p_]]
-                            if e == "g" and src:
+                            if e[0] == "g" and src:
                                 aff(out, T["T%d%s" % (src[0], h)][:, 1 + RR[src[0]].index(r):64 * WID[src[0]]:WID[src[0]]], [[0, 64]], O.is_equal, 0, 0,
                                     ("T%d_%d%s" % (src[0], r, h),), ("T%d_%d%s" % (q, r, h),), 64)
                             else:
-                                LIN("v" if e == "v" else "s", out, T[bk][:, 64 * j:64 * j + 64], 1.0, -4.0 if r > 16 else 0.0, ("dM" + bk,),
+                                LIN("v" if e[-1] == "v" else "s", out, T[bk][:, 64 * j:64 * j + 64], 1.0, -4.0 if r > 16 else 0.0, ("dM" + bk,),
                                     ("T%d_%d%s" % (q, r, h),), (bk,))
+        if t == 0:
+            spans(256, 84, 344)
+            dma("y", [(T.SP[16 * a + d + 1:16 * a + 16, 8 + 1024 * d:1032 + 1024 * d], T.TB[16 * a:16 * a + 15 - d, 344:1368]) for d in range(4) for a in range(8)],
+                tuple("TB1024_%d" % e for e in range(4)), ("SP",), 4.0)
         if last:
             for hi, h in enumerate("AB"):
                 pE, prev = T["pE" + h], ()
@@ -344,46 +402,69 @@ def rank_program(g, core, T, topo):
                 bU, bV = "pU" + h, "pV" + h
                 pV = T[bV]
                 z, zr, zs = slot(h, k)
+                z0 = zs if zr == 1 else 0
                 wide = k > 0 or (t and h in OPT["fast"])
                 nv = OPT["gv"].get((k, h), 0)
                 zk = ()
-                for q, a, b in (("s", 0, 64 - nv), ("v", 64 - nv, 64)):
+                parts = [("s", 0, 64 - nv), ("v", 64 - nv, 64)]
+                if OPT["gs"]:
+                    parts = [("s", 0, 32), ("s", 32, 64 - nv), ("v", 64 - nv, 64)]
+                if k == 5 and h in OPT["c5"]:
+                    parts = [("s", a, a + 16) for a in range(0, 64, 16)]
+                for q, a, b in parts:
                     if a < b:
-                        zk += ("z%d%s%s" % (k, q, h),)
-                        gather(q, z[:, 16 * zr * a + zs:16 * zr * b:zr], T.X[:, 0:8192 if wide else 4096], T["off" + h][:, a:b], 16 * (b - a),
+                        zk += ("z%d_%d_%d%s" % (k, a, b, h),)
+                        gather(q, z[:, 16 * zr * a + zs:16 * zr * b + z0:zr], T.X[:, 0:8192 if wide else 4096], T["off" + h][:, a:b], 16 * (b - a),
                                ("X", "off" + h) + (("X2",) if wide else ()), zk[-1:])
-                y, by = (T[bU][:, 0:64], bU) if k < 5 else (pV[:, 320:384], bV)
+                y, by = T[bU][:, 0:64], bU
                 k0 = P(128, [MM(y, mat("kc"), T.ones[:, 0:64], True, False), MM(y, mat("ke"), T.ones[:, 0:64], False, False)],
                        ("kc0", "kc1", "ke", "ones"), ("u0" + h,), (by,))
-                P(1024, [MM(y, win(T.Wz, m), z[:, zr * m + zs:1024 * zr:16 * zr], False, m == 15) for m in range(16)], zk + ("Wz",), ("u" + h,), (by,), after=(k0,))
+                P(1024, [MM(y, win(T.Wz, m), z[:, zr * m + zs:1024 * zr + z0:16 * zr], False, m == 15) for m in range(16)], zk + ("Wz",), ("u" + h,), (by,), after=(k0,))
                 ut = ("u0" + h, "u" + h)
                 na, nb = OPT["na"][h], NB[h]
-                if k == na - 1 and k < 5:
+                if k == OPT["nf"][h] - 1:
+                    zt = tuple(x for x in lastw if x[0] == "z" and x[-1] == h and int(x[1]) <= k)
+                    rid, pid = topo.addr(helper[core])[:2]
+                    tr = RemoteDMATransfer(dst_ids=[DstId(rid=rid, pnc=pid)], dma_engine_mask=topo.mask(core, helper[core]), remote_sem=T.sem["fa%d%s" % (t, h)],
+                                           srcs=[z[:, 1024 * j:1024 * j + 1024] for j in range(k + 1)], dsts=[T["Y" + h][:, 1024 * t:1024 * t + 1024]], alu_op=2)
+                    kf = add("g", 0.8, [lambda tr=tr, s_=T.sem["fl%d%s" % (t, h)]: g.remote_dma_fused([tr], local_sem=s_)], zt, (), sem=("loc", None))
+                    add("r", 2.0, [], zt, (), sem=("fl%d%s" % (t, h), NH), extra=(kf,))
+                    add("r", OPT["fold"], [], (), ("M%d%s" % (t, h),), sem=("fb%d%s" % (t, h), NH), extra=(kf,))
+                if k == na - 1 and k < 5 and not OPT["nf"][h]:
                     zt = tuple(x for x in lastw if x[0] == "z" and x[-1] == h and int(x[1]) < na)
                     c = 1024 // OPT["chunks"] * na
                     for j in range(OPT["chunks"]):
                         V(c // 2, SCAN(T["Y" + h][:, c * nb * j:c * nb * (j + 1):nb], T["mz%d" % na][:, 0:c], T["z" + h][:, c * j:c * (j + 1)],
                                        O.min, O.max), zt + ("mz%d" % na,), ("Y%d%s" % (j, h),))
-                if k == 5:
-                    continue
-                V(64, TT(B("ab" + h, 0, 64), y, B("w8" + h), O.mult), ut + ("w8" + h,), ("a0" + h,), (bU,))
-                V(64, TS(B("ab" + h, 64, 128), y, 37.0, -149.0 - 37.0 / 512, O.mult, O.add), ut, ("b0" + h,), (bU,))
-                V(128, TS(B("am" + h), B("ab" + h), 4095, None, O.bitwise_and), ("a0" + h, "b0" + h), ("am" + h,))
-                V(128, TT(T["off" + h][:], B("am" + h, 0, 64), B("am" + h, 64, 128), O.add), ("am" + h,), ("off" + h,))
+                if k < 5:
+                    V(64, TT(B("ab" + h, 0, 64), y, B("w8" + h), O.mult), ut + ("w8" + h,), ("a0" + h,), (bU,))
+                    V(64, TS(B("ab" + h, 64, 128), y, 37.0, -149.0 - 37.0 / 512, O.mult, O.add), ut, ("b0" + h,), (bU,))
+                    V(128, TS(B("am" + h), B("ab" + h), 4095, None, O.bitwise_and), ("a0" + h, "b0" + h), ("am" + h,))
+                    V(128, TT(T["off" + h][:], B("am" + h, 0, 64), B("am" + h, 64, 128), O.add), ("am" + h,), ("off" + h,))
                 n = WID.get(TILE[k], 1)
                 V(64, TT(B("k8" + h), y, T["co" + h][:, n - 1:64 * n:n] if k else B("c0" + h), O.add), ut + ("co" + h if k else "c0" + h,), ("k8" + h,), (bU,))
                 V(64, TS(B("n1" + h), B("k8" + h), 3, 3, O.arith_shift_right, O.bitwise_and), ("k8" + h,), ("n1" + h,))
                 Pk, pt = pV[:, 64 * k:64 * k + 64], "P%d%s" % (k + 1, h)
                 if k == 0:
                     V(64, TS(Pk, B("n1" + h), 64.0, None, O.add), ("n1" + h,), (pt,), (bV,))
-                else:
+                elif k < 5:
                     V(64, TT(Pk, B("n1" + h), pV[:, 64 * k - 64:64 * k], O.add), ("n1" + h, "P%d%s" % (k, h)), (pt,), (bV,))
-                if k < 4:
+                else:
+                    P(448, SUM(pV[:, 384:448], [(mat("kd"), T.ones[:, 0:64]), (mat("nid"), T.jj[:, 64 * hi:64 * hi + 64])]
+                               + [(mat("a%d" % j), T["db%d%s" % (j, h)][:, 0:64 * WID[TILE[j]]:WID[TILE[j]]]) for j in range(1, 6)]),
+                      ("kd", "nid", "jj", "ones") + tuple("a%d" % j for j in range(1, 6)) + tuple("db%d%s" % (j, h) for j in range(1, 6)), ("cod" + h,), (bV,))
+                    if h in OPT["cmpv"]:
+                        P(64, SUM(pV[:, 320:384], [(T.idn[:], T["F" + h][:, 0:64])]), ("F" + h, "idn"), ("Fp" + h,), (bV,))
+                    V(64, TT(pV[:, 384:448], B("n1" + h), pV[:, 384:448], O.add), ("n1" + h, "cod" + h), ("code" + h,), (bV,))
+                if k < 5:
                     q = TILE[k + 1]
-                    n2, da, db = WID[q], "da%d%s" % (q, h), "db%d%s" % (q, h)
-                    V(64, TS(B("b" + h), Pk, qk(k + 1), None, O.is_ge), (pt, "qk"), ("b" + h,), (bV,))
-                    V(64, TT(T[da][:, 1:64 * n2:n2], B("b" + h), pV[:, 448:512], O.mult), ("b" + h, "L" + h), (da,), (bV,))
+                    n2, da, db = WID[q], "da%d%s" % (q, h), "db%d%s" % (k + 1, h)
+                    if OPT["b"] == "s":
+                        S(64, ACT(B("b" + h), Pk, AF.Relu, scale=4.0, bias=T.col[:, 32 + k + 1:33 + k + 1]), (pt, "qk4"), ("b" + h,), (bV,))
+                    else:
+                        V(64, TS(B("b" + h), Pk, qk(k + 1), 4.0, O.is_ge, O.mult), (pt, "qk"), ("b" + h,), (bV,))
                     LIN(OPT["db"], T[db][:, 0:64 * n2:n2], Pk, 1.0, float(k + 1 - 64 - RR[q][0]), (pt,), (db,), (bV,))
+                    V(64, TT(T[da][:, 1:64 * n2:n2], B("b" + h), pV[:, 448:512], O.min), ("b" + h, "L" + h), (da,), (bV,))
                     entry(k + 1, h)
         for hi, h in enumerate("AB"):
             o = H2 * hi
@@ -393,14 +474,32 @@ def rank_program(g, core, T, topo):
             sL, sC = "s%dL%s" % (t, h), "s%dC%s" % (t, h)
             acc, F, VS = B("acc" + h), T["F" + h][:, 0:64], T["VS" + h]
             na, nb = OPT["na"][h], NB[h]
-            zt = tuple(x for x in lastw if x[0] == "z" and x[-1] == h and (na == 6 or int(x[1]) >= na))
+            zt = tuple(x for x in lastw if x[0] == "z" and x[-1] == h and int(x[1]) >= (OPT["nf"][h] or na))
+            zall = zt
+            nf = OPT["nf"][h]
+            for c, bk in enumerate((bD, bE) if nf else ()):
+                P(512, SUM(T[bk][:], [(T.idn[:], T["Y" + h][:, 4096 + 1024 * t + 512 * c:4608 + 1024 * t + 512 * c])]), ("M%d%s" % (t, h), "idn"), ("Mp" + bk,), (bk,))
+                for k in range(nf, 5):
+                    V(512, TT(T[bk][:], T["Y" + h][:, 1024 * (k - nf) + 512 * c:1024 * (k - nf) + 512 * c + 512], T[bk][:], O.max),
+                      tuple(x for x in zall if int(x[1]) == k) + ("Mp" + bk,), ("Mp" + bk,), (bk,))
             for j in range(4):
+                zt = tuple(x for x in zall if int(x[:-1].split("_")[1]) < 16 * j + 16 and int(x[:-1].split("_")[2]) > 16 * j)
+                if nf:
+                    bk = (bD, bE)[j // 2]
+                    V(256, TT(VS[:, 256 * j:256 * j + 256], T["Y" + h][:, 1024 * (5 - nf) + 256 * j:1024 * (5 - nf) + 256 * j + 256],
+                              T[bk][:, 256 * (j % 2):256 * (j % 2) + 256], O.max), zt + ("Mp" + bk,), ("VS%d%s" % (j, h),), (bk,))
+                    continue
                 src = T["z" + h][:, 1536 * j:1536 * (j + 1)] if na == 6 else T["Y" + h][:, 256 * na * nb * j + (na - 1) * nb % na:256 * na * nb * (j + 1):na]
                 V(128 * nb, SCAN(VS[:, 256 * nb * j:256 * nb * (j + 1)], T["mz%d" % nb][:], src, O.min, O.max),
                   zt + ("mz%d" % nb,) + (() if na == 6 else tuple("Y%d%s" % (i, h) for i in range(OPT["chunks"] // 4 * j, OPT["chunks"] // 4 * (j + 1)))), ("VS%d%s" % (j, h),))
             vt = tuple("VS%d%s" % (j, h) for j in range(4))
             for c, bk in enumerate((bD, bE)):
                 ps = T[bk]
+                if h in OPT["cmpv"]:
+                    for m in range(8 * c, 8 * c + 8):
+                        V(64, TT(T["ind" + h][:, 64 * m:64 * m + 64], VS[:, nb * m + nb - 1:1024 * nb:16 * nb], pV[:, 320:384], O.is_ge), vt + ("Fp" + h,),
+                          ("ind%d_%d%s" % (c, m, h),), (bV,))
+                    continue
                 k0 = P(512, [MM(ps[:], mat("nid"), T["F" + h][:], True, False)], ("F" + h, "Fr" + h, "nid"), ("VF" + bk,), (bk,))
                 P(512, [MM(ps[:, 64 * j:64 * j + 64], T.idn[:], VS[:, nb * (8 * c + j) + nb - 1:1024 * nb:16 * nb], False, j == 7) for j in range(8)], vt + ("idn",),
                   ("VG" + bk,), (bk,), after=(k0,))
@@ -408,12 +507,11 @@ def rank_program(g, core, T, topo):
             prev = ()
             for c in range(2):
                 prev = (P(512, [MM(pD[:, 0:64], win(T.Ez, m), T["ind" + h][:, 64 * m:64 * m + 64], m == 0, m == 15) for m in range(8 * c, 8 * c + 8)],
-                          ("ind%d%s" % (c, h), "Ez"), ("cnt%d%s" % (c, h),), (bD,), after=prev),)
-            V(64, TS(B("f" + h), pD[:, 0:64], 8.0, None, O.is_ge), ("cnt0" + h, "cnt1" + h), ("f" + h,), (bD,))
-            V(128, TT(B("E" + h), B("f" + h), B("Kp" + h), O.mult), ("f" + h, "Kp" + h), ("E" + h,))
+                          ("ind%d%s" % (c, h), "Ez") + tuple("ind%d_%d%s" % (c, m, h) for m in range(16)), ("cnt%d%s" % (c, h),), (bD,), after=prev),)
+            V(64, TS(pD[:, 0:64], pD[:, 0:64], 68.0 if h in OPT["cmpv"] else 8.0, None, O.is_ge), ("cnt0" + h, "cnt1" + h), ("f" + h,), (bD,))
+            V(64, TT(B("E" + h), pD[:, 0:64], B("Kp" + h), O.mult), ("f" + h, "Kp" + h), ("E" + h,), (bD,))
             P(64, SUM(pD[:, 64:128], [(mat("hb"), B("E" + h))]), ("E" + h, "hb"), ("Es" + h,), (bD,))
             V(64, TT(acc, B("E" + h), pD[:, 64:128], O.is_gt), ("E" + h, "Es" + h), ("acc" + h,), (bD,))
-            V(64, TT(B("keep" + h), L, pD[:, 64:128], O.subtract), (lt, "Es" + h), ("keep" + h,), (bD,))
             segs = [mat("b" + h)] + ([] if last else [mat("bn")])
             ns = 64 * len(segs)
             P(ns, [MM(pD[:, 128 + 64 * j:192 + 64 * j], m_, acc, True, True) for j, m_ in enumerate(segs)], ("acc" + h, "b" + h + "m", "bn"), ("sg" + h,), (bD,))
@@ -429,7 +527,7 @@ def rank_program(g, core, T, topo):
             V(4, TT(T["toff" + h][:], B("h1" + h), T.Kt[:, 8 + 4 * hi:12 + 4 * hi] if last else B("tb" + h), O.add), ("h1" + h, "tb" + h, "Kl" + h), ("toff" + h,))
             if not last:
                 for a, x in ((0, "X"), (4096, "X2")):
-                    add("v", 0.25, [lambda f_=T["toff" + h], i_=B("Vsel" + h), a_=a: g.vector.tensor_copy(T.X[:, a_:a_ + 12288].indirect(f_[:, 0:4]), i_)],
+                    add("v", (0.05, 240, 0), [lambda f_=T["toff" + h], i_=B("Vsel" + h), a_=a: g.vector.tensor_copy(T.X[:, a_:a_ + 12288].indirect(f_[:, 0:4]), i_)],
                         ("toff" + h, "Vsel" + h), (x, "Xw"))
             else:
                 gather("v", B("xo" + h), T.X[:, 0:4096], T["toff" + h][:, 0:4], 64, ("X", "toff" + h), ("xo" + h,))
@@ -439,7 +537,7 @@ def rank_program(g, core, T, topo):
                 dma("s", [(T.ys[:, o:o + H2], B("yss" + h))], ("yss" + h,), ())
             P(256, [MM(pE[:, 64 * l:64 * l + 64], T.hsh[:, 128 * l:128 * l + 128], C, True, True) for l in range(4)], (ct, "hsh"), ("SH" + h,), (bE,))
             V(64, TT(B("aL" + h), acc, pV[:, 448:512], O.mult), ("acc" + h, "L" + h), ("aL" + h,), (bV,))
-            V(64, TT(B("ay" + h), acc, pV[:, 320:384], O.mult), ("acc" + h, "u0" + h, "u" + h), ("ay" + h,), (bV,))
+            V(64, TT(B("ay" + h), acc, pV[:, 384:448], O.mult), ("acc" + h, "code" + h), ("ay" + h,), (bV,))
             P(64, SUM(pE[:, 256:320], [(T.tri[:], B("aL" + h))]), ("aL" + h, "tri"), ("sh" + h,), (bE,))
             for l in range(1, 5):
                 S(64, ACT(T["ES" + h][:, 64 * l - 64:64 * l], pE[:, 256:320], AF.Sign, bias=half(l)), ("sh" + h, "half"), ("ES%d%s" % (l, h),), (bE,))
@@ -451,26 +549,10 @@ def rank_program(g, core, T, topo):
                 send(T["C%d" % (t + 1)][:, o:o + H2], T[sC][:], "arr%dC%s" % (t + 1, h), 1, (sC,), ("C%d%s" % (t + 1, h),))
             else:
                 dma("y", [(T.yc[:, o:o + H2], T[sC][:])], (sC,), ())
-            AP = T["AP" + h]
-            k0 = P(384, [MM(pU[:, 64:448], T.idn[:], T.Kq[:], True, False)], ("idn", "Kq"), ("Pd0" + h,), (bU,))
-            for k in range(1, 6):
-                V(64, TT(AP[:, k::6], acc, pV[:, 64 * k - 64:64 * k], O.mult), ("acc" + h, "P%d%s" % (k, h)), ("AP%d%s" % (k, h),), (bV,))
-            P(384, [MM(pU[:, 64:448], T.bm[:], AP[:], False, True)], tuple("AP%d%s" % (k, h) for k in range(6)) + ("bm",), ("Pd" + h,), (bU,), after=(k0,))
-            k1 = P(384, [MM(pV[:, 384:448], l_, r_, j == 0, False) for j, (l_, r_) in enumerate([(T.b8[:], B("ay" + h))] + new[:2])],
-                   ("ay" + h, "b8", "hid", "hs4", ct), ("k5a" + h,), (bV,))
-            P(256, [MM(pV[:, 384:448], l_, r_, False, j == 3) for j, (l_, r_) in enumerate(new[2:])], ("EC" + h, "idn"), ("k5b" + h,), (bV,), after=(k1,))
-            if h in OPT["eqs"]:
-                S(384, ACT(T["SQ" + h][:], pU[:, 64:448], AF.Square), ("Pd0" + h, "Pd" + h), ("SQ" + h,), (bU,))
-                S(384, ACT(T["EQ" + h][:], T["SQ" + h][:], AF.Relu, scale=-1.0, bias=T.col[:, 30:31]), ("SQ" + h, "onec"), ("EQ" + h,))
-            else:
-                V(384, TS(T["EQ" + h][:], pU[:, 64:448], 0.0, None, O.is_equal), ("Pd0" + h, "Pd" + h), ("EQ" + h,), (bU,))
-            V(384, TT(T["EN" + h][:, 0:383], T["EQ" + h][:, 0:383], pU[:, 65:448], O.mult), ("EQ" + h, "Pd0" + h, "Pd" + h), ("EN" + h,), (bU,))
-            V(192, SCAN(T["LS" + h][:, 0:383], T.m6[:, 0:383], T["EN" + h][:, 0:383], O.min, O.max, 1.0), ("EN" + h, "m6"), ("LS" + h,))
-            V(128, TT(pU[:, 0:64], T["LS" + h][:, 4::6], B("keep" + h), O.max), ("LS" + h, "keep" + h), ("Lm" + h,), (bU,))
-            V(64, TS(B("k5" + h), pV[:, 384:448], -0.9375, None, O.add), ("k5a" + h, "k5b" + h), ("k5" + h,), (bV,))
-            V(64, TS(B("n5" + h), B("k5" + h), 3, None, O.bitwise_and), ("k5" + h,), ("n5" + h,))
-            V(128, TT(B("e5" + h), B("n5" + h), T["EQ" + h][:, 5::6], O.mult), ("n5" + h, "EQ" + h), ("e5" + h,))
-            V(64, TT(T[sL][:], B("e5" + h), pU[:, 0:64], O.add), ("e5" + h, "Lm" + h), (sL,), (bU,))
+            P(256, SUM(pU[:, 0:64], [(T.b8[:], B("ay" + h))]), ("ay" + h, "b8"), ("cb" + h,), (bU,))
+            V(64, SCAN(B("wc" + h), T.dg[:, 0:64], pU[:, 0:64], O.add, O.min), ("cb" + h, "dg"), ("wc" + h,), (bU,))
+            V(4, TT(T["loff" + h][:], B("wc" + h, 15, 64, 16), T.Kv[:, 8 + 4 * hi:12 + 4 * hi], O.add), ("wc" + h, "Ks" + h), ("loff" + h,))
+            gather(OPT["lg"], T[sL][:], T.SP[:], T["loff" + h][:], 64, ("loff" + h, "SPA", "SPB", "SPz", "SP"), (sL,))
             if not last:
                 send(T["L%d" % (t + 1)][:, o:o + H2], T[sL][:], "arr%dL%s" % (t + 1, h), 1, (sL,), ("L%d%s" % (t + 1, h),))
             else:
@@ -490,35 +572,66 @@ def rank_program(g, core, T, topo):
                 S(64, ACT(T.junk[:], T.pUA[:, 0:64], AF.Copy, accum_out=T.acnt[:]), ("As",), ("acnt", "junk"), ("pUA",))
 
     n = len(ops)
-    succ = [[] for _ in range(n)]
+    succ, above = [[] for _ in range(n)], []
     for k, p in enumerate(ops):
+        far = 0
+        for d in p["all"]:
+            far |= above[d]
+        p["all"] = {d for d in p["all"] if not far >> d & 1}
+        above.append(far | sum(1 << d for d in p["all"]))
         for d in p["all"]:
             succ[d].append(k)
 
     def gap(a, b):
         a, b = min(a, b), max(a, b)
         return 0.0 if a not in ops[b]["deps"] else OPT["ws"] if ops[a]["q"] == ops[b]["q"] else OPT["wx"]
-    cost = [p["cost"] for p in ops]
-    hold = [0.0 if p["q"] == "r" else 0.06 * len(p["fns"]) if p["sem"] is not None and p["q"] in "sy" else p["cost"] for p in ops]
+    queue = [p["q"] for p in ops]
+
+    def times(f, gr):
+        c = [p["cost"][0] + 0.00083 * f * (p["cost"][1] + gr * p["cost"][2]) if isinstance(p["cost"], tuple) else p["cost"] for p in ops]
+        return c, [0.0 if p["q"] == "r" else 0.06 * len(p["fns"]) if p["sem"] is not None and p["q"] in "sy" else c[k] for k, p in enumerate(ops)]
+    cost, hold = times(OPT["f"], OPT["gr"])
+    paces = [times(f, gr) + (1.0 / (f + 0.25 * gr),) for f, gr in OPT["paces"]]
+
+    def replay(at):
+        seq, total = sorted(range(n), key=lambda k: at[k]), 0.0
+        for c, h, w in paces:
+            end, free = [0.0] * n, dict.fromkeys("vstgyr", 0.0)
+            for k in seq:
+                s0 = free[queue[k]] if h[k] else 0.0
+                for d, x in pred[k]:
+                    if end[d] + x > s0:
+                        s0 = end[d] + x
+                if h[k]:
+                    free[queue[k]] = s0 + h[k]
+                end[k] = s0 + c[k]
+            total += w * max(end)
+        return total
     pred = [[(d, gap(d, k)) for d in sorted(p["all"])] for k, p in enumerate(ops)]
     next_ = [[(d, gap(d, k)) for d in succ[k]] for k in range(n)]
 
     def place(seq, before, back):
-        at, taken = [0.0] * n, {}
+        at, end = [0.0] * n, [0.0] * n
+        first, after = {q: [] for q in "vstgyr"}, {q: [] for q in "vstgyr"}
         for k in seq:
-            lead = cost[k] - hold[k] if back else 0.0
-            s0 = max([at[d] + (hold[d] if back else cost[d]) + w for d, w in before[k]], default=0.0) + lead
-            line = taken.setdefault(ops[k]["q"], [])
-            lo, hi_ = 0, len(line)
-            while lo < hi_:
-                mid = (lo + hi_) // 2
-                lo, hi_ = (mid + 1, hi_) if line[mid][1] <= s0 else (lo, mid)
-            while lo < len(line) and line[lo][0] < s0 + hold[k] - 1e-9:
-                s0 = max(s0, line[lo][1])
-                lo += 1
-            if hold[k]:
-                line.insert(lo, (s0, s0 + hold[k]))
+            s0, h = 0.0, hold[k]
+            for d, w in before[k]:
+                if end[d] + w > s0:
+                    s0 = end[d] + w
+            if back:
+                s0 += cost[k] - h
+            if h:
+                a, b = first[queue[k]], after[queue[k]]
+                j = m = len(a)
+                while j and b[j - 1] > s0:
+                    j -= 1
+                while j < m and a[j] < s0 + h - 1e-9:
+                    s0 = b[j]
+                    j += 1
+                a.insert(j, s0)
+                b.insert(j, s0 + h)
             at[k] = s0
+            end[k] = s0 + (h if back else cost[k])
         return at
 
     prio = [0.0] * n
@@ -529,17 +642,21 @@ def rank_program(g, core, T, topo):
         at = place(seq, pred, False)
         back = place(sorted(range(n), key=lambda k: (-(at[k] + cost[k]), -k)), next_, True)
         at = place(sorted(range(n), key=lambda k: (-(back[k] + hold[k]), k)), pred, False)
-        return max(at[k] + cost[k] for k in range(n)), at
+        span = max(at[k] + cost[k] for k in range(n))
+        return span, at, span / (OPT["f"] + 0.25 * OPT["gr"]) + replay(at)
 
     if n not in PLAN:
         best = tighten(sorted(range(n), key=lambda k: -prio[k]))
         rng = np.random.RandomState(OPT["seed"])
         for _ in range(OPT["tries"]):
-            mid, wide, key = rng.uniform(0, best[0]), rng.uniform(2, 12), rng.normal(0, 0.6, n).tolist()
+            mid, wide, at = rng.uniform(0, best[0]), rng.uniform(2, 12), np.array(best[1])
+            key = (at + rng.normal(0, OPT["shake"], n) * (np.abs(at - mid) < wide)).tolist()
             for k in range(n):
-                key[k] = max([best[1][k] + (key[k] if abs(best[1][k] - mid) < wide else 0.0)] + [key[d] + 1e-6 for d, _w in pred[k]])
+                for d, _w in pred[k]:
+                    if key[d] >= key[k]:
+                        key[k] = key[d] + 1e-6
             other = tighten(sorted(range(n), key=lambda k: key[k]))
-            if other[0] <= best[0]:
+            if other[2] <= best[2]:
                 best = other
         if "hook" in OPT:
             best = OPT["hook"](ops, place, pred, next_, cost, hold, best)

@@ -4,8 +4,8 @@ from concourse.bass import DstId, RemoteDMATransfer
 from concourse.mybir import AluOpType as O, ActivationFunctionType as AF
 
 H2 = 64
-OPT = {"tiles": 3, "te": {"A1": "s", "A2": "g", "A3": "g", "B1": "v", "B2": "g", "B3": "g"}, "na": {"A": 3, "B": 4}, "fast": "B", "gv": {}, "eqs": "", "w8": "v", "db": "v",
-       "nf": {"A": 0, "B": 0}, "fold": 6.0, "lg": "s", "b": "v", "gs": 0, "x2": "v", "c0": "v", "c5": "AB", "cmpv": "B", "ws": 0.22, "wx": 0.22, "f": 1.15, "gr": 1.7, "paces": ((1.0, 1.56), (1.35, 2.08), (1.4, 1.25)), "tries": 5000, "shake": 0.6, "seed": 0, "chunks": 16}
+OPT = {"tiles": 3, "te": {"A1": "s", "A2": "g", "A3": "g", "B1": "s", "B2": "g", "B3": "g"}, "na": {"A": 3, "B": 4}, "fast": "B", "gv": {(k, h): (24, 16, 16)[k] for k in range(3) for h in "AB"}, "eqs": "", "w8": "v", "db": "v",
+       "nf": {"A": 3, "B": 3}, "fold": 8.5, "mg": "AB", "um": 4, "issue": 0.7, "fly": 1.6, "hp": "", "lg": "s", "b": "v", "gs": 0, "x2": "v", "c0": "s", "c5": "AB", "cmpv": "B", "ws": 0.22, "wx": 0.22, "f": 1.15, "gr": 1.7, "paces": ((1.0, 1.56), (1.35, 2.08), (1.4, 1.25)), "tries": 5000, "shake": 0.6, "slack": 0.0, "kin": 0.3, "far": 1.5, "seed": 0, "chunks": 16}
 PLAN = {}
 TILES = {3: ((0, 1, 2, 3, 3, 3), {1: (8, 1), 2: (12, 2), 3: (16, 3)})}
 SCRATCH = {}
@@ -13,8 +13,8 @@ SEMAPHORES = ["sv", "ss", "st_", "sg", "loc", "arst1", "arst2"] + ["arr%d%s%s" %
 SEMAPHORES += ["d%d" % k for k in range(40)] + ["f%s%d%s" % (x, t, h) for x in "abl" for t in range(3) for h in "AB"]
 _BF, _F32, _I32, _U16 = "bfloat16", "float32", "int32", "uint16"
 _COL = ("qc", "q8", "iz", "kb", "qA", "qB", "c0", "c1", "c2", "c3", "c4", "c5", "w", "one", "c6", "c7")
-_MAT = ("nid", "hid", "hs4", "kc", "ke", "kq", "bA", "bB", "bn", "b256", "n256", "hb", "Wb", "kd", "a1", "a2", "a3", "a4", "a5")
-for _n, _c, _d in (("X", 16384, _BF), ("C0", 128, _BF), ("C1", 128, _BF), ("C2", 128, _BF), ("L0", 128, _BF), ("L1", 128, _BF), ("L2", 128, _BF),
+_MAT = ("nid", "hid", "hs4", "kc", "ke", "kq", "bA", "bB", "bn", "b256", "n256", "hb", "Wb", "kd", "a1", "a2", "a3", "a4", "a5", "k-3", "k1", "q1", "q2", "q3")
+for _n, _c, _d in (("X", 16384, _BF), ("C0", 128, _BF), ("C1", 128, _BF), ("C2", 128, _BF), ("L0", 128, _BF), ("L1", 128, _F32), ("L2", 128, _F32),
                    ("wts", 1, _BF), ("st0", 128, _I32), ("st1", 128, _I32), ("st2", 128, _I32), ("pI", 1, _I32), ("aI", 1, _I32),
                    ("col", 64, _F32), ("jrow", 18, _F32), ("cqx", 18, _F32), ("dif", 17, _F32), ("dif8", 21, _F32), ("il0", 4, _F32), ("il", 4, _F32),
                    ("Kv", 16, _F32), ("Kt", 16, _F32), ("acnt", 1, _F32), ("junk", 64, _BF), ("b8", 128, _F32),
@@ -26,7 +26,7 @@ for _n, _c, _d in (("X", 16384, _BF), ("C0", 128, _BF), ("C1", 128, _BF), ("C2",
 _PACK = {}
 _SMALL = {_BF: (("b", 64), ("Kp", 64), ("f", 64), ("E", 64), ("acc", 64), ("aL", 64), ("e0", 64), ("t0", 64), ("Vsel", 64), ("xo", 64),
                 ("fr", 64), ("yfs", 64), ("w8", 64), ("c0", 64), ("e5", 64), ("keep", 64)),
-          _F32: (("base", 64), ("wr", 128), ("tb", 4), ("S0", 64), ("xd", 64), ("xe", 64), ("yss", 64), ("ay", 64), ("wc", 64)),
+          _F32: (("base", 64), ("wr", 128), ("tb", 4), ("S0", 64), ("xd", 64), ("xe", 64), ("yss", 64), ("ay", 64), ("wc", 64), ("ah", 64)),
           _I32: (("ab", 128), ("am", 128), ("k8", 64), ("Q", 64), ("s1", 64), ("n1", 64), ("hw", 64), ("h1", 4), ("k5", 64), ("n5", 64))}
 for _h in "AB":
     for _d, _names in _SMALL.items():
@@ -42,7 +42,7 @@ for _h in "AB":
         SCRATCH[_n + _h] = ("sbuf", [128, _c], _d)
     for _x in "LC":
         for _t in (0, 1, 2):
-            SCRATCH["s%d%s%s" % (_t, _x, _h)] = ("sbuf", [128, 64], _BF)
+            SCRATCH["s%d%s%s" % (_t, _x, _h)] = ("sbuf", [128, 64], _F32 if _x == "L" and _t < 2 else _BF)
     for _n in ("pU", "pV", "pD", "pE"):
         SCRATCH[_n + _h] = ("psum", [128, 512], _F32)
 
@@ -87,7 +87,7 @@ def rank_program(g, core, T, topo):
         return T.col[:, j:j + 1]
 
     def qk(k):
-        return T.col[:, 16 + k:17 + k]
+        return T.col[:, 16 + TILE[k]:17 + TILE[k]]
 
     def half(l):
         return T.col[:, 24 + l:25 + l]
@@ -102,12 +102,12 @@ def rank_program(g, core, T, topo):
     def win(Z, m):
         return Z[:, 15 - m:143 - m]
 
-    NB = {h: 1 if OPT["nf"][h] else 7 - a for h, a in OPT["na"].items()}
+    NB = {h: 7 - (OPT["nf"][h] or a) for h, a in OPT["na"].items()}
 
     def slot(h, k):
         a, b = OPT["na"][h], NB[h]
         if OPT["nf"][h]:
-            return (T["z" + h], 1, 1024 * k) if k < OPT["nf"][h] else (T["Y" + h], 1, 1024 * (k - OPT["nf"][h]))
+            return (T["z" + h], 1, 1024 * k) if k < OPT["nf"][h] else (T["Y" + h], b, 1 + k - OPT["nf"][h])
         if k < a:
             return T["z" + h], a, k
         v = (a - 1) * b
@@ -198,8 +198,8 @@ def rank_program(g, core, T, topo):
         rid, pid = topo.addr(dst)[:2]
         lanes = sum(1 << e for e in topo.engines(core, dst)[:NE])
         loc[0] += NE
-        k = add("g", 0.8, [lambda: g.remote_dma(out, in_, T.sem[sem], T.sem.loc, pid, rid, lanes)], r, (), sem=("loc", None))
-        return add("r", 2.0, [], (), w, sem=(sem, NE), extra=(k,))
+        k = add("g", OPT["issue"], [lambda: g.remote_dma(out, in_, T.sem[sem], T.sem.loc, pid, rid, lanes)], r, (), sem=("loc", None))
+        return add("r", OPT["fly"], [], (), w, sem=(sem, NE), extra=(k,))
 
     def spread(h):
         if h not in OPT["cmpv"]:
@@ -230,11 +230,13 @@ def rank_program(g, core, T, topo):
     V(1, CP(col("qc"), T.aI[:]), ("aI",), ("qc",))
     for name, a, b in (("q8", 8.0, 0.0), ("kb", -LN3, 2 * LN3), ("qA", float(NB["A"]), 0.0), ("qB", float(NB["B"]), 0.0),
                        ("c0", -65536.0, 983039.0 + NB["A"]), ("c1", -65536.0, 983039.0 + NB["B"]), ("c2", -65536.0, 983040.0 + 8192),
-                       ("c3", -65536.0, 983040.0 + 10240), ("c4", 0.0, 0.0), ("c5", 0.0, 2048.0), ("one", 1.0, 64.0),
+                       ("c3", -65536.0, 983040.0 + 10240), ("c4", 0.0, 0.0), ("c5", 0.0, 2048.0), ("one", 1.0, -1.0),
                        ("c6", -65536.0, 983040.0 + 4148), ("c7", -65536.0, 983040.0 + 4212)):
         V(1, TS(col(name), col("qc"), a, b, O.mult, O.add), ("qc",), (name,))
-    V(6, TS(T.col[:, 16:22], T.jrow[:, 1:7], -1.0, col("one"), O.mult, O.add), ("jrow", "one"), ("qk",))
-    V(6, TS(T.col[:, 32:38], T.col[:, 16:22], -4.0, 4.0, O.mult, O.add), ("qk",), ("qk4",))
+    for q in RR:
+        V(1, TS(T.col[:, 16 + q:17 + q], col("qc"), -1.0 - RR[q][0], None, O.add), ("qc",), ("qk%d" % q,))
+    V(64, MS(mat("k-3"), -3.0 / 128), (), ("k-3",))
+    V(64, MS(mat("k1"), 1.0 / 128), (), ("k1",))
     V(5, TS(T.col[:, 24:29], T.jrow[:, 0:5], -1.0, -0.5, O.mult, O.add), ("jrow",), ("half",))
     V(1, MS(T.col[:, 30:31], 1.0), (), ("onec",))
     V(1, TS(col("iz"), col("qc"), 0.0, None, O.is_equal), ("qc",), ("iz",))
@@ -276,12 +278,14 @@ def rank_program(g, core, T, topo):
                               ("n256", T.bm[:], "bm", -256.0), ("hb", T.bm[:], "bm", 0.5), ("Wb", T.bm[:], "bm", "w")):
         V(64, TS(mat(name), src, col(a) if a in _COL else a, None, O.mult), (tok, a) if a in _COL else (tok,), (name + "m" if name in ("bA", "bB") else name,))
     V(128, CP(T.b8[:], T.bm[:]), ("bm",), ("b8",))
+    for q in RR:
+        S(128, ACT(mat("q%d" % q), T.idn[:], AF.Copy, scale=T.col[:, 16 + q:17 + q]), ("idn", "qk%d" % q), ("q%dm" % q,))
     for l in range(1, 5):
         V(256, TT(T.hsd[:, (l - 1) * 128:l * 128], T.shm[:, (l - 1) * 128:l * 128],
                   T.idn[:] if l == 1 else T.shm[:, (l - 2) * 128:(l - 1) * 128], O.subtract),
           ("shm%d" % l, "idn" if l == 1 else "shm%d" % (l - 1)), ("hsd%d" % l,))
     V(256, TS(T.hsh[:], T.hsd[:], 0.5, None, O.mult), ("hsd1", "hsd2", "hsd3", "hsd4"), ("hsh",))
-    for n in sorted({x for h in "AB" if not OPT["nf"][h] for x in (OPT["na"][h], NB[h])}):
+    for n in sorted({OPT["na"][h] for h in "AB" if not OPT["nf"][h]} | set(NB.values())):
         iota(T["mz%d" % n][:], [[0, 256], [256, n]], 0, 256 * n, ("mz%d" % n,))
     iota(T.jj[:], [[1, 128]], 0, 128, ("jj",))
     iota(T.j16[:], [[0, 8], [1, 16]], 0, 128, ("j16",))
@@ -350,30 +354,35 @@ def rank_program(g, core, T, topo):
             C, L, ct, lt = Cw[:, o:o + H2], Lw[:, o:o + H2], "C%d%s" % (t, h), "L%d%s" % (t, h)
             bV = "pV" + h
             pV = T[bV]
-            if t and h in OPT["fast"]:
-                V(64, TS(pV[:, 384:448], St[:, o:o + H2], T.acnt[:], None, O.add), ("st%d" % t, "acnt"), ("bs" + h,), (bV,))
-                V(64, TS(B("base" + h), L, 613.0, None, O.mult), (lt,), ("base" + h,))
-                V(64, TT(T["off" + h][:], B("base" + h), pV[:, 384:448], O.add), ("base" + h, "bs" + h), ("off" + h,), (bV,))
+            if t:
+                V(64, TS(T["pU" + h][:, 64:128], St[:, o:o + H2], T.acnt[:], None, O.add), ("st%d" % t, "acnt"), ("bs" + h,), ("pU" + h,))
+                if h in OPT["fast"]:
+                    V(64, TT(T["off" + h][:], L, T["pU" + h][:, 64:128], O.add), (lt, "bs" + h), ("off" + h,), ("pU" + h,))
+                else:
+                    V(64, TT(B("Q" + h), L, T["pU" + h][:, 64:128], O.add), (lt, "bs" + h), ("Q" + h,), ("pU" + h,))
+                    V(64, TS(B("s1" + h), B("Q" + h), 4095, None, O.bitwise_and), ("Q" + h,), ("s1" + h,))
+                    V(64, CP(T["off" + h][:], B("s1" + h)), ("s1" + h,), ("off" + h,))
             else:
                 V(64, TS(B("base" + h), L, 613.0, None, O.mult), (lt,), ("base" + h,))
-                V(128, TT(pV[:, 384:448], B("base" + h), St[:, o:o + H2], O.add), ("base" + h, "st%d" % t), ("bs" + h,), (bV,))
-                V(64, TS(B("Q" + h), pV[:, 384:448], T.acnt[:] if t else 0.0, None, O.add), ("bs" + h, "acnt"), ("Q" + h,), (bV,))
+                V(128, TT(B("Q" + h), B("base" + h), St[:, o:o + H2], O.add), ("base" + h, "st%d" % t), ("Q" + h,))
                 V(64, TS(B("s1" + h), B("Q" + h), 4095, None, O.bitwise_and), ("Q" + h,), ("s1" + h,))
                 V(64, CP(T["off" + h][:], B("s1" + h)), ("s1" + h,), ("off" + h,))
-            P(64, SUM(pV[:, 0:64], [(rm(17), L)]), (lt, "Rm17"), ("Lb" + h,), (bV,))
+            sc = 1.0 / 613 if t else 1.0
+            S(64, ACT(T.SP[:, 4148 + o:4148 + o + H2], L, AF.Copy, scale=sc), (lt,), ("SP" + h,))
+            P(64, SUM(pV[:, 0:64], [(rm(17), T.SP[:, 4148 + o:4148 + o + H2])]), ("SP" + h, "Rm17"), ("Lb" + h,), (bV,))
             V(64, TS(B("e0" + h), pV[:, 0:64], col("q8"), col("iz"), O.is_equal, O.subtract), ("Lb" + h, "q8", "iz"), ("e0" + h,), (bV,))
             V(128, TT(B("t0" + h), B("e0" + h), C, O.mult), ("e0" + h, ct), ("t0" + h,))
             P(128, SUM(pV[:, 64:128], [(rm(17), C), (win(T.Ez, 0), B("t0" + h))]), (ct, "t0" + h, "Rm17", "Ez"), ("c80" + h,), (bV,))
             LIN(OPT["c0"], B("w8" + h), pV[:, 64:128], 1.0 / 32, 0.125, ("c80" + h,), ("w8" + h,), (bV,))
             LIN(OPT["c0"], B("c0" + h), pV[:, 64:128], 1.0, -4.0, ("c80" + h,), ("c0" + h,), (bV,))
-            S(64, ACT(B("Kp" + h), L, AF.Exp, scale=16 * LN3, bias=col("kb")), (lt, "kb"), ("Kp" + h,))
-            S(64, ACT(pV[:, 448:512], L, AF.Copy), (lt,), ("L" + h,), (bV,))
-            S(64, ACT(T.SP[:, 4148 + o:4148 + o + H2], L, AF.Copy), (lt,), ("SP" + h,))
+            S(64, ACT(B("Kp" + h), L, AF.Exp, scale=16 * LN3 * sc, bias=col("kb")), (lt, "kb"), ("Kp" + h,))
+            S(64, ACT(pV[:, 448:512], L, AF.Copy, scale=sc), (lt,), ("L" + h,), (bV,))
             for j0 in range(0, len(jobs), 8):
                 bk = ("pD" + h, "pE" + h)[j0 // 8 % 2]
                 rs = jobs[j0:j0 + 8]
-                P(64 * len(rs), [MM(T[bk][:, 64 * j:64 * j + 64], rm(r), C, True, True) for j, r in enumerate(rs)],
-                  (ct,) + tuple("Rm%d" % r for r in rs), ("dM" + bk,), (bk,))
+                for c in range(0, len(rs), 2):
+                    P(128, [MM(T[bk][:, 64 * j:64 * j + 64], rm(rs[j]), C, True, True) for j in (c, c + 1)],
+                      (ct, "Rm%d" % rs[c], "Rm%d" % rs[c + 1]), ("dM%d%s" % (c // 2, bk),), (bk,))
                 for q in sorted(RR):
                     for j, r in enumerate(rs):
                         if r in RR[q]:
@@ -384,7 +393,7 @@ def rank_program(g, core, T, topo):
                                 aff(out, T["T%d%s" % (src[0], h)][:, 1 + RR[src[0]].index(r):64 * WID[src[0]]:WID[src[0]]], [[0, 64]], O.is_equal, 0, 0,
                                     ("T%d_%d%s" % (src[0], r, h),), ("T%d_%d%s" % (q, r, h),), 64)
                             else:
-                                LIN("v" if e[-1] == "v" else "s", out, T[bk][:, 64 * j:64 * j + 64], 1.0, -4.0 if r > 16 else 0.0, ("dM" + bk,),
+                                LIN("v" if e[-1] == "v" else "s", out, T[bk][:, 64 * j:64 * j + 64], 1.0, -4.0 if r > 16 else 0.0, ("dM%d%s" % (j // 2, bk),),
                                     ("T%d_%d%s" % (q, r, h),), (bk,))
         if t == 0:
             spans(256, 84, 344)
@@ -393,17 +402,17 @@ def rank_program(g, core, T, topo):
         if last:
             for hi, h in enumerate("AB"):
                 pE, prev = T["pE" + h], ()
-                for c in range(4):
-                    prev = (P(512, [MM(pE[:, 0:64], T.idn[:], T.X[:, 2048 * hi + j:2048 * hi + 2048:32], j == 0, j == 31) for j in range(8 * c, 8 * c + 8)],
+                for c in range(8):
+                    prev = (P(256, [MM(pE[:, 0:64], T.idn[:], T.X[:, 2048 * hi + j:2048 * hi + 2048:32], j == 0, j == 31) for j in range(4 * c, 4 * c + 4)],
                               ("X", "idn"), ("sums%d%s" % (c, h),), ("pE" + h,), after=prev),)
-                S(64, ACT(B("S0" + h), pE[:, 0:64], AF.Copy), tuple("sums%d%s" % (c, h) for c in range(4)), ("S0" + h,), ("pE" + h,))
+                S(64, ACT(B("S0" + h), pE[:, 0:64], AF.Copy), tuple("sums%d%s" % (c, h) for c in range(8)), ("S0" + h,), ("pE" + h,))
         for k in range(6):
             for hi, h in enumerate("AB"):
                 bU, bV = "pU" + h, "pV" + h
                 pV = T[bV]
                 z, zr, zs = slot(h, k)
                 z0 = zs if zr == 1 else 0
-                wide = k > 0 or (t and h in OPT["fast"])
+                wide = k > 0 or (t > 0 and h in OPT["fast"])
                 nv = OPT["gv"].get((k, h), 0)
                 zk = ()
                 parts = [("s", 0, 64 - nv), ("v", 64 - nv, 64)]
@@ -419,8 +428,11 @@ def rank_program(g, core, T, topo):
                 y, by = T[bU][:, 0:64], bU
                 k0 = P(128, [MM(y, mat("kc"), T.ones[:, 0:64], True, False), MM(y, mat("ke"), T.ones[:, 0:64], False, False)],
                        ("kc0", "kc1", "ke", "ones"), ("u0" + h,), (by,))
-                P(1024, [MM(y, win(T.Wz, m), z[:, zr * m + zs:1024 * zr + z0:16 * zr], False, m == 15) for m in range(16)], zk + ("Wz",), ("u" + h,), (by,), after=(k0,))
-                ut = ("u0" + h, "u" + h)
+                ut = ("u0" + h,)
+                for c in range(0, 16, OPT["um"]):
+                    ut += ("u_%d%s" % (c, h),)
+                    k0 = P(64 * OPT["um"], [MM(y, win(T.Wz, m), z[:, zr * m + zs:1024 * zr + z0:16 * zr], False, m == 15) for m in range(c, c + OPT["um"])],
+                           zk + ("Wz",), ut[-1:], (by,), after=(k0,))
                 na, nb = OPT["na"][h], NB[h]
                 if k == OPT["nf"][h] - 1:
                     zt = tuple(x for x in lastw if x[0] == "z" and x[-1] == h and int(x[1]) <= k)
@@ -444,11 +456,24 @@ def rank_program(g, core, T, topo):
                 n = WID.get(TILE[k], 1)
                 V(64, TT(B("k8" + h), y, T["co" + h][:, n - 1:64 * n:n] if k else B("c0" + h), O.add), ut + ("co" + h if k else "c0" + h,), ("k8" + h,), (bU,))
                 V(64, TS(B("n1" + h), B("k8" + h), 3, 3, O.arith_shift_right, O.bitwise_and), ("k8" + h,), ("n1" + h,))
-                Pk, pt = pV[:, 64 * k:64 * k + 64], "P%d%s" % (k + 1, h)
-                if k == 0:
-                    V(64, TS(Pk, B("n1" + h), 64.0, None, O.add), ("n1" + h,), (pt,), (bV,))
-                elif k < 5:
-                    V(64, TT(Pk, B("n1" + h), pV[:, 64 * k - 64:64 * k], O.add), ("n1" + h, "P%d%s" % (k, h)), (pt,), (bV,))
+                if k < 5:
+                    q = TILE[k + 1]
+                    n2, da, db = WID[q], "da%d%s" % (q, h), "db%d%s" % (k + 1, h)
+                    D = T[db][:, 0:64 * n2:n2]
+                    if k == 0:
+                        V(64, TS(D, B("n1" + h), 1.0 - RR[q][0], None, O.add), ("n1" + h,), (db,))
+                    else:
+                        V(64, TT(D, B("n1" + h), pV[:, 128:192], O.add), ("n1" + h, "Dp" + h), (db,), (bV,))
+                    if k == 0:
+                        V(64, TS(B("b" + h), B("n1" + h), col("one"), None, O.is_ge), ("n1" + h, "one"), ("b" + h,))
+                    else:
+                        V(64, TT(B("b" + h), B("n1" + h), pV[:, 192:256], O.is_ge), ("n1" + h, "Dp" + h), ("b" + h,), (bV,))
+                    V(64, TT(T[da][:, 1:64 * n2:n2], B("b" + h), pV[:, 448:512], O.mult), ("b" + h, "L" + h), (da,), (bV,))
+                    if k < 4:
+                        on = "k%d" % (1 - RR[TILE[k + 2]][0] + RR[q][0])
+                        P(256, SUM(pV[:, 128:192], [(mat(on), T.ones[:, 0:64]), (T.idn[:], D)]) + SUM(pV[:, 192:256], [(mat("q%d" % q), T.ones[:, 0:64]), (mat("nid"), D)]),
+                          (db, on, "idn", "ones", "nid", "q%dm" % q), ("Dp" + h,), (bV,))
+                    entry(k + 1, h)
                 else:
                     P(448, SUM(pV[:, 384:448], [(mat("kd"), T.ones[:, 0:64]), (mat("nid"), T.jj[:, 64 * hi:64 * hi + 64])]
                                + [(mat("a%d" % j), T["db%d%s" % (j, h)][:, 0:64 * WID[TILE[j]]:WID[TILE[j]]]) for j in range(1, 6)]),
@@ -456,16 +481,6 @@ def rank_program(g, core, T, topo):
                     if h in OPT["cmpv"]:
                         P(64, SUM(pV[:, 320:384], [(T.idn[:], T["F" + h][:, 0:64])]), ("F" + h, "idn"), ("Fp" + h,), (bV,))
                     V(64, TT(pV[:, 384:448], B("n1" + h), pV[:, 384:448], O.add), ("n1" + h, "cod" + h), ("code" + h,), (bV,))
-                if k < 5:
-                    q = TILE[k + 1]
-                    n2, da, db = WID[q], "da%d%s" % (q, h), "db%d%s" % (k + 1, h)
-                    if OPT["b"] == "s":
-                        S(64, ACT(B("b" + h), Pk, AF.Relu, scale=4.0, bias=T.col[:, 32 + k + 1:33 + k + 1]), (pt, "qk4"), ("b" + h,), (bV,))
-                    else:
-                        V(64, TS(B("b" + h), Pk, qk(k + 1), 4.0, O.is_ge, O.mult), (pt, "qk"), ("b" + h,), (bV,))
-                    LIN(OPT["db"], T[db][:, 0:64 * n2:n2], Pk, 1.0, float(k + 1 - 64 - RR[q][0]), (pt,), (db,), (bV,))
-                    V(64, TT(T[da][:, 1:64 * n2:n2], B("b" + h), pV[:, 448:512], O.min), ("b" + h, "L" + h), (da,), (bV,))
-                    entry(k + 1, h)
         for hi, h in enumerate("AB"):
             o = H2 * hi
             C, L, ct, lt = Cw[:, o:o + H2], Lw[:, o:o + H2], "C%d%s" % (t, h), "L%d%s" % (t, h)
@@ -477,17 +492,16 @@ def rank_program(g, core, T, topo):
             zt = tuple(x for x in lastw if x[0] == "z" and x[-1] == h and int(x[1]) >= (OPT["nf"][h] or na))
             zall = zt
             nf = OPT["nf"][h]
-            for c, bk in enumerate((bD, bE) if nf else ()):
-                P(512, SUM(T[bk][:], [(T.idn[:], T["Y" + h][:, 4096 + 1024 * t + 512 * c:4608 + 1024 * t + 512 * c])]), ("M%d%s" % (t, h), "idn"), ("Mp" + bk,), (bk,))
-                for k in range(nf, 5):
-                    V(512, TT(T[bk][:], T["Y" + h][:, 1024 * (k - nf) + 512 * c:1024 * (k - nf) + 512 * c + 512], T[bk][:], O.max),
-                      tuple(x for x in zall if int(x[1]) == k) + ("Mp" + bk,), ("Mp" + bk,), (bk,))
             for j in range(4):
                 zt = tuple(x for x in zall if int(x[:-1].split("_")[1]) < 16 * j + 16 and int(x[:-1].split("_")[2]) > 16 * j)
                 if nf:
-                    bk = (bD, bE)[j // 2]
-                    V(256, TT(VS[:, 256 * j:256 * j + 256], T["Y" + h][:, 1024 * (5 - nf) + 256 * j:1024 * (5 - nf) + 256 * j + 256],
-                              T[bk][:, 256 * (j % 2):256 * (j % 2) + 256], O.max), zt + ("Mp" + bk,), ("VS%d%s" % (j, h),), (bk,))
+                    out, in_ = T["Y" + h][:, 256 * nb * j:256 * nb * (j + 1):nb], T["Y" + h][:, 4096 + 1024 * t + 256 * j:4352 + 1024 * t + 256 * j]
+                    if h in OPT["mg"]:
+                        aff(out, in_, [[0, 256]], O.is_equal, 0, 0, ("M%d%s" % (t, h),), ("Y%d%s" % (j, h),), 256)
+                    else:
+                        V(128, CP(out, in_), ("M%d%s" % (t, h),), ("Y%d%s" % (j, h),))
+                    V(128 * nb, SCAN(VS[:, 256 * nb * j:256 * nb * (j + 1)], T["mz%d" % nb][:], T["Y" + h][:, 256 * nb * j:256 * nb * (j + 1)], O.min, O.max),
+                      zt + ("mz%d" % nb, "Y%d%s" % (j, h)), ("VS%d%s" % (j, h),))
                     continue
                 src = T["z" + h][:, 1536 * j:1536 * (j + 1)] if na == 6 else T["Y" + h][:, 256 * na * nb * j + (na - 1) * nb % na:256 * na * nb * (j + 1):na]
                 V(128 * nb, SCAN(VS[:, 256 * nb * j:256 * nb * (j + 1)], T["mz%d" % nb][:], src, O.min, O.max),
@@ -501,14 +515,15 @@ def rank_program(g, core, T, topo):
                           ("ind%d_%d%s" % (c, m, h),), (bV,))
                     continue
                 k0 = P(512, [MM(ps[:], mat("nid"), T["F" + h][:], True, False)], ("F" + h, "Fr" + h, "nid"), ("VF" + bk,), (bk,))
-                P(512, [MM(ps[:, 64 * j:64 * j + 64], T.idn[:], VS[:, nb * (8 * c + j) + nb - 1:1024 * nb:16 * nb], False, j == 7) for j in range(8)], vt + ("idn",),
-                  ("VG" + bk,), (bk,), after=(k0,))
-                S(512, ACT(T["ind" + h][:, 512 * c:512 * c + 512], ps[:], AF.Sign, bias=half(0)), ("VF" + bk, "VG" + bk, "half"), ("ind%d%s" % (c, h),), (bk,))
+                for e in (0, 4):
+                    k0 = P(256, [MM(ps[:, 64 * j:64 * j + 64], T.idn[:], VS[:, nb * (8 * c + j) + nb - 1:1024 * nb:16 * nb], False, j == 7) for j in range(e, e + 4)],
+                           vt + ("idn",), ("VG%d%s" % (e, bk),), (bk,), after=(k0,))
+                S(512, ACT(T["ind" + h][:, 512 * c:512 * c + 512], ps[:], AF.Sign, bias=half(0)), ("VF" + bk, "VG0" + bk, "VG4" + bk, "half"), ("ind%d%s" % (c, h),), (bk,))
             prev = ()
-            for c in range(2):
-                prev = (P(512, [MM(pD[:, 0:64], win(T.Ez, m), T["ind" + h][:, 64 * m:64 * m + 64], m == 0, m == 15) for m in range(8 * c, 8 * c + 8)],
-                          ("ind%d%s" % (c, h), "Ez") + tuple("ind%d_%d%s" % (c, m, h) for m in range(16)), ("cnt%d%s" % (c, h),), (bD,), after=prev),)
-            V(64, TS(pD[:, 0:64], pD[:, 0:64], 68.0 if h in OPT["cmpv"] else 8.0, None, O.is_ge), ("cnt0" + h, "cnt1" + h), ("f" + h,), (bD,))
+            for c in range(4):
+                prev = (P(256, [MM(pD[:, 0:64], win(T.Ez, m), T["ind" + h][:, 64 * m:64 * m + 64], m == 0, m == 15) for m in range(4 * c, 4 * c + 4)],
+                          ("ind%d%s" % (c // 2, h), "Ez") + tuple("ind%d_%d%s" % (c // 2, m, h) for m in range(4 * c, 4 * c + 4)), ("cnt%d%s" % (c, h),), (bD,), after=prev),)
+            V(64, TS(pD[:, 0:64], pD[:, 0:64], 68.0 if h in OPT["cmpv"] else 8.0, None, O.is_ge), tuple("cnt%d%s" % (c, h) for c in range(4)), ("f" + h,), (bD,))
             V(64, TT(B("E" + h), pD[:, 0:64], B("Kp" + h), O.mult), ("f" + h, "Kp" + h), ("E" + h,), (bD,))
             P(64, SUM(pD[:, 64:128], [(mat("hb"), B("E" + h))]), ("E" + h, "hb"), ("Es" + h,), (bD,))
             V(64, TT(acc, B("E" + h), pD[:, 64:128], O.is_gt), ("E" + h, "Es" + h), ("acc" + h,), (bD,))
@@ -520,9 +535,20 @@ def rank_program(g, core, T, topo):
             gather("v", B("Vsel" + h), VS[:, 0:1024 * nb], T["voff" + h][:], 64, vt + ("voff" + h,), ("Vsel" + h,))
             if not last:
                 V(4, TT(B("tb" + h), B("wr" + h, 79, 128, 16), T.Kt[:, 4 * hi:4 * hi + 4], O.add), ("wr" + h, "Kt" + h), ("tb" + h,))
-            P(128 if last else 64, SUM(pD[:, 320:384], [(mat("Wb"), B("Vsel" + h))]) + (SUM(pD[:, 384:448], [(T.bm[:], acc)]) if last else []),
-              ("Vsel" + h, "Wb", "acc" + h, "bm"), ("hb" + h,), (bD,))
-            V(64, SCAN(B("hw" + h), T.dg[:, 0:64], pD[:, 320:384], O.add, O.min), ("hb" + h, "dg"), ("hw" + h,), (bD,))
+            if h in OPT["hp"]:
+                prev = ()
+                for c in range(0, 16, 4):
+                    prev = (P(256, [MM(pE[:, 0:64], win(T.Wz, m), VS[:, nb * m + nb - 1:1024 * nb:16 * nb], m == 0, m == 15) for m in range(c, c + 4)],
+                              vt + ("Wz",), ("hT%d%s" % (c, h),), (bE,), after=prev),)
+                V(64, TT(B("ah" + h), acc, pE[:, 0:64], O.mult), ("acc" + h,) + tuple("hT%d%s" % (c, h) for c in range(0, 16, 4)), ("ah" + h,), (bE,))
+                P(256, SUM(pE[:, 448:512], [(T.b8[:], B("ah" + h))]), ("ah" + h, "b8"), ("hc" + h,), (bE,))
+                V(64, SCAN(B("hw" + h), T.dg[:, 0:64], pE[:, 448:512], O.add, O.min), ("hc" + h, "dg"), ("hw" + h,), (bE,))
+                if last:
+                    P(64, SUM(pD[:, 384:448], [(T.bm[:], acc)]), ("acc" + h, "bm"), ("hb" + h,), (bD,))
+            else:
+                P(128 if last else 64, SUM(pD[:, 320:384], [(mat("Wb"), B("Vsel" + h))]) + (SUM(pD[:, 384:448], [(T.bm[:], acc)]) if last else []),
+                  ("Vsel" + h, "Wb", "acc" + h, "bm"), ("hb" + h,), (bD,))
+                V(64, SCAN(B("hw" + h), T.dg[:, 0:64], pD[:, 320:384], O.add, O.min), ("hb" + h, "dg"), ("hw" + h,), (bD,))
             V(4, TS(B("h1" + h), B("hw" + h, 15, 64, 16), 31, None, O.bitwise_and), ("hw" + h,), ("h1" + h,))
             V(4, TT(T["toff" + h][:], B("h1" + h), T.Kt[:, 8 + 4 * hi:12 + 4 * hi] if last else B("tb" + h), O.add), ("h1" + h, "tb" + h, "Kl" + h), ("toff" + h,))
             if not last:
@@ -531,9 +557,10 @@ def rank_program(g, core, T, topo):
                         ("toff" + h, "Vsel" + h), (x, "Xw"))
             else:
                 gather("v", B("xo" + h), T.X[:, 0:4096], T["toff" + h][:, 0:4], 64, ("X", "toff" + h), ("xo" + h,))
-                V(128, TT(B("xd" + h), B("Vsel" + h), B("xo" + h), O.subtract), ("Vsel" + h, "xo" + h), ("xd" + h,))
-                V(64, TT(B("xe" + h), B("xd" + h), pD[:, 384:448], O.mult), ("xd" + h, "hb" + h), ("xe" + h,), (bD,))
-                V(128, TT(B("yss" + h), B("xe" + h), B("S0" + h), O.add), ("xe" + h, "S0" + h), ("yss" + h,))
+                V(64, TT(B("xd" + h), B("Vsel" + h), pD[:, 384:448], O.mult), ("Vsel" + h, "hb" + h), ("xd" + h,), (bD,))
+                V(128, TT(pD[:, 448:512], B("xd" + h), B("S0" + h), O.add), ("xd" + h, "S0" + h), ("xs" + h,), (bD,))
+                V(64, TT(B("xe" + h), B("xo" + h), pD[:, 384:448], O.mult), ("xo" + h, "hb" + h), ("xe" + h,), (bD,))
+                V(64, TT(B("yss" + h), pD[:, 448:512], B("xe" + h), O.subtract), ("xe" + h, "xs" + h), ("yss" + h,), (bD,))
                 dma("s", [(T.ys[:, o:o + H2], B("yss" + h))], ("yss" + h,), ())
             P(256, [MM(pE[:, 64 * l:64 * l + 64], T.hsh[:, 128 * l:128 * l + 128], C, True, True) for l in range(4)], (ct, "hsh"), ("SH" + h,), (bE,))
             V(64, TT(B("aL" + h), acc, pV[:, 448:512], O.mult), ("acc" + h, "L" + h), ("aL" + h,), (bV,))
@@ -552,20 +579,21 @@ def rank_program(g, core, T, topo):
             P(256, SUM(pU[:, 0:64], [(T.b8[:], B("ay" + h))]), ("ay" + h, "b8"), ("cb" + h,), (bU,))
             V(64, SCAN(B("wc" + h), T.dg[:, 0:64], pU[:, 0:64], O.add, O.min), ("cb" + h, "dg"), ("wc" + h,), (bU,))
             V(4, TT(T["loff" + h][:], B("wc" + h, 15, 64, 16), T.Kv[:, 8 + 4 * hi:12 + 4 * hi], O.add), ("wc" + h, "Ks" + h), ("loff" + h,))
-            gather(OPT["lg"], T[sL][:], T.SP[:], T["loff" + h][:], 64, ("loff" + h, "SPA", "SPB", "SPz", "SP"), (sL,))
+            add("s", (0.065, 0, 64), [lambda o_=T[sL][:], f_=T["loff" + h][:], a_=1.0 if last else 613.0: g.scalar.activation(o_, T.SP[:].indirect(f_), AF.Copy, scale=a_)],
+                ("loff" + h, "SPA", "SPB", "SPz", "SP"), (sL,))
             if not last:
                 send(T["L%d" % (t + 1)][:, o:o + H2], T[sL][:], "arr%dL%s" % (t + 1, h), 1, (sL,), ("L%d%s" % (t + 1, h),))
             else:
                 dma("y", [(T.yl[:, o:o + H2], T[sL][:])], (sL,), ())
-            P(384, SUM(pE[:, 384:448], [(mat("hid"), F), (mat("b256"), acc), (mat("kq"), T.ones[:, 0:64]), (mat("hid"), B("Vsel" + h))])
-              + SUM(pE[:, 448:512], [(T.idn[:], F), (mat("n256"), acc)]),
-              ("F" + h, "acc" + h, "Vsel" + h, "hid", "idn", "b256", "n256", "kq", "ones"), ("fa" + h,), (bE,))
-            V(64, TS(B("fr" + h), pE[:, 384:448], 12582912.0 - 256, -12582912.0, O.add, O.add), ("fa" + h,), ("fr" + h,), (bE,))
+            P(384, SUM(pV[:, 0:64], [(mat("hid"), F), (mat("b256"), acc), (mat("kq"), T.ones[:, 0:64]), (mat("hid"), B("Vsel" + h))])
+              + SUM(pV[:, 64:128], [(T.idn[:], F), (mat("n256"), acc)]),
+              ("F" + h, "acc" + h, "Vsel" + h, "hid", "idn", "b256", "n256", "kq", "ones"), ("fa" + h,), (bV,))
+            V(64, TS(B("fr" + h), pV[:, 0:64], 12582912.0 - 256, -12582912.0, O.add, O.add), ("fa" + h,), ("fr" + h,), (bV,))
             if not last:
-                V(64, TT(F, B("fr" + h), pE[:, 448:512], O.max), ("fr" + h, "fa" + h), ("F" + h,), (bE,))
+                V(64, TT(F, B("fr" + h), pV[:, 64:128], O.max), ("fr" + h, "fa" + h), ("F" + h,), (bV,))
                 spread(h)
             else:
-                V(64, TT(B("yfs" + h), B("fr" + h), pE[:, 448:512], O.max), ("fr" + h, "fa" + h), ("yfs" + h,), (bE,))
+                V(64, TT(B("yfs" + h), B("fr" + h), pV[:, 64:128], O.max), ("fr" + h, "fa" + h), ("yfs" + h,), (bV,))
                 dma("s", [(T.yf[:, o:o + H2], B("yfs" + h))], ("yfs" + h,), ())
             if hi and not last:
                 P(128, SUM(T.pUA[:, 0:64], [(ones, B("accA")), (ones, acc)]), ("accA", "accB", "ones"), ("As",), ("pUA",))
@@ -646,18 +674,26 @@ def rank_program(g, core, T, topo):
         return span, at, span / (OPT["f"] + 0.25 * OPT["gr"]) + replay(at)
 
     if n not in PLAN:
-        best = tighten(sorted(range(n), key=lambda k: -prio[k]))
+        best = kept = tighten(sorted(range(n), key=lambda k: -prio[k]))
         rng = np.random.RandomState(OPT["seed"])
+        kinds = sorted({p["name"][:2] + p["name"][-1] for p in ops})
+        kind = np.array([kinds.index(p["name"][:2] + p["name"][-1]) for p in ops])
         for _ in range(OPT["tries"]):
             mid, wide, at = rng.uniform(0, best[0]), rng.uniform(2, 12), np.array(best[1])
-            key = (at + rng.normal(0, OPT["shake"], n) * (np.abs(at - mid) < wide)).tolist()
+            push = rng.normal(0, OPT["shake"], n)
+            if rng.uniform() < OPT["kin"]:
+                wide, push = wide / 2, 0.3 * push + rng.normal(0, OPT["far"], len(kinds))[kind] * (rng.uniform(size=len(kinds)) < 0.3)[kind]
+            key = (at + push * (np.abs(at - mid) < wide)).tolist()
             for k in range(n):
                 for d, _w in pred[k]:
                     if key[d] >= key[k]:
                         key[k] = key[d] + 1e-6
             other = tighten(sorted(range(n), key=lambda k: key[k]))
-            if other[2] <= best[2]:
+            if other[2] <= best[2] * (1 + OPT["slack"] * (1 - _ / OPT["tries"])):
                 best = other
+                if best[2] < kept[2]:
+                    kept = best
+        best = kept
         if "hook" in OPT:
             best = OPT["hook"](ops, place, pred, next_, cost, hold, best)
         PLAN[n] = best

import math
import numpy as np
from concourse.bass import DstId, RemoteDMATransfer
from concourse.mybir import AluOpType as O, ActivationFunctionType as AF

H2 = 64
OPT = {"tiles": 3, "te": {"A1": "s", "A2": "g", "A3": "g", "B1": "s", "B2": "g", "B3": "g"}, "na": {"A": 3, "B": 4}, "fast": "B", "gv": {(k, h): (24, 16, 16)[k] for k in range(3) for h in "AB"}, "eqs": "", "w8": "v", "db": "v",
       "nf": {"A": 3, "B": 3}, "fold": 8.5, "mg": "AB", "um": 4, "issue": 0.7, "fly": 1.6, "hp": "", "lg": "s", "b": "v", "gs": 0, "x2": "v", "c0": "s", "c5": "AB", "cmpv": "B", "ws": 0.22, "wx": 0.22, "f": 1.15, "gr": 1.7, "paces": ((1.0, 1.56), (1.35, 2.08), (1.4, 1.25)), "tries": 5000, "shake": 0.6, "slack": 0.0, "kin": 0.3, "far": 1.5, "seed": 0, "chunks": 16}
PLAN = {}
TILES = {3: ((0, 1, 2, 3, 3, 3), {1: (8, 1), 2: (12, 2), 3: (16, 3)})}
SCRATCH = {}
SEMAPHORES = ["sv", "ss", "st_", "sg", "loc", "arst1", "arst2"] + ["arr%d%s%s" % (t, x, h) for t in (1, 2) for x in "LC" for h in "AB"]
SEMAPHORES += ["d%d" % k for k in range(40)] + ["f%s%d%s" % (x, t, h) for x in "abl" for t in range(3) for h in "AB"]
_BF, _F32, _I32, _U16 = "bfloat16", "float32", "int32", "uint16"
_COL = ("qc", "q8", "iz", "kb", "qA", "qB", "c0", "c1", "c2", "c3", "c4", "c5", "w", "one", "c6", "c7")
_MAT = ("nid", "hid", "hs4", "kc", "ke", "kq", "bA", "bB", "bn", "b256", "n256", "hb", "Wb", "kd", "a1", "a2", "a3", "a4", "a5", "k-3", "k1", "q1", "q2", "q3")
for _n, _c, _d in (("X", 16384, _BF), ("C0", 128, _BF), ("C1", 128, _BF), ("C2", 128, _BF), ("L0", 128, _BF), ("L1", 128, _F32), ("L2", 128, _F32),
                   ("wts", 1, _BF), ("st0", 128, _I32), ("st1", 128, _I32), ("st2", 128, _I32), ("pI", 1, _I32), ("aI", 1, _I32),
                   ("col", 64, _F32), ("jrow", 18, _F32), ("cqx", 18, _F32), ("dif", 17, _F32), ("dif8", 21, _F32), ("il0", 4, _F32), ("il", 4, _F32),
                   ("Kv", 16, _F32), ("Kt", 16, _F32), ("acnt", 1, _F32), ("junk", 64, _BF), ("b8", 128, _F32),
                   ("ones", 960, _BF), ("bm0", 128, _BF), ("bm", 128, _BF), ("idn", 128, _BF), ("tri", 128, _BF), ("shm", 512, _BF),
                   ("hsd", 512, _BF), ("hsh", 512, _BF), ("mat", len(_MAT) * 128, _BF), ("Wz", 144, _BF), ("Ez", 144, _BF), ("Rm", 21 * 128, _BF),
                   ("mz2", 512, _BF), ("mz3", 768, _BF), ("mz4", 1024, _BF), ("mz5", 1280, _BF), ("mz6", 1536, _BF),
                   ("SP", 4276, _BF), ("TB", 1368, _BF), ("shd", 512, _BF), ("jj", 128, _BF), ("j16", 128, _BF), ("dg0", 128, _BF), ("dg", 128, _BF)):
    SCRATCH[_n] = ("sbuf", [128, _c], _d)
_PACK = {}
_SMALL = {_BF: (("b", 64), ("Kp", 64), ("f", 64), ("E", 64), ("acc", 64), ("aL", 64), ("e0", 64), ("t0", 64), ("Vsel", 64), ("xo", 64),
                ("fr", 64), ("yfs", 64), ("w8", 64), ("c0", 64), ("e5", 64), ("keep", 64)),
          _F32: (("base", 64), ("wr", 128), ("tb", 4), ("S0", 64), ("xd", 64), ("xe", 64), ("yss", 64), ("ay", 64), ("wc", 64), ("ah", 64)),
          _I32: (("ab", 128), ("am", 128), ("k8", 64), ("Q", 64), ("s1", 64), ("n1", 64), ("hw", 64), ("h1", 4), ("k5", 64), ("n5", 64))}
for _h in "AB":
    for _d, _names in _SMALL.items():
        _at = 0
        for _n, _c in _names:
            _PACK[_n + _h] = ("pk" + _d[0] + _h, _at, _c)
            _at += -(-_c // 32) * 32
        SCRATCH["pk" + _d[0] + _h] = ("sbuf", [128, _at], _d)
    for _n, _c, _d in (("z", 5120, _BF), ("Y", 12288, _BF), ("VS", 4096, _BF), ("ind", 1024, _BF), ("off", 64, _U16), ("mk", 960, _BF), ("co", 960, _BF),
                       ("ES", 256, _BF), ("EC", 256, _BF), ("db4", 960, _BF), ("db5", 960, _BF), ("loff", 4, _U16),
                       ("F", 512, _BF), ("voff", 4, _U16), ("toff", 4, _U16), ("da1", 832, _BF), ("db1", 832, _BF), ("da2", 768, _BF),
                       ("db2", 768, _BF), ("da3", 960, _BF), ("db3", 960, _BF), ("T1", 832, _BF), ("T2", 768, _BF), ("T3", 960, _BF)):
        SCRATCH[_n + _h] = ("sbuf", [128, _c], _d)
    for _x in "LC":
        for _t in (0, 1, 2):
            SCRATCH["s%d%s%s" % (_t, _x, _h)] = ("sbuf", [128, 64], _F32 if _x == "L" and _t < 2 else _BF)
    for _n in ("pU", "pV", "pD", "pE"):
        SCRATCH[_n + _h] = ("psum", [128, 512], _F32)


def rank_program(g, core, T, topo):
    rank = T.rank_of(core)
    helper = {}
    for c in T.cores:
        helper[c] = [x for x in topo.cores_of(c) if topo.die(x) == topo.die(c) and x not in T.cores and x not in helper.values()][0]
    if rank is None:
        for c in [c for c in T.cores if helper[c] == core]:
            rid, pid = topo.addr(c)[:2]
            n, sent = len(topo.engines(core, c)), 0
            for t in range(3):
                for h in "AB":
                    if OPT["nf"][h]:
                        g.wait_ge(T.sem["fa%d%s" % (t, h)], n)
                        g.remote_dma(T["Y" + h][:, 4096 + 1024 * t:5120 + 1024 * t], T["Y" + h][:, 1024 * t:1024 * t + 1024], T.sem["fb%d%s" % (t, h)],
                                     T.sem.loc, pid, rid, topo.mask(core, c))
                        sent += n
            if sent:
                g.wait_ge(T.sem.loc, sent)
        return
    NH = len(topo.engines(core, helper[core]))
    N = len(T.cores)
    TILE, ENDS = TILES[OPT["tiles"]]
    WID = {q: a - b + 2 for q, (a, b) in ENDS.items()}
    RR = {q: list(range(a, b, -1)) + [17 + b] for q, (a, b) in ENDS.items()}
    eng = {"v": g.vector, "s": g.scalar, "t": g.tensor, "y": g.sync, "g": g}
    qsem = {"v": "sv", "s": "ss", "t": "st_", "g": "sg"}
    ops = []
    lastw, readers, bank = {}, {}, {}
    ndma, loc = [0], [0]

    def B(name, a=0, b=None, step=1):
        big, at, c = _PACK[name] if name in _PACK else (name, 0, SCRATCH[name][1][1])
        e = c if b is None else b
        return T[big][:, at + a:at + e:step] if step != 1 else T[big][:, at + a:at + e]

    def col(name):
        j = _COL.index(name)
        return T.col[:, j:j + 1]

    def qk(k):
        return T.col[:, 16 + TILE[k]:17 + TILE[k]]

    def half(l):
        return T.col[:, 24 + l:25 + l]

    def mat(name):
        j = _MAT.index(name)
        return T.mat[:, 128 * j:128 * j + 128]

    def rm(r):
        return T.Rm[:, 128 * r:128 * r + 128]

    def win(Z, m):
        return Z[:, 15 - m:143 - m]

    NB = {h: 7 - (OPT["nf"][h] or a) for h, a in OPT["na"].items()}

    def slot(h, k):
        a, b = OPT["na"][h], NB[h]
        if OPT["nf"][h]:
            return (T["z" + h], 1, 1024 * k) if k < OPT["nf"][h] else (T["Y" + h], b, 1 + k - OPT["nf"][h])
        if k < a:
            return T["z" + h], a, k
        v = (a - 1) * b
        return T["Y" + h], a * b, [p for p in range(v % a, a * b, a) if p != v][k - a]

    def add(q, cost, fns, r=(), w=(), banks=(), sem=None, extra=(), after=()):
        k = len(ops)
        deps = set(extra)
        for x in r:
            if x in lastw:
                deps.add(lastw[x])
            readers.setdefault(x, []).append(k)
        for x in w:
            if x in lastw:
                deps.add(lastw[x])
            deps.update(readers.get(x, ()))
            lastw[x] = k
            readers[x] = []
        for x in banks:
            st = bank.setdefault(x, [None, [], []])
            if st[0] != q:
                st[0], st[1], st[2] = q, st[2], []
            deps.update(st[1])
            st[2].append(k)
        deps.discard(k)
        ops.append({"q": q, "cost": cost, "fns": fns, "deps": deps, "all": deps | set(after), "sem": sem, "name": w[0] if w else "-"})
        return k

    def V(n, fn, r, w, banks=(), **kw):
        return add("v", (0.002, max(64, n), 0), [fn], r, w, banks, **kw)

    def S(n, fn, r, w, banks=()):
        return add("s", (0.03, max(64, n), 0), [fn], r, w, banks)

    def P(cols, fns, r, w, banks=(), **kw):
        return add("t", (0.002, cols, 0), fns, r, w, banks, **kw)

    def TS(out, in0, s1, s2, o0, o1=None):
        if o1 is None:
            return lambda: g.vector.tensor_scalar(out, in0, s1, None, o0)
        return lambda: g.vector.tensor_scalar(out, in0, s1, s2, o0, o1)

    def TT(out, a, b, op):
        return lambda: g.vector.tensor_tensor(out, a, b, op)

    def CP(out, a):
        return lambda: g.vector.tensor_copy(out, a)

    def MS(ap, c):
        return lambda: g.vector.memset(ap, c)

    def SCAN(out, d0, d1, o0, o1, first=0.0):
        return lambda: g.vector.tensor_tensor_scan(out, d0, d1, first, o0, o1)

    def ACT(out, in_, f, **kw):
        return lambda: g.scalar.activation(out, in_, f, **kw)

    def MM(out, l, r, a, z):
        return lambda: g.tensor.matmul(out, l, r, a, z)

    def SUM(out, pairs):
        return [MM(out, l, r, j == 0, j == len(pairs) - 1) for j, (l, r) in enumerate(pairs)]

    def LIN(q, out, in_, a, b, r, w, banks=()):
        if q == "v":
            return V(64, TS(out, in_, a, b, O.mult, O.add), r, w, banks)
        return S(64, ACT(out, in_, AF.Copy, scale=a, bias=b), r, w, banks)

    def gather(q, out, window, offs, n, r, w):
        fn = (lambda: g.scalar.activation(out, window.indirect(offs), AF.Copy)) if q == "s" else (lambda: g.vector.tensor_copy(out, window.indirect(offs)))
        return add(q, (0.065, 0, n), [fn], r, w)

    def dma(q, pairs, r, w, cost=2.2):
        s = "d%d" % ndma[0]
        ndma[0] += 1
        return add(q, cost, [lambda o_=o_, i_=i_: eng[q].dma_start(o_, i_) for o_, i_ in pairs], r, w, sem=(s, 16 * len(pairs)))

    def aff(out, in_, pat, cmp, base, cm, r, w, n=128):
        return add("g", (0.17, 2 * n, 0), [lambda: g.affine_select(out, in_, pat, cmp, 0.0, base, cm)], r, w)

    def iota(out, pat, base, n, w):
        add("g", (0.13, 2 * n, 0), [lambda: g.iota(out, pat, base, 0, allow_small_or_imprecise_dtypes=True)], (), w)

    NE = min(len(topo.engines(core, c)) for c in T.cores if c != core)

    def send(out, in_, sem, hop, r, w):
        dst = T.cores[(rank + hop) % N]
        rid, pid = topo.addr(dst)[:2]
        lanes = sum(1 << e for e in topo.engines(core, dst)[:NE])
        loc[0] += NE
        k = add("g", OPT["issue"], [lambda: g.remote_dma(out, in_, T.sem[sem], T.sem.loc, pid, rid, lanes)], r, (), sem=("loc", None))
        return add("r", OPT["fly"], [], (), w, sem=(sem, NE), extra=(k,))

    def spread(h):
        if h not in OPT["cmpv"]:
            dma("y", [(T["F" + h][:, 64 * j:64 * j + 64], T["F" + h][:, 0:64]) for j in range(1, 8)], ("F" + h,), ("Fr" + h,), 2.6)

    dma("y", [(T.X[:, 0:4096], T.x[:])], (), ("X",), 6.0)
    dma("s", [(T.st0[:], T.st[:])], (), ("st0",))
    dma("s", [(T.L0[:], T.sp[:])], (), ("L0A", "L0B"))
    dma("s", [(T.wts[:], T.wt[:])], (), ("wts",))
    dma("s", [(T.C0[:], T.ch[:])], (), ("C0A", "C0B"))
    for hi, h in enumerate("AB"):
        dma("y", [(T["F" + h][:, 0:64], T.fl[:, H2 * hi:H2 * hi + H2])], (), ("F" + h,))
        spread(h)
    send(T.st1[:], T.st0[:], "arst1", 1, ("st0",), ("st1",))
    send(T.st2[:], T.st0[:], "arst2", 2, ("st0",), ("st2",))
    if OPT["x2"] == "v":
        V(2048, CP(T.X[:, 4096:8192], T.X[:, 0:4096]), ("X",), ("X2",))
    else:
        dma("y", [(T.X[:, 4096:8192], T.x[:])], ("X",), ("X2",), 4.0)
    ones = T.ones[:, 0:128]
    LN3 = math.log(3.0)
    add("g", 0.14, [lambda: g.iota(T.pI[:], [[0, 1]], 0, 1)], (), ("pI",))
    iota(T.jrow[:], [[1, 18]], -1, 18, ("jrow",))
    iota(T.il0[:], [[16, 4]], 0, 4, ("il0",))
    V(64, MS(ones, 1.0), (), ("ones",))
    V(416, MS(T.ones[:, 128:960], 1.0), (), ("onesw",))
    V(1, TS(T.aI[:], T.pI[:], 15, None, O.bitwise_and), ("pI",), ("aI",))
    V(1, CP(col("qc"), T.aI[:]), ("aI",), ("qc",))
    for name, a, b in (("q8", 8.0, 0.0), ("kb", -LN3, 2 * LN3), ("qA", float(NB["A"]), 0.0), ("qB", float(NB["B"]), 0.0),
                       ("c0", -65536.0, 983039.0 + NB["A"]), ("c1", -65536.0, 983039.0 + NB["B"]), ("c2", -65536.0, 983040.0 + 8192),
                       ("c3", -65536.0, 983040.0 + 10240), ("c4", 0.0, 0.0), ("c5", 0.0, 2048.0), ("one", 1.0, -1.0),
                       ("c6", -65536.0, 983040.0 + 4148), ("c7", -65536.0, 983040.0 + 4212)):
        V(1, TS(col(name), col("qc"), a, b, O.mult, O.add), ("qc",), (name,))
    for q in RR:
        V(1, TS(T.col[:, 16 + q:17 + q], col("qc"), -1.0 - RR[q][0], None, O.add), ("qc",), ("qk%d" % q,))
    V(64, MS(mat("k-3"), -3.0 / 128), (), ("k-3",))
    V(64, MS(mat("k1"), 1.0 / 128), (), ("k1",))
    V(5, TS(T.col[:, 24:29], T.jrow[:, 0:5], -1.0, -0.5, O.mult, O.add), ("jrow",), ("half",))
    V(1, MS(T.col[:, 30:31], 1.0), (), ("onec",))
    V(1, TS(col("iz"), col("qc"), 0.0, None, O.is_equal), ("qc",), ("iz",))
    V(1, CP(col("w"), T.wts[:]), ("wts",), ("w",))
    aff(T.bm0[:], ones, [[-16, 8], [0, 16]], O.is_ge, 0, 1, ("ones",), ("bm0",))
    aff(T.bm[:], T.bm0[:], [[16, 8], [0, 16]], O.is_ge, 15, -1, ("bm0",), ("bm",))
    aff(T.idn[:], ones, [[-1, 128]], O.is_equal, 0, 1, ("ones",), ("idn",))
    V(4, TS(T.il[:], T.il0[:], col("qc"), None, O.add), ("il0", "qc"), ("il",))
    for out, a, c, w in ((T.Kv[:, 0:4], 16.0 * NB["A"], "c0", "KvA"), (T.Kv[:, 4:8], 16.0 * NB["B"], "c1", "KvB"), (T.Kt[:, 0:4], 32.0, "c2", "KtA"), (T.Kt[:, 4:8], 32.0, "c3", "KtB"),
                         (T.Kt[:, 8:12], 32.0, "c4", "KlA"), (T.Kt[:, 12:16], 32.0, "c5", "KlB"), (T.Kv[:, 8:12], 1.0, "c6", "KsA"),
                         (T.Kv[:, 12:16], 1.0, "c7", "KsB")):
        V(4, TS(out, T.il[:], a, col(c), O.mult, O.add), ("il", c), (w,))
    V(18, TS(T.cqx[:], T.jrow[:], col("qc"), None, O.is_equal), ("jrow", "qc"), ("cqx",))
    V(17, TT(T.dif[:], T.cqx[:, 1:18], T.cqx[:, 0:17], O.subtract), ("cqx",), ("dif",))
    V(17, TS(T.dif8[:, 0:17], T.dif[:], 8.0, None, O.mult), ("dif",), ("dif8a",))
    V(4, TS(T.dif8[:, 17:21], T.cqx[:, 1:5], 8.0, None, O.mult), ("cqx",), ("dif8b",))
    jobs = [r for q in sorted(RR) for r in RR[q]]
    jobs = sorted(set(jobs), key=jobs.index)
    for j, r in enumerate([17] + jobs):
        tok = ("bm", "dif8b" if r > 16 else "dif8a")
        if j % 3:
            V(64, TS(rm(r), T.bm[:], T.dif8[:, r:r + 1], None, O.mult), tok, ("Rm%d" % r,))
        else:
            S(128, ACT(rm(r), T.bm[:], AF.Copy, scale=T.dif8[:, r:r + 1]), tok, ("Rm%d" % r,))
    V(72, MS(T.Wz[:], 0.0), (), ("Wz",))
    V(8, TS(T.Wz[:, 15:143:16], T.bm[:, 0::16], col("w"), None, O.mult), ("bm", "w"), ("Wz",))
    V(72, MS(T.Ez[:], 0.0), (), ("Ez",))
    V(8, TS(T.Ez[:, 15:143:16], T.bm[:, 0::16], 8.0, None, O.mult), ("bm",), ("Ez",))
    kc = _MAT.index("kc") * 128
    V(64, MS(T.mat[0:64, kc:kc + 128], -512.0), (), ("kc0",))
    V(64, MS(T.mat[64:128, kc:kc + 128], 0.0625), (), ("kc1",))
    V(64, MS(mat("ke"), 1.0 / 65536), (), ("ke",))
    V(64, MS(mat("kq"), -1.0 / 512), (), ("kq",))
    aff(T.tri[:], T.bm[:], [[1, 128]], O.is_ge, 0, -1, ("bm",), ("tri",))
    for l in range(1, 5):
        aff(T.shm[:, (l - 1) * 128:l * 128], T.bm[:], [[-1, 128]], O.is_equal, -l, 1, ("bm",), ("shm%d" % l,))
    for name, src, tok, a in (("nid", T.idn[:], "idn", -1.0), ("hid", T.idn[:], "idn", 0.5), ("hs4", T.shm[:, 384:512], "shm4", 0.5),
                              ("bA", T.bm[:], "bm", "qA"), ("bB", T.bm[:], "bm", "qB"), ("bn", T.bm[:], "bm", -8192.0), ("b256", T.bm[:], "bm", 256.0),
                              ("n256", T.bm[:], "bm", -256.0), ("hb", T.bm[:], "bm", 0.5), ("Wb", T.bm[:], "bm", "w")):
        V(64, TS(mat(name), src, col(a) if a in _COL else a, None, O.mult), (tok, a) if a in _COL else (tok,), (name + "m" if name in ("bA", "bB") else name,))
    V(128, CP(T.b8[:], T.bm[:]), ("bm",), ("b8",))
    for q in RR:
        S(128, ACT(mat("q%d" % q), T.idn[:], AF.Copy, scale=T.col[:, 16 + q:17 + q]), ("idn", "qk%d" % q), ("q%dm" % q,))
    for l in range(1, 5):
        V(256, TT(T.hsd[:, (l - 1) * 128:l * 128], T.shm[:, (l - 1) * 128:l * 128],
                  T.idn[:] if l == 1 else T.shm[:, (l - 2) * 128:(l - 1) * 128], O.subtract),
          ("shm%d" % l, "idn" if l == 1 else "shm%d" % (l - 1)), ("hsd%d" % l,))
    V(256, TS(T.hsh[:], T.hsd[:], 0.5, None, O.mult), ("hsd1", "hsd2", "hsd3", "hsd4"), ("hsh",))
    for n in sorted({OPT["na"][h] for h in "AB" if not OPT["nf"][h]} | set(NB.values())):
        iota(T["mz%d" % n][:], [[0, 256], [256, n]], 0, 256 * n, ("mz%d" % n,))
    iota(T.jj[:], [[1, 128]], 0, 128, ("jj",))
    iota(T.j16[:], [[0, 8], [1, 16]], 0, 128, ("j16",))
    digit = {k: 3.0 * 4 ** (5 - k) if k < 5 else 4.0 for k in range(1, 6)}
    for k in digit:
        S(128, ACT(mat("a%d" % k), T.idn[:], AF.Copy, scale=digit[k]), ("idn",), ("a%d" % k,))
    V(64, MS(mat("kd"), (8 - 4148 - sum(digit[k] * (k - RR[TILE[k]][0]) for k in digit)) / 128), (), ("kd",))
    for d in range(4):
        aff(T.shd[:, 128 * d:128 * d + 128], T.bm[:], [[-1, 128]], O.is_equal, d + 1, 1, ("bm",), ("shd%d" % d,))
    V(64, TS(T.dg0[:], T.j16[:], col("qc"), 65.0 * 65536, O.is_equal, O.mult), ("j16", "qc"), ("dg0",))
    V(64, TS(T.dg[:], T.dg0[:], -65536.0, None, O.add), ("dg0",), ("dg",))
    for hi, h in enumerate("AB"):
        for q in WID:
            n = WID[q]
            a, bs = "da%d%s" % (q, h), tuple("db%d%s" % (k, h) for k in range(1, 6) if TILE[k] == q)
            if q == 1:
                for x in (a,) + bs:
                    V(n * 32, MS(T[x][:, 0:64 * n], 1.0), (), (x,))
            else:
                dma("y", [(T[x][:, 0:64 * n], T.ones[:, 0:64 * n]) for x in (a,) + bs], ("ones", "onesw", "X"), (a,) + bs, 3.0)
            for b in bs:
                V(64, MS(T[b][:, 1:64 * n:n], 0.0), (), (b,))
            V(64, MS(T["T%d%s" % (q, h)][:, 0:64 * n:n], 0.0), (), ("T%dz%s" % (q, h),))

    def entry(k, h):
        q = TILE[k]
        n = WID[q]
        V(n * 32, SCAN(T["mk" + h][:, 0:64 * n], T["da%d%s" % (q, h)][:, 0:64 * n], T["db%d%s" % (k, h)][:, 0:64 * n], O.add, O.min, 1.0),
          ("da%d%s" % (q, h), "db%d%s" % (k, h)), ("mk" + h,))
        V(n * 32, SCAN(T["co" + h][:, 0:64 * n], T["mk" + h][:, 0:64 * n], T["T%d%s" % (q, h)][:, 0:64 * n], O.mult, O.add),
          ("mk" + h, "T%dz%s" % (q, h)) + tuple("T%d_%d%s" % (q, r, h) for r in RR[q]), ("co" + h,))
        if k < 5:
            LIN(OPT["w8"], B("w8" + h), T["co" + h][:, n - 1:64 * n:n], 1.0 / 32, 0.25, ("co" + h,), ("w8" + h,))

    def spans(n, a, b):
        for d in range(4):
            bk = "pEB" if n < 256 else ("pDB", "pEB")[d % 2]
            ps = T[bk][:, 64 * d:64 * d + n] if n < 256 else T[bk][:, 0:n]
            P(max(64, n), SUM(ps, [(T.shd[:, 128 * d:128 * d + 128], T.TB[:, a:a + n])]),
              ("shd%d" % d,) + tuple("TB%d_%d" % (n, e) for e in range(4)), ("tp%d_%d" % (n, d),), (bk,))
            if n == 256:
                S(n, ACT(T.TB[:, b + n * d:b + n * d + n], ps, AF.Identity, bias=T.col[:, 44 + d:45 + d]), ("tp%d_%d" % (n, d), "diz"), ("TB%d_%d" % (4 * n, d),), (bk,))
        for d in range(4 if n < 256 else 0):
            V(64, TS(T.TB[:, b + n * d:b + n * d + n], T.pEB[:, 64 * d:64 * d + n], T.col[:, 40 + d:41 + d], None, O.add), ("tp%d_%d" % (n, d), "diz"),
              ("TB%d_%d" % (4 * n, d),), ("pEB",))

    V(4, TS(T.col[:, 40:44], T.jrow[:, 1:5], col("iz"), None, O.mult), ("jrow", "iz"), ("diz",))
    V(4, TS(T.col[:, 44:48], T.col[:, 40:44], 1.0, None, O.add), ("diz",), ("diz",))
    V(4, CP(T.TB[:, 0:4], T.col[:, 40:44]), ("diz",), tuple("TB4_%d" % e for e in range(4)))
    V(4, MS(T.SP[:, 0:8], 0.0), (), ("SPz",))
    V(44, MS(T.SP[:, 4104:4148], 0.0), (), ("SPz",))
    for d in range(4):
        V(64, TS(T.SP[:, 8 + 1024 * d:136 + 1024 * d], ones, T.col[:, 44 + d:45 + d], None, O.mult), ("ones", "diz"), ("SP",))
    for c in (128, 512):
        dma("y", [(T.SP[:, 8 + 1024 * d + c * j:8 + 1024 * d + c * j + c], T.SP[:, 8 + 1024 * d:8 + 1024 * d + c]) for d in range(4) for j in range(1, 512 // c + (c > 128))],
            ("X",), ("SP",), 2.6)
    spans(4, 0, 4)
    spans(16, 4, 20)
    spans(64, 20, 84)

    for t in range(3):
        last = t == 2
        Cw, Lw, St = T["C%d" % t], T["L%d" % t], T["st%d" % t]
        for hi, h in enumerate("AB"):
            o = H2 * hi
            C, L, ct, lt = Cw[:, o:o + H2], Lw[:, o:o + H2], "C%d%s" % (t, h), "L%d%s" % (t, h)
            bV = "pV" + h
            pV = T[bV]
            if t:
                V(64, TS(T["pU" + h][:, 64:128], St[:, o:o + H2], T.acnt[:], None, O.add), ("st%d" % t, "acnt"), ("bs" + h,), ("pU" + h,))
                if h in OPT["fast"]:
                    V(64, TT(T["off" + h][:], L, T["pU" + h][:, 64:128], O.add), (lt, "bs" + h), ("off" + h,), ("pU" + h,))
                else:
                    V(64, TT(B("Q" + h), L, T["pU" + h][:, 64:128], O.add), (lt, "bs" + h), ("Q" + h,), ("pU" + h,))
                    V(64, TS(B("s1" + h), B("Q" + h), 4095, None, O.bitwise_and), ("Q" + h,), ("s1" + h,))
                    V(64, CP(T["off" + h][:], B("s1" + h)), ("s1" + h,), ("off" + h,))
            else:
                V(64, TS(B("base" + h), L, 613.0, None, O.mult), (lt,), ("base" + h,))
                V(128, TT(B("Q" + h), B("base" + h), St[:, o:o + H2], O.add), ("base" + h, "st%d" % t), ("Q" + h,))
                V(64, TS(B("s1" + h), B("Q" + h), 4095, None, O.bitwise_and), ("Q" + h,), ("s1" + h,))
                V(64, CP(T["off" + h][:], B("s1" + h)), ("s1" + h,), ("off" + h,))
            sc = 1.0 / 613 if t else 1.0
            S(64, ACT(T.SP[:, 4148 + o:4148 + o + H2], L, AF.Copy, scale=sc), (lt,), ("SP" + h,))
            P(64, SUM(pV[:, 0:64], [(rm(17), T.SP[:, 4148 + o:4148 + o + H2])]), ("SP" + h, "Rm17"), ("Lb" + h,), (bV,))
            V(64, TS(B("e0" + h), pV[:, 0:64], col("q8"), col("iz"), O.is_equal, O.subtract), ("Lb" + h, "q8", "iz"), ("e0" + h,), (bV,))
            V(128, TT(B("t0" + h), B("e0" + h), C, O.mult), ("e0" + h, ct), ("t0" + h,))
            P(128, SUM(pV[:, 64:128], [(rm(17), C), (win(T.Ez, 0), B("t0" + h))]), (ct, "t0" + h, "Rm17", "Ez"), ("c80" + h,), (bV,))
            LIN(OPT["c0"], B("w8" + h), pV[:, 64:128], 1.0 / 32, 0.125, ("c80" + h,), ("w8" + h,), (bV,))
            LIN(OPT["c0"], B("c0" + h), pV[:, 64:128], 1.0, -4.0, ("c80" + h,), ("c0" + h,), (bV,))
            S(64, ACT(B("Kp" + h), L, AF.Exp, scale=16 * LN3 * sc, bias=col("kb")), (lt, "kb"), ("Kp" + h,))
            S(64, ACT(pV[:, 448:512], L, AF.Copy, scale=sc), (lt,), ("L" + h,), (bV,))
            for j0 in range(0, len(jobs), 8):
                bk = ("pD" + h, "pE" + h)[j0 // 8 % 2]
                rs = jobs[j0:j0 + 8]
                for c in range(0, len(rs), 2):
                    P(128, [MM(T[bk][:, 64 * j:64 * j + 64], rm(rs[j]), C, True, True) for j in (c, c + 1)],
                      (ct, "Rm%d" % rs[c], "Rm%d" % rs[c + 1]), ("dM%d%s" % (c // 2, bk),), (bk,))
                for q in sorted(RR):
                    for j, r in enumerate(rs):
                        if r in RR[q]:
                            n = WID[q]
                            out, e = T["T%d%s" % (q, h)][:, 1 + RR[q].index(r):64 * n:n], OPT["te"][h + str(q)]
                            src = [p_ for p_ in sorted(RR) if p_ < q and r in RR[p_]]
                            if e[0] == "g" and src:
                                aff(out, T["T%d%s" % (src[0], h)][:, 1 + RR[src[0]].index(r):64 * WID[src[0]]:WID[src[0]]], [[0, 64]], O.is_equal, 0, 0,
                                    ("T%d_%d%s" % (src[0], r, h),), ("T%d_%d%s" % (q, r, h),), 64)
                            else:
                                LIN("v" if e[-1] == "v" else "s", out, T[bk][:, 64 * j:64 * j + 64], 1.0, -4.0 if r > 16 else 0.0, ("dM%d%s" % (j // 2, bk),),
                                    ("T%d_%d%s" % (q, r, h),), (bk,))
        if t == 0:
            spans(256, 84, 344)
            dma("y", [(T.SP[16 * a + d + 1:16 * a + 16, 8 + 1024 * d:1032 + 1024 * d], T.TB[16 * a:16 * a + 15 - d, 344:1368]) for d in range(4) for a in range(8)],
                tuple("TB1024_%d" % e for e in range(4)), ("SP",), 4.0)
        if last:
            for hi, h in enumerate("AB"):
                pE, prev = T["pE" + h], ()
                for c in range(8):
                    prev = (P(256, [MM(pE[:, 0:64], T.idn[:], T.X[:, 2048 * hi + j:2048 * hi + 2048:32], j == 0, j == 31) for j in range(4 * c, 4 * c + 4)],
                              ("X", "idn"), ("sums%d%s" % (c, h),), ("pE" + h,), after=prev),)
                S(64, ACT(B("S0" + h), pE[:, 0:64], AF.Copy), tuple("sums%d%s" % (c, h) for c in range(8)), ("S0" + h,), ("pE" + h,))
        for k in range(6):
            for hi, h in enumerate("AB"):
                bU, bV = "pU" + h, "pV" + h
                pV = T[bV]
                z, zr, zs = slot(h, k)
                z0 = zs if zr == 1 else 0
                wide = k > 0 or (t > 0 and h in OPT["fast"])
                nv = OPT["gv"].get((k, h), 0)
                zk = ()
                parts = [("s", 0, 64 - nv), ("v", 64 - nv, 64)]
                if OPT["gs"]:
                    parts = [("s", 0, 32), ("s", 32, 64 - nv), ("v", 64 - nv, 64)]
                if k == 5 and h in OPT["c5"]:
                    parts = [("s", a, a + 16) for a in range(0, 64, 16)]
                for q, a, b in parts:
                    if a < b:
                        zk += ("z%d_%d_%d%s" % (k, a, b, h),)
                        gather(q, z[:, 16 * zr * a + zs:16 * zr * b + z0:zr], T.X[:, 0:8192 if wide else 4096], T["off" + h][:, a:b], 16 * (b - a),
                               ("X", "off" + h) + (("X2",) if wide else ()), zk[-1:])
                y, by = T[bU][:, 0:64], bU
                k0 = P(128, [MM(y, mat("kc"), T.ones[:, 0:64], True, False), MM(y, mat("ke"), T.ones[:, 0:64], False, False)],
                       ("kc0", "kc1", "ke", "ones"), ("u0" + h,), (by,))
                ut = ("u0" + h,)
                for c in range(0, 16, OPT["um"]):
                    ut += ("u_%d%s" % (c, h),)
                    k0 = P(64 * OPT["um"], [MM(y, win(T.Wz, m), z[:, zr * m + zs:1024 * zr + z0:16 * zr], False, m == 15) for m in range(c, c + OPT["um"])],
                           zk + ("Wz",), ut[-1:], (by,), after=(k0,))
                na, nb = OPT["na"][h], NB[h]
                if k == OPT["nf"][h] - 1:
                    zt = tuple(x for x in lastw if x[0] == "z" and x[-1] == h and int(x[1]) <= k)
                    rid, pid = topo.addr(helper[core])[:2]
                    tr = RemoteDMATransfer(dst_ids=[DstId(rid=rid, pnc=pid)], dma_engine_mask=topo.mask(core, helper[core]), remote_sem=T.sem["fa%d%s" % (t, h)],
                                           srcs=[z[:, 1024 * j:1024 * j + 1024] for j in range(k + 1)], dsts=[T["Y" + h][:, 1024 * t:1024 * t + 1024]], alu_op=2)
                    kf = add("g", 0.8, [lambda tr=tr, s_=T.sem["fl%d%s" % (t, h)]: g.remote_dma_fused([tr], local_sem=s_)], zt, (), sem=("loc", None))
                    add("r", 2.0, [], zt, (), sem=("fl%d%s" % (t, h), NH), extra=(kf,))
                    add("r", OPT["fold"], [], (), ("M%d%s" % (t, h),), sem=("fb%d%s" % (t, h), NH), extra=(kf,))
                if k == na - 1 and k < 5 and not OPT["nf"][h]:
                    zt = tuple(x for x in lastw if x[0] == "z" and x[-1] == h and int(x[1]) < na)
                    c = 1024 // OPT["chunks"] * na
                    for j in range(OPT["chunks"]):
                        V(c // 2, SCAN(T["Y" + h][:, c * nb * j:c * nb * (j + 1):nb], T["mz%d" % na][:, 0:c], T["z" + h][:, c * j:c * (j + 1)],
                                       O.min, O.max), zt + ("mz%d" % na,), ("Y%d%s" % (j, h),))
                if k < 5:
                    V(64, TT(B("ab" + h, 0, 64), y, B("w8" + h), O.mult), ut + ("w8" + h,), ("a0" + h,), (bU,))
                    V(64, TS(B("ab" + h, 64, 128), y, 37.0, -149.0 - 37.0 / 512, O.mult, O.add), ut, ("b0" + h,), (bU,))
                    V(128, TS(B("am" + h), B("ab" + h), 4095, None, O.bitwise_and), ("a0" + h, "b0" + h), ("am" + h,))
                    V(128, TT(T["off" + h][:], B("am" + h, 0, 64), B("am" + h, 64, 128), O.add), ("am" + h,), ("off" + h,))
                n = WID.get(TILE[k], 1)
                V(64, TT(B("k8" + h), y, T["co" + h][:, n - 1:64 * n:n] if k else B("c0" + h), O.add), ut + ("co" + h if k else "c0" + h,), ("k8" + h,), (bU,))
                V(64, TS(B("n1" + h), B("k8" + h), 3, 3, O.arith_shift_right, O.bitwise_and), ("k8" + h,), ("n1" + h,))
                if k < 5:
                    q = TILE[k + 1]
                    n2, da, db = WID[q], "da%d%s" % (q, h), "db%d%s" % (k + 1, h)
                    D = T[db][:, 0:64 * n2:n2]
                    if k == 0:
                        V(64, TS(D, B("n1" + h), 1.0 - RR[q][0], None, O.add), ("n1" + h,), (db,))
                    else:
                        V(64, TT(D, B("n1" + h), pV[:, 128:192], O.add), ("n1" + h, "Dp" + h), (db,), (bV,))
                    if k == 0:
                        V(64, TS(B("b" + h), B("n1" + h), col("one"), None, O.is_ge), ("n1" + h, "one"), ("b" + h,))
                    else:
                        V(64, TT(B("b" + h), B("n1" + h), pV[:, 192:256], O.is_ge), ("n1" + h, "Dp" + h), ("b" + h,), (bV,))
                    V(64, TT(T[da][:, 1:64 * n2:n2], B("b" + h), pV[:, 448:512], O.mult), ("b" + h, "L" + h), (da,), (bV,))
                    if k < 4:
                        on = "k%d" % (1 - RR[TILE[k + 2]][0] + RR[q][0])
                        P(256, SUM(pV[:, 128:192], [(mat(on), T.ones[:, 0:64]), (T.idn[:], D)]) + SUM(pV[:, 192:256], [(mat("q%d" % q), T.ones[:, 0:64]), (mat("nid"), D)]),
                          (db, on, "idn", "ones", "nid", "q%dm" % q), ("Dp" + h,), (bV,))
                    entry(k + 1, h)
                else:
                    P(448, SUM(pV[:, 384:448], [(mat("kd"), T.ones[:, 0:64]), (mat("nid"), T.jj[:, 64 * hi:64 * hi + 64])]
                               + [(mat("a%d" % j), T["db%d%s" % (j, h)][:, 0:64 * WID[TILE[j]]:WID[TILE[j]]]) for j in range(1, 6)]),
                      ("kd", "nid", "jj", "ones") + tuple("a%d" % j for j in range(1, 6)) + tuple("db%d%s" % (j, h) for j in range(1, 6)), ("cod" + h,), (bV,))
                    if h in OPT["cmpv"]:
                        P(64, SUM(pV[:, 320:384], [(T.idn[:], T["F" + h][:, 0:64])]), ("F" + h, "idn"), ("Fp" + h,), (bV,))
                    V(64, TT(pV[:, 384:448], B("n1" + h), pV[:, 384:448], O.add), ("n1" + h, "cod" + h), ("code" + h,), (bV,))
        for hi, h in enumerate("AB"):
            o = H2 * hi
            C, L, ct, lt = Cw[:, o:o + H2], Lw[:, o:o + H2], "C%d%s" % (t, h), "L%d%s" % (t, h)
            bU, bV, bD, bE = ("p" + x + h for x in "UVDE")
            pU, pV, pD, pE = T[bU], T[bV], T[bD], T[bE]
            sL, sC = "s%dL%s" % (t, h), "s%dC%s" % (t, h)
            acc, F, VS = B("acc" + h), T["F" + h][:, 0:64], T["VS" + h]
            na, nb = OPT["na"][h], NB[h]
            zt = tuple(x for x in lastw if x[0] == "z" and x[-1] == h and int(x[1]) >= (OPT["nf"][h] or na))
            zall = zt
            nf = OPT["nf"][h]
            for j in range(4):
                zt = tuple(x for x in zall if int(x[:-1].split("_")[1]) < 16 * j + 16 and int(x[:-1].split("_")[2]) > 16 * j)
                if nf:
                    out, in_ = T["Y" + h][:, 256 * nb * j:256 * nb * (j + 1):nb], T["Y" + h][:, 4096 + 1024 * t + 256 * j:4352 + 1024 * t + 256 * j]
                    if h in OPT["mg"]:
                        aff(out, in_, [[0, 256]], O.is_equal, 0, 0, ("M%d%s" % (t, h),), ("Y%d%s" % (j, h),), 256)
                    else:
                        V(128, CP(out, in_), ("M%d%s" % (t, h),), ("Y%d%s" % (j, h),))
                    V(128 * nb, SCAN(VS[:, 256 * nb * j:256 * nb * (j + 1)], T["mz%d" % nb][:], T["Y" + h][:, 256 * nb * j:256 * nb * (j + 1)], O.min, O.max),
                      zt + ("mz%d" % nb, "Y%d%s" % (j, h)), ("VS%d%s" % (j, h),))
                    continue
                src = T["z" + h][:, 1536 * j:1536 * (j + 1)] if na == 6 else T["Y" + h][:, 256 * na * nb * j + (na - 1) * nb % na:256 * na * nb * (j + 1):na]
                V(128 * nb, SCAN(VS[:, 256 * nb * j:256 * nb * (j + 1)], T["mz%d" % nb][:], src, O.min, O.max),
                  zt + ("mz%d" % nb,) + (() if na == 6 else tuple("Y%d%s" % (i, h) for i in range(OPT["chunks"] // 4 * j, OPT["chunks"] // 4 * (j + 1)))), ("VS%d%s" % (j, h),))
            vt = tuple("VS%d%s" % (j, h) for j in range(4))
            for c, bk in enumerate((bD, bE)):
                ps = T[bk]
                if h in OPT["cmpv"]:
                    for m in range(8 * c, 8 * c + 8):
                        V(64, TT(T["ind" + h][:, 64 * m:64 * m + 64], VS[:, nb * m + nb - 1:1024 * nb:16 * nb], pV[:, 320:384], O.is_ge), vt + ("Fp" + h,),
                          ("ind%d_%d%s" % (c, m, h),), (bV,))
                    continue
                k0 = P(512, [MM(ps[:], mat("nid"), T["F" + h][:], True, False)], ("F" + h, "Fr" + h, "nid"), ("VF" + bk,), (bk,))
                for e in (0, 4):
                    k0 = P(256, [MM(ps[:, 64 * j:64 * j + 64], T.idn[:], VS[:, nb * (8 * c + j) + nb - 1:1024 * nb:16 * nb], False, j == 7) for j in range(e, e + 4)],
                           vt + ("idn",), ("VG%d%s" % (e, bk),), (bk,), after=(k0,))
                S(512, ACT(T["ind" + h][:, 512 * c:512 * c + 512], ps[:], AF.Sign, bias=half(0)), ("VF" + bk, "VG0" + bk, "VG4" + bk, "half"), ("ind%d%s" % (c, h),), (bk,))
            prev = ()
            for c in range(4):
                prev = (P(256, [MM(pD[:, 0:64], win(T.Ez, m), T["ind" + h][:, 64 * m:64 * m + 64], m == 0, m == 15) for m in range(4 * c, 4 * c + 4)],
                          ("ind%d%s" % (c // 2, h), "Ez") + tuple("ind%d_%d%s" % (c // 2, m, h) for m in range(4 * c, 4 * c + 4)), ("cnt%d%s" % (c, h),), (bD,), after=prev),)
            V(64, TS(pD[:, 0:64], pD[:, 0:64], 68.0 if h in OPT["cmpv"] else 8.0, None, O.is_ge), tuple("cnt%d%s" % (c, h) for c in range(4)), ("f" + h,), (bD,))
            V(64, TT(B("E" + h), pD[:, 0:64], B("Kp" + h), O.mult), ("f" + h, "Kp" + h), ("E" + h,), (bD,))
            P(64, SUM(pD[:, 64:128], [(mat("hb"), B("E" + h))]), ("E" + h, "hb"), ("Es" + h,), (bD,))
            V(64, TT(acc, B("E" + h), pD[:, 64:128], O.is_gt), ("E" + h, "Es" + h), ("acc" + h,), (bD,))
            segs = [mat("b" + h)] + ([] if last else [mat("bn")])
            ns = 64 * len(segs)
            P(ns, [MM(pD[:, 128 + 64 * j:192 + 64 * j], m_, acc, True, True) for j, m_ in enumerate(segs)], ("acc" + h, "b" + h + "m", "bn"), ("sg" + h,), (bD,))
            V(ns, SCAN(B("wr" + h, 0, ns), T.dg[:, 0:ns], pD[:, 128:128 + ns], O.add, O.min), ("sg" + h, "dg"), ("wr" + h,), (bD,))
            V(4, TT(T["voff" + h][:], B("wr" + h, 15, 64, 16), T.Kv[:, 4 * hi:4 * hi + 4], O.add), ("wr" + h, "Kv" + h), ("voff" + h,))
            gather("v", B("Vsel" + h), VS[:, 0:1024 * nb], T["voff" + h][:], 64, vt + ("voff" + h,), ("Vsel" + h,))
            if not last:
                V(4, TT(B("tb" + h), B("wr" + h, 79, 128, 16), T.Kt[:, 4 * hi:4 * hi + 4], O.add), ("wr" + h, "Kt" + h), ("tb" + h,))
            if h in OPT["hp"]:
                prev = ()
                for c in range(0, 16, 4):
                    prev = (P(256, [MM(pE[:, 0:64], win(T.Wz, m), VS[:, nb * m + nb - 1:1024 * nb:16 * nb], m == 0, m == 15) for m in range(c, c + 4)],
                              vt + ("Wz",), ("hT%d%s" % (c, h),), (bE,), after=prev),)
                V(64, TT(B("ah" + h), acc, pE[:, 0:64], O.mult), ("acc" + h,) + tuple("hT%d%s" % (c, h) for c in range(0, 16, 4)), ("ah" + h,), (bE,))
                P(256, SUM(pE[:, 448:512], [(T.b8[:], B("ah" + h))]), ("ah" + h, "b8"), ("hc" + h,), (bE,))
                V(64, SCAN(B("hw" + h), T.dg[:, 0:64], pE[:, 448:512], O.add, O.min), ("hc" + h, "dg"), ("hw" + h,), (bE,))
                if last:
                    P(64, SUM(pD[:, 384:448], [(T.bm[:], acc)]), ("acc" + h, "bm"), ("hb" + h,), (bD,))
            else:
                P(128 if last else 64, SUM(pD[:, 320:384], [(mat("Wb"), B("Vsel" + h))]) + (SUM(pD[:, 384:448], [(T.bm[:], acc)]) if last else []),
                  ("Vsel" + h, "Wb", "acc" + h, "bm"), ("hb" + h,), (bD,))
                V(64, SCAN(B("hw" + h), T.dg[:, 0:64], pD[:, 320:384], O.add, O.min), ("hb" + h, "dg"), ("hw" + h,), (bD,))
            V(4, TS(B("h1" + h), B("hw" + h, 15, 64, 16), 31, None, O.bitwise_and), ("hw" + h,), ("h1" + h,))
            V(4, TT(T["toff" + h][:], B("h1" + h), T.Kt[:, 8 + 4 * hi:12 + 4 * hi] if last else B("tb" + h), O.add), ("h1" + h, "tb" + h, "Kl" + h), ("toff" + h,))
            if not last:
                for a, x in ((0, "X"), (4096, "X2")):
                    add("v", (0.05, 240, 0), [lambda f_=T["toff" + h], i_=B("Vsel" + h), a_=a: g.vector.tensor_copy(T.X[:, a_:a_ + 12288].indirect(f_[:, 0:4]), i_)],
                        ("toff" + h, "Vsel" + h), (x, "Xw"))
            else:
                gather("v", B("xo" + h), T.X[:, 0:4096], T["toff" + h][:, 0:4], 64, ("X", "toff" + h), ("xo" + h,))
                V(64, TT(B("xd" + h), B("Vsel" + h), pD[:, 384:448], O.mult), ("Vsel" + h, "hb" + h), ("xd" + h,), (bD,))
                V(128, TT(pD[:, 448:512], B("xd" + h), B("S0" + h), O.add), ("xd" + h, "S0" + h), ("xs" + h,), (bD,))
                V(64, TT(B("xe" + h), B("xo" + h), pD[:, 384:448], O.mult), ("xo" + h, "hb" + h), ("xe" + h,), (bD,))
                V(64, TT(B("yss" + h), pD[:, 448:512], B("xe" + h), O.subtract), ("xe" + h, "xs" + h), ("yss" + h,), (bD,))
                dma("s", [(T.ys[:, o:o + H2], B("yss" + h))], ("yss" + h,), ())
            P(256, [MM(pE[:, 64 * l:64 * l + 64], T.hsh[:, 128 * l:128 * l + 128], C, True, True) for l in range(4)], (ct, "hsh"), ("SH" + h,), (bE,))
            V(64, TT(B("aL" + h), acc, pV[:, 448:512], O.mult), ("acc" + h, "L" + h), ("aL" + h,), (bV,))
            V(64, TT(B("ay" + h), acc, pV[:, 384:448], O.mult), ("acc" + h, "code" + h), ("ay" + h,), (bV,))
            P(64, SUM(pE[:, 256:320], [(T.tri[:], B("aL" + h))]), ("aL" + h, "tri"), ("sh" + h,), (bE,))
            for l in range(1, 5):
                S(64, ACT(T["ES" + h][:, 64 * l - 64:64 * l], pE[:, 256:320], AF.Sign, bias=half(l)), ("sh" + h, "half"), ("ES%d%s" % (l, h),), (bE,))
            V(256, TT(T["EC" + h][:], T["ES" + h][:], pE[:, 0:256], O.mult), ("SH" + h,) + tuple("ES%d%s" % (l, h) for l in range(1, 5)), ("EC" + h,), (bE,))
            new = [(mat("hid"), C), (mat("hs4"), C)] + [(T.idn[:], T["EC" + h][:, 64 * l:64 * l + 64]) for l in range(4)]
            P(384, SUM(pE[:, 320:384], new), ("EC" + h, "idn", "hid", "hs4", ct), ("cs" + h,), (bE,))
            S(64, ACT(T[sC][:], pE[:, 320:384], AF.Copy), ("cs" + h,), (sC,), (bE,))
            if not last:
                send(T["C%d" % (t + 1)][:, o:o + H2], T[sC][:], "arr%dC%s" % (t + 1, h), 1, (sC,), ("C%d%s" % (t + 1, h),))
            else:
                dma("y", [(T.yc[:, o:o + H2], T[sC][:])], (sC,), ())
            P(256, SUM(pU[:, 0:64], [(T.b8[:], B("ay" + h))]), ("ay" + h, "b8"), ("cb" + h,), (bU,))
            V(64, SCAN(B("wc" + h), T.dg[:, 0:64], pU[:, 0:64], O.add, O.min), ("cb" + h, "dg"), ("wc" + h,), (bU,))
            V(4, TT(T["loff" + h][:], B("wc" + h, 15, 64, 16), T.Kv[:, 8 + 4 * hi:12 + 4 * hi], O.add), ("wc" + h, "Ks" + h), ("loff" + h,))
            add("s", (0.065, 0, 64), [lambda o_=T[sL][:], f_=T["loff" + h][:], a_=1.0 if last else 613.0: g.scalar.activation(o_, T.SP[:].indirect(f_), AF.Copy, scale=a_)],
                ("loff" + h, "SPA", "SPB", "SPz", "SP"), (sL,))
            if not last:
                send(T["L%d" % (t + 1)][:, o:o + H2], T[sL][:], "arr%dL%s" % (t + 1, h), 1, (sL,), ("L%d%s" % (t + 1, h),))
            else:
                dma("y", [(T.yl[:, o:o + H2], T[sL][:])], (sL,), ())
            P(384, SUM(pV[:, 0:64], [(mat("hid"), F), (mat("b256"), acc), (mat("kq"), T.ones[:, 0:64]), (mat("hid"), B("Vsel" + h))])
              + SUM(pV[:, 64:128], [(T.idn[:], F), (mat("n256"), acc)]),
              ("F" + h, "acc" + h, "Vsel" + h, "hid", "idn", "b256", "n256", "kq", "ones"), ("fa" + h,), (bV,))
            V(64, TS(B("fr" + h), pV[:, 0:64], 12582912.0 - 256, -12582912.0, O.add, O.add), ("fa" + h,), ("fr" + h,), (bV,))
            if not last:
                V(64, TT(F, B("fr" + h), pV[:, 64:128], O.max), ("fr" + h, "fa" + h), ("F" + h,), (bV,))
                spread(h)
            else:
                V(64, TT(B("yfs" + h), B("fr" + h), pV[:, 64:128], O.max), ("fr" + h, "fa" + h), ("yfs" + h,), (bV,))
                dma("s", [(T.yf[:, o:o + H2], B("yfs" + h))], ("yfs" + h,), ())
            if hi and not last:
                P(128, SUM(T.pUA[:, 0:64], [(ones, B("accA")), (ones, acc)]), ("accA", "accB", "ones"), ("As",), ("pUA",))
                S(64, ACT(T.junk[:], T.pUA[:, 0:64], AF.Copy, accum_out=T.acnt[:]), ("As",), ("acnt", "junk"), ("pUA",))

    n = len(ops)
    succ, above = [[] for _ in range(n)], []
    for k, p in enumerate(ops):
        far = 0
        for d in p["all"]:
            far |= above[d]
        p["all"] = {d for d in p["all"] if not far >> d & 1}
        above.append(far | sum(1 << d for d in p["all"]))
        for d in p["all"]:
            succ[d].append(k)

    def gap(a, b):
        a, b = min(a, b), max(a, b)
        return 0.0 if a not in ops[b]["deps"] else OPT["ws"] if ops[a]["q"] == ops[b]["q"] else OPT["wx"]
    queue = [p["q"] for p in ops]

    def times(f, gr):
        c = [p["cost"][0] + 0.00083 * f * (p["cost"][1] + gr * p["cost"][2]) if isinstance(p["cost"], tuple) else p["cost"] for p in ops]
        return c, [0.0 if p["q"] == "r" else 0.06 * len(p["fns"]) if p["sem"] is not None and p["q"] in "sy" else c[k] for k, p in enumerate(ops)]
    cost, hold = times(OPT["f"], OPT["gr"])
    paces = [times(f, gr) + (1.0 / (f + 0.25 * gr),) for f, gr in OPT["paces"]]

    def replay(at):
        seq, total = sorted(range(n), key=lambda k: at[k]), 0.0
        for c, h, w in paces:
            end, free = [0.0] * n, dict.fromkeys("vstgyr", 0.0)
            for k in seq:
                s0 = free[queue[k]] if h[k] else 0.0
                for d, x in pred[k]:
                    if end[d] + x > s0:
                        s0 = end[d] + x
                if h[k]:
                    free[queue[k]] = s0 + h[k]
                end[k] = s0 + c[k]
            total += w * max(end)
        return total
    pred = [[(d, gap(d, k)) for d in sorted(p["all"])] for k, p in enumerate(ops)]
    next_ = [[(d, gap(d, k)) for d in succ[k]] for k in range(n)]

    def place(seq, before, back):
        at, end = [0.0] * n, [0.0] * n
        first, after = {q: [] for q in "vstgyr"}, {q: [] for q in "vstgyr"}
        for k in seq:
            s0, h = 0.0, hold[k]
            for d, w in before[k]:
                if end[d] + w > s0:
                    s0 = end[d] + w
            if back:
                s0 += cost[k] - h
            if h:
                a, b = first[queue[k]], after[queue[k]]
                j = m = len(a)
                while j and b[j - 1] > s0:
                    j -= 1
                while j < m and a[j] < s0 + h - 1e-9:
                    s0 = b[j]
                    j += 1
                a.insert(j, s0)
                b.insert(j, s0 + h)
            at[k] = s0
            end[k] = s0 + (h if back else cost[k])
        return at

    prio = [0.0] * n
    for k in range(n - 1, -1, -1):
        prio[k] = cost[k] + max([prio[s] + w for s, w in next_[k]], default=0.0)

    def tighten(seq):
        at = place(seq, pred, False)
        back = place(sorted(range(n), key=lambda k: (-(at[k] + cost[k]), -k)), next_, True)
        at = place(sorted(range(n), key=lambda k: (-(back[k] + hold[k]), k)), pred, False)
        span = max(at[k] + cost[k] for k in range(n))
        return span, at, span / (OPT["f"] + 0.25 * OPT["gr"]) + replay(at)

    if n not in PLAN:
        best = kept = tighten(sorted(range(n), key=lambda k: -prio[k]))
        rng = np.random.RandomState(OPT["seed"])
        kinds = sorted({p["name"][:2] + p["name"][-1] for p in ops})
        kind = np.array([kinds.index(p["name"][:2] + p["name"][-1]) for p in ops])
        for _ in range(OPT["tries"]):
            mid, wide, at = rng.uniform(0, best[0]), rng.uniform(2, 12), np.array(best[1])
            push = rng.normal(0, OPT["shake"], n)
            if rng.uniform() < OPT["kin"]:
                wide, push = wide / 2, 0.3 * push + rng.normal(0, OPT["far"], len(kinds))[kind] * (rng.uniform(size=len(kinds)) < 0.3)[kind]
            key = (at + push * (np.abs(at - mid) < wide)).tolist()
            for k in range(n):
                for d, _w in pred[k]:
                    if key[d] >= key[k]:
                        key[k] = key[d] + 1e-6
            other = tighten(sorted(range(n), key=lambda k: key[k]))
            if other[2] <= best[2] * (1 + OPT["slack"] * (1 - _ / OPT["tries"])):
                best = other
                if best[2] < kept[2]:
                    kept = best
        best = kept
        if "hook" in OPT:
            best = OPT["hook"](ops, place, pred, next_, cost, hold, best)
        PLAN[n] = best
    best = PLAN[n]
    order = sorted(range(n), key=lambda k: (best[1][k], k))
    OPT["span"] = best[0]
    count = {q: 0 for q in qsem}
    know = {q: {} for q in eng}
    done, seen = {}, {}
    for k in order:
        p = ops[k]
        q = p["q"]
        if q == "r":
            done[k], seen[k] = p["sem"], {}
            continue
        need, via = {}, {}
        for d in p["deps"]:
            if done[d] is None:
                continue
            s, v = done[d]
            if know[q].get(s, 0) < v:
                need[s] = max(need.get(s, 0), v)
                for s2, v2 in seen[d].items():
                    via[s2] = max(via.get(s2, 0), v2)
        for s, v in need.items():
            eng[q].wait_ge(T.sem[s], v)
            know[q][s] = max(know[q].get(s, 0), v)
        for s, v in via.items():
            know[q][s] = max(know[q].get(s, 0), v)
        seen[k] = dict(know[q])
        if p["sem"] is not None:
            s, v = p["sem"]
            for f in p["fns"]:
                ins = f()
                if v is not None:
                    ins.then_inc(T.sem[s], 16)
            done[k] = None if v is None else (s, v)
        else:
            for f in p["fns"]:
                f().then_inc(T.sem[qsem[q]], 1)
                count[q] += 1
            done[k] = (qsem[q], count[q])
    for q, s in qsem.items():
        g.wait_ge(T.sem[s], count[q])
    for p in ops:
        if p["sem"] is not None and p["sem"][1] is not None:
            g.wait_ge(T.sem[p["sem"][0]], p["sem"][1])
    g.wait_ge(T.sem.loc, loc[0])
